import numpy as np, ml_dtypes
CORES = [51,54,179,182]
N = 4
BF = ml_dtypes.bfloat16
def gentries(a):
    return np.ascontiguousarray(a.reshape(8, 16, -1).transpose(0, 2, 1)).reshape(8, -1)
def gtable(e):
    e = np.asarray(e); return np.ascontiguousarray(e.reshape(8, -1, 16).transpose(0, 2, 1)).reshape(128, -1).astype(np.int32)
V, S0, C, T = 4096, 320, 48, 4
A, B = (14, 12, 13, 12), (8, 11, 10, 9)
S = S0 + C * T
K = 64
def first(m):
    return np.take_along_axis(m, np.argmax(m < V, axis=-1)[..., None], -1)[..., 0]
def parts(rng):
    n, h = V // K, S0 // K
    vp = np.argsort(rng.random((8, V)), axis=1); w = np.full((N, 8, K, 16 * h), V); w[..., :n] = vp.reshape(8, K, n)
    m = np.take_along_axis(w, np.argsort(rng.random(w.shape), axis=-1), -1).reshape(N, 8, S0, 16)
    s = np.arange(S0)[:, None]; pos = s // h * n
    up = s + ((S0 - s) * rng.random(m.shape)).astype(np.int64); j = pos + ((V - pos) * rng.random(m.shape)).astype(np.int64)
    e1 = np.take_along_axis(first(m), up.reshape(N, 8, -1), 2).reshape(m.shape)
    e2 = np.take_along_axis(np.broadcast_to(vp, (N, 8, V)), j.reshape(N, 8, -1), 2).reshape(m.shape)
    z = rng.random(m.shape)
    return vp, m, np.where(z < 0.45, e1, np.where(z < 0.75, e2, np.where(z < 0.95, rng.integers(0, V, m.shape), V)))
def steps(rng, vp, dev, down):
    u = np.arange(K) + rng.integers(0, 24, (N, 8, 16, K)); cl = np.argsort(vp, axis=1) // (V // K)
    ix = np.take_along_axis(u, cl[None, :, None, :], 3) + 4
    i = np.arange(16)[:, None]; off = (i * (2 * rng.integers(0, 8, dev.shape) + 1) + rng.integers(0, 16, dev.shape)) % 16 < dev
    d = -1 if down else rng.integers(1, 4, ix.shape) * (2 * rng.integers(0, 2, ix.shape) - 1)
    return ix + np.where(off, d, 0)
def pack(rng, tab, ix, m, e):
    o = np.argsort(rng.random((N, 8, S0)), axis=2)[..., None]; e = np.where(np.any(m < V, axis=3, keepdims=True), e, V)
    m = np.take_along_axis(m, o, 2); e = np.take_along_axis(e, o, 2)
    return {"xs": np.take_along_axis(tab, ix, 3).astype(np.float32).reshape(N, 128, V).astype(BF),
            "mem0": np.stack([gtable(a.reshape(8, -1)) for a in m]), "inv0": np.stack([gtable(a.reshape(8, -1)) for a in e])}
def plain(rng):
    return np.sort(rng.standard_normal((N, 8, 16, 128)), axis=3) * np.exp2(rng.integers(-2, 3, (N, 8, 16, 1)))
def even(rng):
    return (np.arange(128) - 50) * np.exp2(rng.integers(-2, 3, (N, 8, 16, 1)))
def some(rng, share):
    return np.where(rng.random((N, 8, 1, V)) < share, rng.integers(1, 17, (N, 8, 1, V)), 0)
def chain(rng, vp, m, e, dev):
    n, h = V // K, S0 // K
    a = np.full((K, h, 16), V); a[:, :n // 16] = vp[7].reshape(K, n // 16, 16); a = a.reshape(S0, 16)
    s, row = np.argwhere(a == 0)[0]; a[s, row] = a[s, 1]; a[s, 1] = 0
    full = np.flatnonzero(a[:, 0] < V); sp = np.append(rng.permutation(full[full != s])[:C // 8 - 1], s)
    c = np.stack([np.append([0, 15], rng.permutation(np.arange(1, 15))) for b in sp]) ^ int(rng.integers(0, 16))
    m[:, 7] = a; dev[:, 7] = 0
    for q in range(N): dev[q, 7, 0, a[sp]] = 16 * ((c >> (q % 4)) & 1)
    z = rng.random((N, S0, 16))
    e[:, 7] = np.where(z < 0.5, a[:, :1], np.where(z < 0.75, rng.choice(a[sp, 0], z.shape), e[:, 7])); e[:, 7, :, 2] = a[:, 0]
def setup_inputs(rng):
    vp, m, e = parts(rng); share = rng.choice(np.array([0.004, 0.01, 0.02, 0.05]), (N, 8, 1, 1))
    return pack(rng, plain(rng), steps(rng, vp, some(rng, share), False), m, e)
def setup_inputs_room(rng):
    vp, m, e = parts(rng); dev = np.zeros((N, 8, 1, V), np.int64)
    for q in range(1, N, 2):
        for g in range(8):
            a = m[q - 1, g]; can = np.flatnonzero(np.sum(a < V, axis=1) > 1); row = np.argmax((a < V) * (rng.random(a.shape) + 0.5), axis=1)
            n = (C, C + 1, C - 1, S0, 1, 0, C, 2)[g] if q == 1 else int(rng.choice(np.array([0, 1, 2, C - 1, C, C + 1, S0])))
            s = rng.permutation(can)[:n]; dev[q, g, 0, a[s, row[s]]] = 16
    return pack(rng, even(rng), steps(rng, vp, dev, False), m, e)
def setup_inputs_ties(rng):
    vp, m, e = parts(rng); n, h = V // K, S0 // K
    j = np.arange(S0)[:, None] // h * n + rng.integers(0, n, m.shape)
    own = np.take_along_axis(np.broadcast_to(vp, (N, 8, V)), j.reshape(N, 8, -1), 2).reshape(m.shape)
    e = np.where(rng.random(m.shape) < 0.8, own, e); z = rng.random((N, 8, 1, V)); t = rng.integers(0, T, z.shape); one = rng.integers(0, 2, z.shape)
    dev = np.where(z < 0.02, 16 - np.array(B)[t] + one, np.where(z < 0.3, 16 - np.array(A)[t] + one, 0))
    chain(rng, vp, m, e, dev)
    return pack(rng, even(rng), steps(rng, vp, dev, True), m, e)
def setup_inputs_alike(rng):
    vp, m, e = parts(rng)
    m = np.where(rng.random(m.shape) < rng.random((N, 8, S0, 1)) * 1.2, m, V); m[:, :, 3::7, :15] = V; m[:, :, 5::11] = V
    lead = first(m); e[:, ::2] = rng.choice(np.array([0, V - 1, V // 2, V]), (N, 4, S0, 16))
    e[:, 1] = lead[:, 1, :, None]; e[:, 3] = lead[:, 3, S0 // 2, None, None]; e[:, 5] = V
    return pack(rng, plain(rng), steps(rng, vp, some(rng, 0.1), False), m, e)
def setup_inputs_crowd(rng):
    vp, m, e = parts(rng); share = rng.choice(np.array([0.1, 0.3, 0.8]), (N, 8, 1, 1)); share[rng.integers(0, N)] = 0.0; share[:, rng.integers(0, 8)] = 0.0
    return pack(rng, plain(rng), steps(rng, vp, some(rng, share), False), m, e)
def setup_inputs_spread(rng):
    vp, m, e = parts(rng); share = rng.choice(np.array([0.004, 0.01, 0.02, 0.05]), (N, 8, 1, 1)); w = (N, 8, 16, 128)
    z = rng.standard_normal(w); z = z * (np.abs(z) > 2.0 ** -8)
    size = np.exp2(rng.choice(np.array([-65, -62, -40, -20, -2, 0, 2, 20, 40, 80]), (N, 8, 16, 1)))
    tab = np.sort(z * np.exp2(rng.integers(-6, 7, w)) * (rng.random(w) > 0.0625), axis=3) * size
    return pack(rng, tab, steps(rng, vp, some(rng, share), False), m, e)
def check_inputs(d):
    bad = []
    x = np.abs(d["xs"].astype(np.float32))
    if not np.all((x == 0) | ((x >= 2.0 ** -100) & (x <= 2.0 ** 100))): bad.append("sizes of the numbers in xs")
    for k in ("mem0", "inv0"):
        if np.min(d[k]) < 0 or np.max(d[k]) > V: bad.append("range of " + k)
    z = np.sort(np.stack([gentries(a) for a in d["mem0"]]), axis=2)
    if np.any((z[..., 1:] == z[..., :-1]) & (z[..., 1:] < V)): bad.append("no variable twice in a group of mem0")
    a, b = d["mem0"].reshape(-1, 8, 16, S0), d["inv0"].reshape(-1, 8, 16, S0)
    if np.any(np.any(b < V, axis=2) & ~np.any(a < V, axis=2)): bad.append("no bounds in slots without members")
    return bad
def reference(xs, mem0, inv0):
    x = np.concatenate([xs.astype(np.float32).reshape(N, 8, 16, V), np.zeros((N, 8, 16, 1), np.float32)], axis=3)
    M = np.full((N, 8, S, 16), V, np.int64); I = np.full((N, 8, S, 16), V, np.int64)
    for r in range(N):
        M[r, :, :S0] = gentries(mem0[r]).reshape(8, S0, 16); I[r, :, :S0] = gentries(inv0[r]).reshape(8, S0, 16)
    for t in range(T):
        n = S0 + C * t
        for r in range(N):
            w = x[(r + t) % N]; m = M[r, :, :n].copy(); e = I[r, :, :n].copy(); lead = first(m)
            xl = np.take_along_axis(w, lead[:, None, :], 2)[..., None]
            xm = np.take_along_axis(w, m.reshape(8, 1, -1), 2).reshape(8, 16, n, 16); xe = np.take_along_axis(w, e.reshape(8, 1, -1), 2).reshape(8, 16, n, 16)
            e = np.where(np.sum(xl <= xe, axis=1) < A[t], V, e)
            leave = (m < V) & (np.sum(xm == xl, axis=1) < B[t])
            has = np.any(leave, axis=2).astype(np.int64); before = np.add.accumulate(has, axis=1) - has
            split = (has == 1) & (before < C); leave = leave & split[..., None]
            stay = np.where(leave, V, m); go = np.where(leave, m, V)
            M[r, :, :n] = stay; I[r, :, :n] = e
            for g in range(8):
                ids = np.flatnonzero(split[g]); k = len(ids)
                f = np.arange(V + 1); f[lead[g, ids]] = first(go[g, ids])
                M[r, g, n:n + k] = go[g, ids]; I[r, g, n:n + k] = np.where(e[g, ids] < V, f[e[g, ids]], stay[g, ids])
    return {"ym": np.stack([gtable(a.reshape(8, -1)) for a in M]).astype(np.float32), "yi": np.stack([gtable(a.reshape(8, -1)) for a in I]).astype(np.float32)}

@@ -1,0 +1,570 @@
+from concourse.bass import DstId, RemoteDMATransfer
+from concourse.mybir import AluOpType as ALU, ActivationFunctionType as AF
+
+NV, S0, C, NT, NS = 4096, 320, 48, 4, 512
+TA, TB = (14, 12, 13, 12), (8, 11, 10, 9)
+BIG = 8192.0
+FS = (14, 14, 10, 10)
+RV, RS, LONE, HALF = 2, 2, 6, 2
+BLOCKS = ("bm0 la0 bm1 lm0 lf0 fm01 fm02 bm2 be0 be1 le0 fe01 la1 lm1 lf1 fm12 fm13 la2 fm03 fe02 lm2 fm23 le1 fe12 "
+          "fe03 fe13 lf2 bm3 la3 lm3 be2 le2 lf3 be3 fe23 oe le3 om")
+DUE = {"bm0": 12.7, "la0": 9.8, "lm0": 28.6, "be0": 34.4, "lf0": 19.7, "le0": 42.4, "bm1": 19.0, "fm01": 24.2, "fm02": 25.8,
+       "fm03": 52.0, "la1": 51.7, "lm1": 26.5, "be1": 39.2, "fe01": 30.0, "lf1": 29.3, "le1": 66.5, "bm2": 29.2, "fm12": 31.5,
+       "la2": 46.9, "lm2": 58.3, "fm13": 40.6, "be2": 86.7, "fe02": 53.9, "fe12": 67.9, "lf2": 73.8, "le2": 68.7, "bm3": 80.0,
+       "fm23": 43.9, "la3": 53.3, "lm3": 60.2, "lf3": 66.5, "om": 95.5, "fe03": 69.0, "fe13": 73.5, "fe23": 84.0, "be3": 74.5,
+       "oe": 74.0, "le3": 92.0}
+XW, FW = 4112, 4160
+PAIRS = [(0, 1), (0, 2), (1, 2), (0, 3), (1, 3), (2, 3)]
+
+f32, bf, i32, u16 = "float32", "bfloat16", "int32", "uint16"
+SCRATCH = {
+    "Y0": ("sbuf", [128, 40, 16], i32), "Yf": ("sbuf", [128, 20, 32], f32), "OTf": ("sbuf", [128, 640], f32),
+    "MI": ("sbuf", [128, S0], i32), "EI": ("sbuf", [128, S0], i32), "X": ("sbuf", [128, XW], bf),
+    "CMP": ("sbuf", [128, 32 * S0], bf), "XE": ("sbuf", [128, 16 * S0], bf),
+    "NX": ("sbuf", [128, 6 * 768], bf), "NC": ("sbuf", [128, 3 * 768], bf),
+    "F": ("sbuf", [128, FW], f32), "FX": ("sbuf", [128, 768], f32),
+    "MP": ("sbuf", [128, NS], f32), "ER": ("sbuf", [128, NS], f32), "LP": ("sbuf", [128, NS], f32),
+    "FM": ("sbuf", [128, S0], f32), "DG": ("sbuf", [128, S0], f32), "SC": ("sbuf", [128, S0], f32),
+    "WB": ("sbuf", [128, NS], bf), "HAS": ("sbuf", [128, NS], bf), "PP": ("sbuf", [128, NS], bf),
+    "JK": ("sbuf", [128, 3 * NS], bf), "ACC": ("sbuf", [128, 48], f32),
+    "IDS": ("sbuf", [128, 16], u16), "OLS": ("sbuf", [128, 16], u16), "ELS": ("sbuf", [128, C], u16),
+    "YM": ("sbuf", [128, NS], f32), "YI": ("sbuf", [128, NS], f32),
+    "PI": ("sbuf", [128, 8], i32), "COL": ("sbuf", [128, 24], f32),
+    "IA": ("sbuf", [128, 128], f32), "ID": ("sbuf", [128, 128], f32), "IX": ("sbuf", [128, 144], f32),
+    "IC": ("sbuf", [128, S0], f32), "DIAG": ("sbuf", [128, S0], f32), "RST": ("sbuf", [128, S0], f32),
+    "ONEF": ("sbuf", [128, 128], f32), "ONEB": ("sbuf", [128, 128], bf), "TRI": ("sbuf", [128, 128], f32),
+    "IDF": ("sbuf", [128, 128], f32), "IDB": ("sbuf", [128, 128], bf), "NEG": ("sbuf", [128, 128], bf),
+    "SEL": ("sbuf", [128, 144], bf), "SELF": ("sbuf", [128, 144], f32), "ZER": ("sbuf", [128, C], f32),
+    "D0": ("psum", [128, 1024], f32), "D1": ("psum", [128, 1024], f32),
+    "CM": ("psum", [128, 512], f32), "CE": ("psum", [128, 512], f32),
+    "LB": ("psum", [128, 512], f32), "NB": ("psum", [128, 512], f32),
+}
+for _t in range(NT):
+    SCRATCH["LST%d" % _t] = ("sbuf", [128, 664], u16)
+    SCRATCH["XL%d" % _t] = ("sbuf", [128, RV * S0], bf)
+    SCRATCH["RW%d" % _t] = ("sbuf", [128, NS], bf)
+    SCRATCH["RD%d" % _t] = ("sbuf", [128, NS], bf)
+    SCRATCH["W%d" % _t] = ("sbuf", [128, 10 * C], f32)
+    if _t:
+        SCRATCH["OUT%d" % _t] = ("sbuf", [128, 2 * NS], bf)
+        SCRATCH["NL%d" % _t] = ("sbuf", [128, 3 * C * _t], u16)
+    if _t < NT - 1:
+        SCRATCH["SN%d" % _t] = ("sbuf", [128, 3 * C], u16)
+
+SEMAPHORES = (["eV", "eS", "eP", "eG", "sent", "ldY", "ldM", "ldE", "ldX", "stored"]
+              + ["rep%d" % t for t in range(NT)]
+              + [n + str(t) for n in ("lst", "rw", "rd") for t in (1, 2, 3)]
+              + ["%s%d%d" % (n, k, t) for n in ("nm", "ne", "nw", "nd") for k, t in PAIRS])
+
+CASES = [(1.25, 1.56, 3.8, 0.417, 2.4, 0.6, 0.10)]
+LOOK = 0.12
+BANK = ("D0", "D1", "CM", "CE", "LB", "NB")
+
+
+def build(case):
+    ops, last, block = [], {}, ["in"]
+    CY, GA, SCT, PC, HOP, ISSUE = 0.83e-3 * case[0], case[1], case[2], case[3] * 1e-3 * case[0], case[4], case[5]
+
+    def cyc(n):
+        return max(64.0, n) * CY
+
+    def add(eng, fn, busy, rd, wr, done=None, sem=None, sends=None, name=""):
+        me, deps = len(ops), set()
+        for (b, lo, hi) in rd:
+            deps.update(o for (l2, h2, o, w) in last.get(b, []) if w and l2 < hi and lo < h2)
+        for (b, lo, hi) in wr:
+            deps.update(o for (l2, h2, o, w) in last.get(b, []) if l2 < hi and lo < h2)
+        for (b, lo, hi) in wr:
+            last[b] = [e for e in last.get(b, []) if not (lo <= e[0] and e[1] <= hi)] + [(lo, hi, me, True)]
+        for (b, lo, hi) in rd:
+            last.setdefault(b, []).append((lo, hi, me, False))
+        ops.append(dict(eng=eng, fn=fn, busy=busy, done=busy if done is None else done, deps=deps, sem=sem,
+                        sends=sends, name=name, block=block[0], rd=rd, wr=wr))
+
+    def ap(T, r):
+        return T[r[0]][:, r[1]:r[2]]
+
+    def ind(T, w, o):
+        return ap(T, w).indirect(ap(T, o))
+
+    def n_(r):
+        return r[2] - r[1]
+
+    def rw(rd, wr):
+        return ([r for r in rd if r[0] not in BANK],
+                [r for r in wr if r[0] not in BANK] + [(r[0], 0, 1024) for r in rd + wr if r[0] in BANK])
+
+    def col(j):
+        return ("COL", j, j + 1)
+
+    def sv(T, s):
+        return ap(T, s) if isinstance(s, tuple) else s
+
+    def ts(out, in0, s1, s2, op0, op1=None, step=1):
+        def fn(g, T, cx):
+            a = T[in0[0]][:, in0[1] + step - 1:in0[2]:step] if step > 1 else ap(T, in0)
+            if op1 is None:
+                return [g.vector.tensor_scalar(ap(T, out), a, sv(T, s1), None, op0)]
+            return [g.vector.tensor_scalar(ap(T, out), a, sv(T, s1), sv(T, s2), op0, op1)]
+        r, w = rw([in0] + [s for s in (s1, s2) if isinstance(s, tuple)], [out])
+        add("V", fn, cyc(n_(out)), r, w, name="ts " + out[0])
+
+    def flip(out, in0, step=1):
+        ts(out, in0, -1.0, float(NV), ALU.mult, ALU.add, step)
+
+    def tt(out, in0, in1, op):
+        r, w = rw([in0, in1], [out])
+        k = 1 if (in0[0] in BANK or in1[0] in BANK) else 2
+        add("V", lambda g, T, cx: [g.vector.tensor_tensor(ap(T, out), ap(T, in0), ap(T, in1), op)],
+            cyc(n_(out) * k), r, w, name="tt " + out[0])
+
+    def gtt(out, win, off, in1, op):
+        add("V", lambda g, T, cx: [g.vector.tensor_tensor(ap(T, out), ind(T, win, off), ap(T, in1), op)],
+            0.05 + n_(out) * GA * CY, [win, off, in1], [out], name="gtt " + out[0])
+
+    def vcopy(out, in0):
+        add("V", lambda g, T, cx: [g.vector.tensor_copy(ap(T, out), ap(T, in0))], cyc(n_(out)), [in0], [out],
+            name="cp " + out[0])
+
+    def vgather(out, win, off):
+        add("V", lambda g, T, cx: [g.vector.tensor_copy(ap(T, out), ind(T, win, off))],
+            0.05 + n_(out) * GA * CY, [win, off], [out], name="vg " + out[0])
+
+    def vscatter(win, off, in0, in1=None):
+        def fn(g, T, cx):
+            if in1 is None:
+                return [g.vector.tensor_copy(ind(T, win, off), ap(T, in0))]
+            return [g.vector.tensor_tensor(ind(T, win, off), ap(T, in0), ap(T, in1), ALU.subtract)]
+        add("V", fn, 0.05 + n_(in0) * SCT * CY, [off, in0] + ([in1] if in1 else []), [win], name="sc " + win[0])
+
+    def scan(out, d0, d1, op0, op1, half=False, init=0.0):
+        add("V", lambda g, T, cx: [g.vector.tensor_tensor_scan(ap(T, out), ap(T, d0), ap(T, d1), sv(T, init), op0, op1)],
+            cyc(n_(out) * (0.5 if half else 1)), [d0, d1] + ([init] if init else []), [out], name="scan")
+
+    def mset(out, v, half=False):
+        add("V", lambda g, T, cx: [g.vector.memset(ap(T, out), v)], cyc(n_(out) * (0.5 if half else 1)), [], [out],
+            name="ms " + out[0])
+
+    def act(out, in0, func, bias=None, scale=None, acc=None, off=None):
+        def fn(g, T, cx):
+            kw = {}
+            if bias is not None:
+                kw["bias"] = sv(T, bias)
+            if scale is not None:
+                kw["scale"] = sv(T, scale)
+            if acc is not None:
+                kw["accum_out"] = ap(T, acc)
+            return [g.scalar.activation(ap(T, out), ap(T, in0) if off is None else ind(T, in0, off), func, **kw)]
+        r, w = rw([in0] + [s for s in (bias, scale, off) if isinstance(s, tuple)], [out] if acc is None else [out, acc])
+        busy = cyc(n_(out)) + (0.02 if acc else 0) if off is None else 0.065 + n_(out) * GA * CY
+        add("S", fn, busy, r, w, name="act " + (out[0] if acc is None else "ACC"))
+
+    def mm(items, wide=False):
+        def fn(g, T, cx):
+            return [g.tensor.matmul(ap(T, o), ap(T, l), T[x[0]][:, x[1]:x[2]:st] if st > 1 else ap(T, x), a, z)
+                    for (o, l, x, st, a, z) in items]
+        r, w = rw([i[1] for i in items] + [i[2] for i in items], [i[0] for i in items])
+        add("P", fn, sum(max(64, n_(i[0])) for i in items) * PC * (4 if wide else 1), r, w, name="mm " + items[0][0][0])
+
+    def count_row(bank, i, rhs, key):
+        def fn(g, T, cx):
+            k = cx.get(key, 0)
+            cx[key] = k + 1
+            return [g.tensor.matmul(T[bank][:, 0:S0], T.SEL[:, 15 - i:143 - i], ap(T, rhs), k == 0, k == 15)]
+        add("P", fn, S0 * PC, [rhs, ("SEL", 0, 144)], [(bank, i, i + 1)], name="cnt " + key)
+
+    def iota(out, pat, base, cm, flt=True):
+        def fn(g, T, cx):
+            if flt:
+                return [g.iota(ap(T, out), pat, base, cm, allow_small_or_imprecise_dtypes=True)]
+            return [g.iota(ap(T, out), pat, base, cm)]
+        add("G", fn, 0.13 + 2 * n_(out) * CY, [], [out], name="iota " + out[0])
+
+    def dma(q, fn, rd, wr, sem, done):
+        add(q, fn, 0.08, rd, wr, done=done, sem=sem, name="dma " + sem)
+
+    def send(tr, extra=0.0):
+        add("G", None, ISSUE, [x[0] for x in tr], [x[1] for x in tr], done=HOP + extra, sends=tr, name="send " + tr[0][3])
+
+    dma("Y", lambda g, T, cx: [g.sync.dma_start(T.MI[:], T.mem0[:])], [], [("MI", 0, S0)], "ldM", 2.4)
+    k = 0
+    for G in range(4):
+        for kind in range(2):
+            for g0 in range(2):
+                def fn(g, T, cx, G=G, kind=kind, g0=g0, q=k % 2):
+                    src = (T.mem0, T.inv0)[kind][32 * G + 16 * g0:32 * G + 16 * g0 + 16, :]
+                    dst = T.Y0[32 * G + 16 * kind:32 * G + 16 * kind + 16, 20 * g0:20 * g0 + 20, :]
+                    return [(g.scalar, g.sync)[q].dma_start(dst, src)]
+                dma("SY"[k % 2], fn, [], [("Y0", k, k + 1)], "ldY", 2.6)
+                k += 1
+    dma("S", lambda g, T, cx: [g.scalar.dma_start(T.X[:, 0:2048], T.xs[:, 0:2048])], [], [("X", 0, 2048)], "ldX", 5.0)
+    dma("Y", lambda g, T, cx: [g.sync.dma_start(T.X[:, 2048:NV], T.xs[:, 2048:NV])], [], [("X", 2048, NV)], "ldX", 5.0)
+    dma("Y", lambda g, T, cx: [g.sync.dma_start(T.EI[:], T.inv0[:])], [], [("EI", 0, S0)], "ldE", 5.5)
+
+    iota(("PI", 0, 1), [[0, 1]], 0, 1, flt=False)
+    iota(("IA", 0, 128), [[1, 8], [0, 16]], 0, 0)
+    iota(("ID", 0, 128), [[1, 128]], 0, -1)
+    iota(("IC", 0, S0), [[0, 20], [1, 16]], 0, 0)
+    iota(("IX", 0, 144), [[1, 144]], -15, 0)
+    iota(("LP", S0, NS), [[0, 4], [-1, C]], -1, 0)
+    for j in range(4):
+        iota(("F", j * FW // 4, (j + 1) * FW // 4), [[0, FW // 4]], 0, 0)
+    ts(("PI", 2, 3), ("PI", 0, 1), 4, None, ALU.arith_shift_right)
+    ts(("PI", 3, 4), ("PI", 0, 1), 15, None, ALU.bitwise_and)
+    vcopy(("COL", 0, 2), ("PI", 2, 4))
+    ts(("ONEF", 0, 128), ("IA", 0, 128), col(0), None, ALU.is_equal)
+    ts(("TRI", 0, 128), ("ID", 0, 128), 0.0, -BIG, ALU.is_gt, ALU.mult)
+    tt(("TRI", 0, 128), ("TRI", 0, 128), ("ONEF", 0, 128), ALU.mult)
+    ts(("IDF", 0, 128), ("ID", 0, 128), 0.0, None, ALU.is_equal)
+    tt(("TRI", 0, 128), ("TRI", 0, 128), ("IDF", 0, 128), ALU.add)
+    ts(("DIAG", 0, S0), ("IC", 0, S0), col(1), None, ALU.is_equal)
+    ts(("RST", 0, S0), ("IC", 0, S0), 0.0, None, ALU.is_gt)
+    ts(col(2), col(0), 16.0, None, ALU.mult)
+    ts(("SEL", 0, 144), ("IX", 0, 144), col(2), None, ALU.is_equal)
+    act(("SELF", 0, 144), ("SEL", 0, 144), AF.Copy, scale=1.0 / 16)
+    act(("ONEB", 0, 128), ("ONEF", 0, 128), AF.Copy)
+    act(("IDB", 0, 128), ("IDF", 0, 128), AF.Copy)
+    act(("NEG", 0, 128), ("IDF", 0, 128), AF.Copy, scale=-1.0)
+    ts(("COL", 4, 7), ("IC", 0, 3), 16.0, 0.5, ALU.mult, ALU.add)
+    ts(("COL", 4, 7), ("COL", 4, 7), col(1), None, ALU.add)
+    scol = {}
+    for t in range(NT):
+        if FS[t] not in scol:
+            j = scol[FS[t]] = 8 + 2 * len(scol)
+            ts(col(j), col(1), float(FS[t]), None, ALU.is_lt)
+            ts(col(j + 1), col(j), BIG / 2, -BIG, ALU.mult, ALU.add)
+        ts(col(16 + t), col(scol[FS[t]]), -8 * BIG, BIG * TA[t], ALU.mult, ALU.add)
+    mset(("X", NV, XW), 0.0)
+    mset(("ZER", 0, C), 0.0)
+    mset(("CMP", 0, S0), 1.0, True)
+    mset(("HAS", S0, NS), 1.0, True)
+    mset(("MP", S0, NS), 0.0)
+    mset(("ER", S0, NS), float(NV))
+    for t in range(NT):
+        n = S0 + C * t
+        mset(("RW%d" % t, n, n + C), 0.0, True)
+        mset(("RD%d" % t, n, NS), 0.0, True)
+
+    flip(("MP", 0, S0), ("MI", 0, S0))
+    mm([(("LB", 0, S0), ("TRI", 0, 128), ("MP", 0, S0), 1, True, True)], True)
+    act(("FM", 0, S0), ("LB", 0, S0), AF.Relu)
+    mm([(("LB", 0, S0), ("ONEF", 0, 128), ("FM", 0, S0), 1, True, True)], True)
+    tt(("DG", 0, S0), ("LB", 0, S0), ("DIAG", 0, S0), ALU.mult)
+    act(("LP", 0, S0), ("LB", 0, S0), AF.Copy)
+    scan(("SC", 0, S0), ("RST", 0, S0), ("DG", 0, S0), ALU.mult, ALU.add)
+    flip(("LST0", 640, 660), ("SC", 0, S0), 16)
+    for g0 in range(2):
+        add("V", lambda g, T, cx, g0=g0: [g.vector.tensor_copy(T.Yf[:, :, 16 * g0:16 * g0 + 16], T.Y0[:, 20 * g0:20 * g0 + 20, :])],
+            cyc(S0), [("Y0", 0, 16)], [("Yf", g0, g0 + 1)], name="reord")
+    for a in range(20):
+        add("V", lambda g, T, cx, a=a: [g.vector.transpose(T.OTf[:, a:640:20], T.Yf[:, a, :])],
+            cyc(32), [("Yf", 0, 2)], [("OTv", a, a + 1)], name="tr")
+    for h in (1, 0):
+        add("V", lambda g, T, cx, h=h: [g.vector.tensor_copy(T.LST0[:, S0 * h:S0 * h + S0], T.OTf[:, S0 * h:S0 * h + S0])],
+            cyc(S0), [("OTv", 0, 20)], [("LST0", S0 * h, S0 * h + S0)], name="cvt")
+    vcopy(("ER", 0, S0), ("EI", 0, S0))
+    src = ("LST0", 0, 660)
+    send([(src, ("LST1", 0, 660), 1, "lst1")], 3.0)
+    send([(src, ("LST%d" % t, 0, 660), t, "lst%d" % t) for t in (2, 3)], 2.0)
+
+    XA = ("X", 0, XW)
+    dcount, ncount = [0], [0]
+
+    def rows(t, i0, i1, op, single):
+        L, XL = "LST%d" % t, "XL%d" % t
+        i = i0
+        while i < i1:
+            m = 1 if i - i0 < single else min(RV, i1 - i)
+            gtt(("CMP", S0 * i, S0 * (i + m)), XA, (L, 20 * i, 20 * (i + m)), (XL, 0, S0 * m), op)
+            for j in range(i, i + m):
+                count_row("CM" if j < 16 else "CE", j % 16, ("CMP", S0 * j, S0 * j + S0), "ME"[j // 16] + str(t))
+            i += m
+
+    def bulk_m(t):
+        L, XL = "LST%d" % t, "XL%d" % t
+        act((XL, 0, S0), XA, AF.Copy, off=(L, 640, 660))
+        for j in range(1, RV):
+            dma("Y", lambda g, T, cx, j=j: [g.sync.dma_start(T[XL][:, S0 * j:S0 * j + S0], T[XL][:, 0:S0])],
+                [(XL, 0, S0)], [(XL, S0 * j, S0 * j + S0)], "rep%d" % t, 2.2)
+        count_row("CM", 0, ("CMP", 0, S0), "M" + str(t))
+        rows(t, 1, 16, ALU.is_equal, LONE if t == 0 else 0)
+        ow = ("RW0", 0, S0) if t == 0 else ("OUT%d" % t, 0, S0)
+        act(ow, ("CM", 0, S0), AF.Relu, bias=BIG * TB[t], scale=-BIG)
+        if t:
+            send([(ow, ("RW%d" % t, 0, S0), -t, "rw%d" % t)], 0.3)
+
+    def bulk_e(t):
+        L, XL, F = "LST%d" % t, "XL%d" % t, FS[t]
+        for p in range(F // 2):
+            D = "D%d" % (dcount[0] % 2)
+            dcount[0] += 1
+            if 2 * p % RS == 0:
+                m = min(RS, F - 2 * p)
+                act(("XE", 640 * p, 640 * p + S0 * m), XA, AF.Copy, off=(L, S0 + 40 * p, S0 + 40 * p + 20 * m))
+            it = []
+            for j in range(2):
+                o = (D, 192 + S0 * j, 512 + S0 * j)
+                it.append((o, ("NEG", 0, 128), (XL, 0, S0), 1, True, False))
+                it.append((o, ("IDB", 0, 128), ("XE", 640 * p + S0 * j, 640 * p + S0 * j + S0), 1, False, True))
+            mm(it)
+            c0 = S0 * (16 + 2 * p)
+            act(("CMP", c0, c0 + 640), (D, 192, 832), AF.Sign, bias=2.0 ** -110)
+            for j in range(2):
+                count_row("CE", 2 * p + j, ("CMP", c0 + S0 * j, c0 + S0 * j + S0), "E" + str(t))
+        rows(t, 16 + F, 32, ALU.is_ge, 0)
+        od = ("RD0", 0, S0) if t == 0 else ("OUT%d" % t, NS, NS + S0)
+        act(od, ("CE", 0, S0), AF.Relu, bias=col(16 + t), scale=col(scol[F] + 1))
+        if t:
+            send([(od, ("RD%d" % t, 0, S0), -t, "rd%d" % t)], 0.3)
+
+    def fresh(k, t, h):
+        NL, x, c = "NL%d" % t, 768 * PAIRS.index((k, t)), 768 * (ncount[0] % 3)
+        ncount[0] += 1
+        b, n = 3 * C * k, S0 + C * k
+        off, op, th, R, sm = ((b, ALU.is_equal, TB[t], "RW", "nw"), (b + 2 * C, ALU.is_ge, TA[t], "RD", "nd"))[h]
+        m = HALF if (h == 0 and t == k + 1) else 1
+        for j in range(m):
+            lo, hi = C * j // m, C * (j + 1) // m
+            if h == 0:
+                act(("NX", x + 16 * lo, x + 16 * hi), XA, AF.Copy, off=(NL, b + C + lo, b + C + hi))
+            gtt(("NC", c + 16 * lo, c + 16 * hi), XA, (NL, off + lo, off + hi), ("NX", x + 16 * lo, x + 16 * hi), op)
+        mm([(("NB", 0, C), ("SEL", 15 - i, 143 - i), ("NC", c + i, c + 768), 16, i == 0, i == 15) for i in range(16)])
+        o = ("OUT%d" % t, NS * h + n, NS * h + n + C)
+        act(o, ("NB", 0, C), AF.Relu, bias=BIG * th, scale=-BIG)
+        send([(o, (R + str(t), n, n + C), -t, "%s%d%d" % (sm, k, t))])
+
+    def share(k, lo, hi, sm):
+        s = ("SN%d" % k, lo, hi)
+        tr = [(s, ("NL%d" % t, 3 * C * k + lo, 3 * C * k + hi), t, "%s%d%d" % (sm, k, t)) for t in range(k + 1, NT)]
+        send(tr[:1])
+        if tr[1:]:
+            send(tr[1:])
+
+    def w(t, j):
+        return ("W%d" % t, C * j, C * j + C)
+
+    def places(t, lo, hi, end, j):
+        if hi - lo > 2 * C:
+            mm([(("LB", lo, hi), ("IDB", 0, 128), ("RW%d" % t, lo, hi), 1, True, True)])
+            tt(("WB", lo, hi), ("MP", lo, hi), ("LB", lo, hi), ALU.min)
+        else:
+            tt(("WB", lo, hi), ("MP", lo, hi), ("RW%d" % t, lo, hi), ALU.min)
+        mm([(("LB", lo, hi), ("ONEB", 0, 128), ("WB", lo, hi), 1, True, True)])
+        act(("HAS", lo, hi), ("LB", lo, hi), AF.Sign)
+        scan(("PP", lo, end), ("HAS", lo, end), ("HAS", lo, end), ALU.add, ALU.max, True, ("PP", lo - 1, lo) if lo else 0.0)
+        for a in range(3):
+            act(("JK", NS * a + lo, NS * a + end), ("PP", lo, end), AF.Sign, bias=col(4 + a), scale=-1.0,
+                acc=("ACC", j + a, j + a + 1))
+
+    def logic_a(t):
+        n = S0 + C * t
+        places(t, 0, n - C if t else n, n - C if t else n + C, 12 * t)
+
+    def logic_m(t):
+        n = S0 + C * t
+        ids, new, j = ("IDS", 4 * t, 4 * t + 3), (n, n + C), 12 * t
+        if t:
+            places(t, n - C, n, n + C, j + 4)
+            tt(("ACC", j + 8, j + 11), ("ACC", j, j + 3), ("ACC", j + 4, j + 7), ALU.add)
+            j += 8
+        ts(ids, ("ACC", j, j + 3), 0.5, (n + C) / 2.0, ALU.mult, ALU.add)
+        vgather(w(t, 0), ("MP", 0, NS), ids)
+        gtt(w(t, 1), ("RW%d" % t, 0, n + C), ids, w(t, 0), ALU.min)
+        mm([(("LB", 0, C), ("TRI", 0, 128), w(t, 1), 1, True, True)], True)
+        act(w(t, 2), ("LB", 0, C), AF.Relu)
+        mm([(("LB", 0, C), ("ONEF", 0, 128), w(t, 2), 1, True, True)], True)
+        act(w(t, 3), ("LP", 0, NS), AF.Copy, off=ids)
+        gtt(w(t, 4), ("LP", 0, NS), ids, ("DIAG", 0, C), ALU.mult)
+        act(("LP",) + new, ("LB", 0, C), AF.Copy)
+        if t < NT - 1:
+            flip(("SN%d" % t, 0, C), w(t, 1))
+            flip(("SN%d" % t, C, 2 * C), ("LP",) + new)
+            share(t, 0, 2 * C, "nm")
+        tt(w(t, 6), w(t, 0), w(t, 1), ALU.subtract)
+        vscatter(("MP", 0, NS), ids, w(t, 6))
+        act(("MP",) + new, w(t, 1), AF.Copy)
+        act(w(t, 7), w(t, 6), AF.Identity, bias=float(NV), scale=-1.0)
+
+    def logic_f(t):
+        ids, ols = ("IDS", 4 * t, 4 * t + 3), ("OLS", 4 * t, 4 * t + 3)
+        scan(w(t, 5), ("RST", 0, C), w(t, 4), ALU.mult, ALU.add)
+        flip(ols, w(t, 5), 16)
+        vscatter(("F", 0, FW), ols, w(t, 3), ("LP", S0 + C * t, S0 + C * t + C))
+        vgather(("ELS", 0, C), ("ER", 0, NS), ids)
+        act(w(t, 8), ("ER", 0, NS), AF.Copy, off=ids)
+        act(("FX", 0, 768), ("F", 0, FW), AF.Copy, off=("ELS", 0, C))
+        mm([(("LB", 0, C), ("SELF", 15 - i, 143 - i), ("FX", i, 768), 16, i == 0, i == 15) for i in range(16)], True)
+        tt(w(t, 8), ("LB", 0, C), w(t, 8), ALU.add)
+        if t < NT - 1:
+            vscatter(("F", 0, FW), ols, ("ZER", 0, C))
+
+    def logic_e(t):
+        n = S0 + C * t
+        ids = ("IDS", 4 * t, 4 * t + 3)
+        for j in range(t + 1):
+            gtt(w(t, 8), ("RD%d" % j, 0, NS), ids, w(t, 8), ALU.max)
+        ts(w(t, 9), w(t, 8), float(NV), BIG, ALU.is_lt, ALU.mult)
+        tt(w(t, 9), w(t, 9), w(t, 7), ALU.add)
+        if t < NT - 1:
+            tt(("ER", n, n + C), w(t, 8), w(t, 9), ALU.min)
+            vcopy(("SN%d" % t, 2 * C, 3 * C), ("ER", n, n + C))
+            share(t, 2 * C, 3 * C, "ne")
+        else:
+            tt(("YI", n, NS), w(t, 8), w(t, 9), ALU.min)
+            dma("Y", lambda g, T, cx: [g.sync.dma_start(T.yi[:, n:NS], T.YI[:, n:NS])], [("YI", n, NS)], [], "stored", 2.2)
+
+    def out_m():
+        act(("YM", 0, NS), ("MP", 0, NS), AF.Identity, bias=float(NV), scale=-1.0)
+        dma("Y", lambda g, T, cx: [g.sync.dma_start(T.ym[:], T.YM[:])], [("YM", 0, NS)], [], "stored", 2.6)
+
+    def out_e():
+        n = NS - C
+        mm([(("CM", 0, n), ("IDF", 0, 128), ("ER", 0, n), 1, True, False)], True)
+        for j in range(NT):
+            mm([(("CM", 0, n), ("IDB", 0, 128), ("RD%d" % j, 0, n), 1, False, j == NT - 1)])
+        ts(("YI", 0, n), ("CM", 0, n), float(NV), None, ALU.min)
+        dma("Y", lambda g, T, cx: [g.sync.dma_start(T.yi[:, 0:n], T.YI[:, 0:n])], [("YI", 0, n)], [], "stored", 2.6)
+
+    for b in BLOCKS.split():
+        block[0] = b
+        {"bm": bulk_m, "be": bulk_e, "fm": lambda k, t: fresh(k, t, 0), "fe": lambda k, t: fresh(k, t, 1), "la": logic_a,
+         "lm": logic_m, "lf": logic_f, "le": logic_e, "om": out_m, "oe": out_e}[b[:2]](*[int(x) for x in b[2:]])
+    return ops
+
+
+def schedule(sets):
+    ops = sets[0]
+    n = len(ops)
+    by_sem = {}
+    for i, o in enumerate(ops):
+        if o["sem"]:
+            by_sem.setdefault(o["sem"], []).append(i)
+    for o in ops:
+        for d in list(o["deps"]):
+            if ops[d]["sem"]:
+                o["deps"].update(by_sem[ops[d]["sem"]])
+    eng = [o["eng"] for o in ops]
+    succ = [[] for _ in range(n)]
+    for i in range(n):
+        for d in sorted(ops[i]["deps"]):
+            succ[d].append(i)
+
+    def lat(d, i, c):
+        if eng[d] == "P" and eng[i] == "P":
+            return 0.0
+        return CASES[c][6] * (0.6 if eng[d] == eng[i] else 1.0)
+
+    pr = [0.0] * n
+    for i in range(n - 1, -1, -1):
+        pr[i] = ops[i]["done"] + max([pr[s] + lat(i, s, 0) for s in succ[i]] + [-DUE.get(ops[i]["block"], 99.0)])
+    left, ready = [len(o["deps"]) for o in ops], [0.0] * n
+    cand = {e: [i for i in range(n) if eng[i] == e and not left[i]] for e in "VSPGY"}
+    free, order = {e: 0.0 for e in cand}, []
+    while len(order) < n:
+        t0, e = min((max(free[e], min(ready[i] for i in c)), e) for e, c in cand.items() if c)
+        now = max((i for i in cand[e] if ready[i] <= t0), key=lambda i: (pr[i], -i))
+        look = LOOK if ops[now]["busy"] > 0.2 else 0.0
+        i = max((i for i in cand[e] if ready[i] <= t0 + look), key=lambda i: (pr[i], -i))
+        cand[e].remove(i)
+        t0 = max(t0, ready[i])
+        free[e] = t0 + ops[i]["busy"]
+        order.append(i)
+        for s in succ[i]:
+            ready[s] = max(ready[s], t0 + ops[i]["done"] + lat(i, s, 0))
+            left[s] -= 1
+            if not left[s]:
+                cand[eng[s]].append(s)
+
+    def replay(c):
+        free, start = {e: 0.0 for e in "VSPGY"}, [0.0] * n
+        for i in order:
+            start[i] = max([free[eng[i]]] + [start[d] + sets[c][d]["done"] + lat(d, i, c) for d in ops[i]["deps"]])
+            free[eng[i]] = start[i] + sets[c][i]["busy"]
+        return max(start[i] + sets[c][i]["done"] for i in range(n)), start
+    return order, replay(0)[1], by_sem, [replay(c)[0] for c in range(len(sets))]
+
+
+_PLAN = {}
+
+
+def plan():
+    if not _PLAN:
+        sets = [build(c) for c in CASES]
+        _PLAN["ops"] = sets[0]
+        _PLAN["order"], _PLAN["start"], _PLAN["by_sem"], _PLAN["ends"] = schedule(sets)
+    return _PLAN
+
+
+def engine_sets(topo, cores, r, tr):
+    can = [topo.engines(cores[r], cores[(r + x[2]) % len(cores)]) for x in tr]
+    if len(tr) == 1:
+        return can
+    a, b = can
+    if len(a) > len(b):
+        return [[e for e in a if e not in b][:len(b)], b]
+    if len(b) > len(a):
+        return [a, [e for e in b if e not in a][:len(a)]]
+    return [a[:len(a) // 2], b[len(b) // 2:]]
+
+
+def rank_program(g, core, T, topo):
+    r = T.rank_of(core)
+    if r is None:
+        return
+    P = plan()
+    ops, cores = P["ops"], list(T.cores)
+    N = len(cores)
+    queue = {"V": g.vector, "S": g.scalar, "P": g.tensor, "G": g, "Y": g.sync}
+    count = {e: 0 for e in "VSPG"}
+    mark, waited, cx, sent = {}, {}, {}, 0
+
+    def wait(e, sem, val):
+        if waited.get((e, sem), 0) < val:
+            waited[(e, sem)] = val
+            queue[e].wait_ge(T.sem[sem], val)
+
+    def meets(x, y):
+        return x[0] == y[0] and x[1] < y[2] and y[1] < x[2]
+
+    for i in P["order"]:
+        o, need = ops[i], {}
+        e = o["eng"]
+        for d in o["deps"]:
+            p = ops[d]
+            if p["sends"]:
+                for j, x in enumerate(p["sends"]):
+                    if any(meets(x[1], y) for y in o["rd"] + o["wr"]):
+                        need[x[3]] = len(engine_sets(topo, cores, (r - x[2]) % N, p["sends"])[j])
+            elif p["sem"]:
+                need[p["sem"]] = 16 * len(P["by_sem"][p["sem"]])
+            elif not (e == "P" and p["eng"] == "P"):
+                s = "e" + p["eng"]
+                need[s] = max(need.get(s, 0), mark[d])
+        for s in sorted(need):
+            wait(e, s, need[s])
+        if o["sends"]:
+            trs = []
+            for x, en in zip(o["sends"], engine_sets(topo, cores, r, o["sends"])):
+                rid, pid = topo.addr(cores[(r + x[2]) % N], core)
+                trs.append((T[x[1][0]][:, x[1][1]:x[1][2]], T[x[0][0]][:, x[0][1]:x[0][2]], T.sem[x[3]], pid, rid,
+                            sum(1 << k for k in en)))
+                sent += len(en)
+            if len(trs) == 1:
+                x = trs[0]
+                g.remote_dma(x[0], x[1], x[2], T.sem.sent, x[3], x[4], x[5])
+            else:
+                g.remote_dma_fused([RemoteDMATransfer(dst_ids=[DstId(rid=x[4], pnc=x[3])], dma_engine_mask=x[5],
+                                                      remote_sem=x[2], src=x[1], dst=x[0]) for x in trs],
+                                   local_sem=T.sem.sent)
+        elif o["sem"]:
+            for ins in o["fn"](g, T, cx):
+                ins.then_inc(T.sem[o["sem"]], 16)
+        else:
+            for ins in o["fn"](g, T, cx):
+                ins.then_inc(T.sem["e" + e], 1)
+                count[e] += 1
+            mark[i] = count[e]
+    for e in "VSPG":
+        wait("G", "e" + e, count[e])
+    wait("G", "sent", sent)
+    wait("G", "stored", 16 * len(P["by_sem"]["stored"]))

@@ -4,15 +4,23 @@ from concourse.mybir import AluOpType as ALU, ActivationFunctionType as AF
 NV, S0, C, NT, NS = 4096, 320, 48, 4, 512
 TA, TB = (14, 12, 13, 12), (8, 11, 10, 9)
 BIG = 8192.0
-FS = (14, 14, 10, 10)
-RV, RS, LONE, HALF = 2, 2, 6, 2
-BLOCKS = ("bm0 la0 bm1 lm0 lf0 fm01 fm02 bm2 be0 be1 le0 fe01 la1 lm1 lf1 fm12 fm13 la2 fm03 fe02 lm2 fm23 le1 fe12 "
-          "fe03 fe13 lf2 bm3 la3 lm3 be2 le2 lf3 be3 fe23 oe le3 om")
-DUE = {"bm0": 12.7, "la0": 9.8, "lm0": 28.6, "be0": 34.4, "lf0": 19.7, "le0": 42.4, "bm1": 19.0, "fm01": 24.2, "fm02": 25.8,
-       "fm03": 52.0, "la1": 51.7, "lm1": 26.5, "be1": 39.2, "fe01": 30.0, "lf1": 29.3, "le1": 66.5, "bm2": 29.2, "fm12": 31.5,
-       "la2": 46.9, "lm2": 58.3, "fm13": 40.6, "be2": 86.7, "fe02": 53.9, "fe12": 67.9, "lf2": 73.8, "le2": 68.7, "bm3": 80.0,
-       "fm23": 43.9, "la3": 53.3, "lm3": 60.2, "lf3": 66.5, "om": 95.5, "fe03": 69.0, "fe13": 73.5, "fe23": 84.0, "be3": 74.5,
-       "oe": 74.0, "le3": 92.0}
+FS = (12, 12, 10, 12)
+RV, RS, LONE, HALF = 2, 2, 4, 2
+LAST, SPLIT = 1, (0, 1, 1)
+BLOCKS = ("bm0 la0 lm0 lf0 fm01 fm02 bm1 bm2 la1 lm1 fm12 fm03 be0 be1 le0 lf1 fe01 fe02 fm13 le1 fe12 la2 lm2 fm23 "
+          "fe03 fe13 be2 lf2 le2 fe23 bm3 la3 lm3 lf3 om be3 oe le3")
+ORDER = (
+    "0k0h00060e010l03050i0u070v090c080b0204100d0f0g18110a0j1g0m0o1k1b1213141o1c1q1d1i151h191a1j261l1r3a1n0n1s271e171m1f2d2e1u0p"
+    "16282i2f0q292h2l2m2k2j2r2g2n2q312p2t32302s2o2v2u34332c388g2a8h353936378l8q0s0r8i0t3b423h3d3f3s3p3c438m8n8v3m3v3j3i3g8r3t3q"
+    "3r3e8p8j903u403o413l3k3n8s942b5j991t1p44205k1v9e6b6f954521468k478t8o916g6c22245l8u9f48239a9h25499692939g97989i9j4b4a4c5m77"
+    "624d5s5n5o4e5t4k4f4g649v9l9m9b4j4h9c4i9q4l9r9na49d63685p4m4n6i4q654u5v4v4r50516u5u5q4t9s9ka9525r696a4oa0606167669o9t595a57"
+    "6d4p9pa55853a14s6h6k5b745475716o6q725c6e6r556laa6t6v5d8ba65eaeabfcfd6s7b7c6n7673787d6j6p6m707eaf9ua279a3a77aar5f7fas8c5g7h"
+    "7i7gat567jaua8acadfeagaidj7k7qb5b2av7laj807mah7n7p5hb67o7rdtb0b1b37s7tb4amfofibbflb7aldkak7u7v5ianaob8dldoap8684e2bjdudp87"
+    "85aq888981bab9dnc4ffc5bfdq8a82838dfj8e8fdmbcc6e7bdc7dvhgbkfhe3fqbgc8cce1cdfrbececac9cfbobhchcicgcbfubpbicjbqckbrclbscmg1bt"
+    "crdsfpfkfgftfmfne8e4hle0g0blcncoercqbme5fvdre6cpg2fsg3cse9g4enbug5hhhmebcteocueqepg6escvbnbvg7hvhqd0efecc0eid4d6eaegetc1eh"
+    "eeekedejc2hic3elhneud5d3d7d8f0g8dbd1f1g9emd9i9i4dahkhrdcgahji0gbddhsd2dedfhpdgf2gcf3evf4f5ggf6i5ghiegegdgii1f7gjihglgkgmgf"
+    "gngoi6h8gpgvgqimhoifi3iaijighti7i2grhuibdhdigsi8idgticiiinh9guh0h5h1h6h4ikf8f9h7hbh2ilhafahcioipfbhditiuh3hehfiviqj0irj1j2"
+    "j3isj4")
 XW, FW = 4112, 4160
 PAIRS = [(0, 1), (0, 2), (1, 2), (0, 3), (1, 3), (2, 3)]
 
@@ -24,14 +32,14 @@ SCRATCH = {
     "NX": ("sbuf", [128, 6 * 768], bf), "NC": ("sbuf", [128, 3 * 768], bf),
     "F": ("sbuf", [128, FW], f32), "FX": ("sbuf", [128, 768], f32),
     "MP": ("sbuf", [128, NS], f32), "ER": ("sbuf", [128, NS], f32), "LP": ("sbuf", [128, NS], f32),
-    "FM": ("sbuf", [128, S0], f32), "DG": ("sbuf", [128, S0], f32), "SC": ("sbuf", [128, S0], f32),
+    "FM": ("sbuf", [128, S0], f32),
     "WB": ("sbuf", [128, NS], bf), "HAS": ("sbuf", [128, NS], bf), "PP": ("sbuf", [128, NS], bf),
     "JK": ("sbuf", [128, 3 * NS], bf), "ACC": ("sbuf", [128, 48], f32),
     "IDS": ("sbuf", [128, 16], u16), "OLS": ("sbuf", [128, 16], u16), "ELS": ("sbuf", [128, C], u16),
     "YM": ("sbuf", [128, NS], f32), "YI": ("sbuf", [128, NS], f32),
     "PI": ("sbuf", [128, 8], i32), "COL": ("sbuf", [128, 24], f32),
     "IA": ("sbuf", [128, 128], f32), "ID": ("sbuf", [128, 128], f32), "IX": ("sbuf", [128, 144], f32),
-    "IC": ("sbuf", [128, S0], f32), "DIAG": ("sbuf", [128, S0], f32), "RST": ("sbuf", [128, S0], f32),
+    "IC": ("sbuf", [128, C], f32), "DIAG": ("sbuf", [128, C], f32), "RST": ("sbuf", [128, C], f32),
     "ONEF": ("sbuf", [128, 128], f32), "ONEB": ("sbuf", [128, 128], bf), "TRI": ("sbuf", [128, 128], f32),
     "IDF": ("sbuf", [128, 128], f32), "IDB": ("sbuf", [128, 128], bf), "NEG": ("sbuf", [128, 128], bf),
     "SEL": ("sbuf", [128, 144], bf), "SELF": ("sbuf", [128, 144], f32), "ZER": ("sbuf", [128, C], f32),
@@ -55,20 +63,13 @@ SEMAPHORES = (["eV", "eS", "eP", "eG", "sent", "ldY", "ldM", "ldE", "ldX", "stor
               + ["rep%d" % t for t in range(NT)]
               + [n + str(t) for n in ("lst", "rw", "rd") for t in (1, 2, 3)]
               + ["%s%d%d" % (n, k, t) for n in ("nm", "ne", "nw", "nd") for k, t in PAIRS])
-
-CASES = [(1.25, 1.56, 3.8, 0.417, 2.4, 0.6, 0.10)]
-LOOK = 0.12
 BANK = ("D0", "D1", "CM", "CE", "LB", "NB")
 
 
-def build(case):
-    ops, last, block = [], {}, ["in"]
-    CY, GA, SCT, PC, HOP, ISSUE = 0.83e-3 * case[0], case[1], case[2], case[3] * 1e-3 * case[0], case[4], case[5]
+def build():
+    ops, last = [], {}
 
-    def cyc(n):
-        return max(64.0, n) * CY
-
-    def add(eng, fn, busy, rd, wr, done=None, sem=None, sends=None, name=""):
+    def add(eng, fn, rd, wr, sem=None, sends=None):
         me, deps = len(ops), set()
         for (b, lo, hi) in rd:
             deps.update(o for (l2, h2, o, w) in last.get(b, []) if w and l2 < hi and lo < h2)
@@ -78,17 +79,13 @@ def build(case):
             last[b] = [e for e in last.get(b, []) if not (lo <= e[0] and e[1] <= hi)] + [(lo, hi, me, True)]
         for (b, lo, hi) in rd:
             last.setdefault(b, []).append((lo, hi, me, False))
-        ops.append(dict(eng=eng, fn=fn, busy=busy, done=busy if done is None else done, deps=deps, sem=sem,
-                        sends=sends, name=name, block=block[0], rd=rd, wr=wr))
+        ops.append(dict(eng=eng, fn=fn, deps=deps, sem=sem, sends=sends, rd=rd, wr=wr))
 
     def ap(T, r):
         return T[r[0]][:, r[1]:r[2]]
 
     def ind(T, w, o):
         return ap(T, w).indirect(ap(T, o))
-
-    def n_(r):
-        return r[2] - r[1]
 
     def rw(rd, wr):
         return ([r for r in rd if r[0] not in BANK],
@@ -106,44 +103,34 @@ def build(case):
             if op1 is None:
                 return [g.vector.tensor_scalar(ap(T, out), a, sv(T, s1), None, op0)]
             return [g.vector.tensor_scalar(ap(T, out), a, sv(T, s1), sv(T, s2), op0, op1)]
-        r, w = rw([in0] + [s for s in (s1, s2) if isinstance(s, tuple)], [out])
-        add("V", fn, cyc(n_(out)), r, w, name="ts " + out[0])
+        add("V", fn, *rw([in0] + [s for s in (s1, s2) if isinstance(s, tuple)], [out]))
 
-    def flip(out, in0, step=1):
-        ts(out, in0, -1.0, float(NV), ALU.mult, ALU.add, step)
+    def flip(out, in0, step=1, k=1.0):
+        ts(out, in0, -k, float(NV), ALU.mult, ALU.add, step)
 
     def tt(out, in0, in1, op):
-        r, w = rw([in0, in1], [out])
-        k = 1 if (in0[0] in BANK or in1[0] in BANK) else 2
-        add("V", lambda g, T, cx: [g.vector.tensor_tensor(ap(T, out), ap(T, in0), ap(T, in1), op)],
-            cyc(n_(out) * k), r, w, name="tt " + out[0])
+        add("V", lambda g, T, cx: [g.vector.tensor_tensor(ap(T, out), ap(T, in0), ap(T, in1), op)], *rw([in0, in1], [out]))
 
     def gtt(out, win, off, in1, op):
         add("V", lambda g, T, cx: [g.vector.tensor_tensor(ap(T, out), ind(T, win, off), ap(T, in1), op)],
-            0.05 + n_(out) * GA * CY, [win, off, in1], [out], name="gtt " + out[0])
+            [win, off, in1], [out])
 
     def vcopy(out, in0):
-        add("V", lambda g, T, cx: [g.vector.tensor_copy(ap(T, out), ap(T, in0))], cyc(n_(out)), [in0], [out],
-            name="cp " + out[0])
+        add("V", lambda g, T, cx: [g.vector.tensor_copy(ap(T, out), ap(T, in0))], [in0], [out])
 
     def vgather(out, win, off):
-        add("V", lambda g, T, cx: [g.vector.tensor_copy(ap(T, out), ind(T, win, off))],
-            0.05 + n_(out) * GA * CY, [win, off], [out], name="vg " + out[0])
+        add("V", lambda g, T, cx: [g.vector.tensor_copy(ap(T, out), ind(T, win, off))], [win, off], [out])
 
     def vscatter(win, off, in0, in1=None):
         def fn(g, T, cx):
             if in1 is None:
                 return [g.vector.tensor_copy(ind(T, win, off), ap(T, in0))]
             return [g.vector.tensor_tensor(ind(T, win, off), ap(T, in0), ap(T, in1), ALU.subtract)]
-        add("V", fn, 0.05 + n_(in0) * SCT * CY, [off, in0] + ([in1] if in1 else []), [win], name="sc " + win[0])
+        add("V", fn, [off, in0] + ([in1] if in1 else []), [win])
 
-    def scan(out, d0, d1, op0, op1, half=False, init=0.0):
+    def scan(out, d0, d1, op0, op1, init=0.0):
         add("V", lambda g, T, cx: [g.vector.tensor_tensor_scan(ap(T, out), ap(T, d0), ap(T, d1), sv(T, init), op0, op1)],
-            cyc(n_(out) * (0.5 if half else 1)), [d0, d1] + ([init] if init else []), [out], name="scan")
-
-    def mset(out, v, half=False):
-        add("V", lambda g, T, cx: [g.vector.memset(ap(T, out), v)], cyc(n_(out) * (0.5 if half else 1)), [], [out],
-            name="ms " + out[0])
+            [d0, d1] + ([init] if init else []), [out])
 
     def act(out, in0, func, bias=None, scale=None, acc=None, off=None):
         def fn(g, T, cx):
@@ -155,38 +142,38 @@ def build(case):
             if acc is not None:
                 kw["accum_out"] = ap(T, acc)
             return [g.scalar.activation(ap(T, out), ap(T, in0) if off is None else ind(T, in0, off), func, **kw)]
-        r, w = rw([in0] + [s for s in (bias, scale, off) if isinstance(s, tuple)], [out] if acc is None else [out, acc])
-        busy = cyc(n_(out)) + (0.02 if acc else 0) if off is None else 0.065 + n_(out) * GA * CY
-        add("S", fn, busy, r, w, name="act " + (out[0] if acc is None else "ACC"))
+        add("S", fn, *rw([in0] + [s for s in (bias, scale, off) if isinstance(s, tuple)], [out] if acc is None else [out, acc]))
 
-    def mm(items, wide=False):
+    def mm(items):
         def fn(g, T, cx):
             return [g.tensor.matmul(ap(T, o), ap(T, l), T[x[0]][:, x[1]:x[2]:st] if st > 1 else ap(T, x), a, z)
                     for (o, l, x, st, a, z) in items]
-        r, w = rw([i[1] for i in items] + [i[2] for i in items], [i[0] for i in items])
-        add("P", fn, sum(max(64, n_(i[0])) for i in items) * PC * (4 if wide else 1), r, w, name="mm " + items[0][0][0])
+        add("P", fn, *rw([i[1] for i in items] + [i[2] for i in items], [i[0] for i in items]))
+
+    def pick(out, sel, buf, lo, hi):
+        mm([(out, (sel, 15 - i, 143 - i), (buf, lo + i, hi), 16, i == 0, i == 15) for i in range(16)])
 
     def count_row(bank, i, rhs, key):
         def fn(g, T, cx):
             k = cx.get(key, 0)
             cx[key] = k + 1
             return [g.tensor.matmul(T[bank][:, 0:S0], T.SEL[:, 15 - i:143 - i], ap(T, rhs), k == 0, k == 15)]
-        add("P", fn, S0 * PC, [rhs, ("SEL", 0, 144)], [(bank, i, i + 1)], name="cnt " + key)
+        add("P", fn, [rhs, ("SEL", 0, 144)], [(bank, i, i + 1)])
 
     def iota(out, pat, base, cm, flt=True):
         def fn(g, T, cx):
             if flt:
                 return [g.iota(ap(T, out), pat, base, cm, allow_small_or_imprecise_dtypes=True)]
             return [g.iota(ap(T, out), pat, base, cm)]
-        add("G", fn, 0.13 + 2 * n_(out) * CY, [], [out], name="iota " + out[0])
+        add("G", fn, [], [out])
 
-    def dma(q, fn, rd, wr, sem, done):
-        add(q, fn, 0.08, rd, wr, done=done, sem=sem, name="dma " + sem)
+    def fill(out, v):
+        iota(out, [[0, out[2] - out[1]]], v, 0)
 
-    def send(tr, extra=0.0):
-        add("G", None, ISSUE, [x[0] for x in tr], [x[1] for x in tr], done=HOP + extra, sends=tr, name="send " + tr[0][3])
+    def send(tr):
+        add("G", None, [x[0] for x in tr], [x[1] for x in tr], sends=tr)
 
-    dma("Y", lambda g, T, cx: [g.sync.dma_start(T.MI[:], T.mem0[:])], [], [("MI", 0, S0)], "ldM", 2.4)
+    add("Y", lambda g, T, cx: [g.sync.dma_start(T.MI[:], T.mem0[:])], [], [("MI", 0, S0)], "ldM")
     k = 0
     for G in range(4):
         for kind in range(2):
@@ -195,20 +182,20 @@ def build(case):
                     src = (T.mem0, T.inv0)[kind][32 * G + 16 * g0:32 * G + 16 * g0 + 16, :]
                     dst = T.Y0[32 * G + 16 * kind:32 * G + 16 * kind + 16, 20 * g0:20 * g0 + 20, :]
                     return [(g.scalar, g.sync)[q].dma_start(dst, src)]
-                dma("SY"[k % 2], fn, [], [("Y0", k, k + 1)], "ldY", 2.6)
+                add("SY"[k % 2], fn, [], [("Y0", k, k + 1)], "ldY")
                 k += 1
-    dma("S", lambda g, T, cx: [g.scalar.dma_start(T.X[:, 0:2048], T.xs[:, 0:2048])], [], [("X", 0, 2048)], "ldX", 5.0)
-    dma("Y", lambda g, T, cx: [g.sync.dma_start(T.X[:, 2048:NV], T.xs[:, 2048:NV])], [], [("X", 2048, NV)], "ldX", 5.0)
-    dma("Y", lambda g, T, cx: [g.sync.dma_start(T.EI[:], T.inv0[:])], [], [("EI", 0, S0)], "ldE", 5.5)
+    add("S", lambda g, T, cx: [g.scalar.dma_start(T.X[:, 0:2048], T.xs[:, 0:2048])], [], [("X", 0, 2048)], "ldX")
+    add("Y", lambda g, T, cx: [g.sync.dma_start(T.X[:, 2048:NV], T.xs[:, 2048:NV])], [], [("X", 2048, NV)], "ldX")
+    add("Y", lambda g, T, cx: [g.sync.dma_start(T.EI[:], T.inv0[:])], [], [("EI", 0, S0)], "ldE")
 
     iota(("PI", 0, 1), [[0, 1]], 0, 1, flt=False)
     iota(("IA", 0, 128), [[1, 8], [0, 16]], 0, 0)
     iota(("ID", 0, 128), [[1, 128]], 0, -1)
-    iota(("IC", 0, S0), [[0, 20], [1, 16]], 0, 0)
+    iota(("IC", 0, C), [[0, 3], [1, 16]], 0, 0)
     iota(("IX", 0, 144), [[1, 144]], -15, 0)
     iota(("LP", S0, NS), [[0, 4], [-1, C]], -1, 0)
     for j in range(4):
-        iota(("F", j * FW // 4, (j + 1) * FW // 4), [[0, FW // 4]], 0, 0)
+        fill(("F", j * FW // 4, (j + 1) * FW // 4), 0)
     ts(("PI", 2, 3), ("PI", 0, 1), 4, None, ALU.arith_shift_right)
     ts(("PI", 3, 4), ("PI", 0, 1), 15, None, ALU.bitwise_and)
     vcopy(("COL", 0, 2), ("PI", 2, 4))
@@ -217,8 +204,8 @@ def build(case):
     tt(("TRI", 0, 128), ("TRI", 0, 128), ("ONEF", 0, 128), ALU.mult)
     ts(("IDF", 0, 128), ("ID", 0, 128), 0.0, None, ALU.is_equal)
     tt(("TRI", 0, 128), ("TRI", 0, 128), ("IDF", 0, 128), ALU.add)
-    ts(("DIAG", 0, S0), ("IC", 0, S0), col(1), None, ALU.is_equal)
-    ts(("RST", 0, S0), ("IC", 0, S0), 0.0, None, ALU.is_gt)
+    ts(("DIAG", 0, C), ("IC", 0, C), col(1), None, ALU.is_equal)
+    ts(("RST", 0, C), ("IC", 0, C), 0.0, None, ALU.is_gt)
     ts(col(2), col(0), 16.0, None, ALU.mult)
     ts(("SEL", 0, 144), ("IX", 0, 144), col(2), None, ALU.is_equal)
     act(("SELF", 0, 144), ("SEL", 0, 144), AF.Copy, scale=1.0 / 16)
@@ -234,38 +221,36 @@ def build(case):
             ts(col(j), col(1), float(FS[t]), None, ALU.is_lt)
             ts(col(j + 1), col(j), BIG / 2, -BIG, ALU.mult, ALU.add)
         ts(col(16 + t), col(scol[FS[t]]), -8 * BIG, BIG * TA[t], ALU.mult, ALU.add)
-    mset(("X", NV, XW), 0.0)
-    mset(("ZER", 0, C), 0.0)
-    mset(("CMP", 0, S0), 1.0, True)
-    mset(("HAS", S0, NS), 1.0, True)
-    mset(("MP", S0, NS), 0.0)
-    mset(("ER", S0, NS), float(NV))
+    fill(("X", NV, XW), 0)
+    fill(("ZER", 0, C), 0)
+    fill(("CMP", 0, S0), 1)
+    fill(("HAS", S0, NS), 1)
+    fill(("MP", S0, NS), 0)
+    fill(("ER", S0, NS), NV)
     for t in range(NT):
         n = S0 + C * t
-        mset(("RW%d" % t, n, n + C), 0.0, True)
-        mset(("RD%d" % t, n, NS), 0.0, True)
+        fill(("RW%d" % t, n, n + C), 0)
+        fill(("RD%d" % t, n, NS), 0)
 
     flip(("MP", 0, S0), ("MI", 0, S0))
-    mm([(("LB", 0, S0), ("TRI", 0, 128), ("MP", 0, S0), 1, True, True)], True)
+    mm([(("LB", 0, S0), ("TRI", 0, 128), ("MP", 0, S0), 1, True, True)])
     act(("FM", 0, S0), ("LB", 0, S0), AF.Relu)
-    mm([(("LB", 0, S0), ("ONEF", 0, 128), ("FM", 0, S0), 1, True, True)], True)
-    tt(("DG", 0, S0), ("LB", 0, S0), ("DIAG", 0, S0), ALU.mult)
+    pick(("NB", 0, 20), "SELF", "FM", 0, S0)
+    mm([(("LB", 0, S0), ("ONEF", 0, 128), ("FM", 0, S0), 1, True, True)])
     act(("LP", 0, S0), ("LB", 0, S0), AF.Copy)
-    scan(("SC", 0, S0), ("RST", 0, S0), ("DG", 0, S0), ALU.mult, ALU.add)
-    flip(("LST0", 640, 660), ("SC", 0, S0), 16)
+    flip(("LST0", 640, 660), ("NB", 0, 20), k=16.0)
     for g0 in range(2):
         add("V", lambda g, T, cx, g0=g0: [g.vector.tensor_copy(T.Yf[:, :, 16 * g0:16 * g0 + 16], T.Y0[:, 20 * g0:20 * g0 + 20, :])],
-            cyc(S0), [("Y0", 0, 16)], [("Yf", g0, g0 + 1)], name="reord")
+            [("Y0", 0, 16)], [("Yf", g0, g0 + 1)])
     for a in range(20):
-        add("V", lambda g, T, cx, a=a: [g.vector.transpose(T.OTf[:, a:640:20], T.Yf[:, a, :])],
-            cyc(32), [("Yf", 0, 2)], [("OTv", a, a + 1)], name="tr")
+        add("V", lambda g, T, cx, a=a: [g.vector.transpose(T.OTf[:, a:640:20], T.Yf[:, a, :])], [("Yf", 0, 2)], [("OTv", a, a + 1)])
     for h in (1, 0):
         add("V", lambda g, T, cx, h=h: [g.vector.tensor_copy(T.LST0[:, S0 * h:S0 * h + S0], T.OTf[:, S0 * h:S0 * h + S0])],
-            cyc(S0), [("OTv", 0, 20)], [("LST0", S0 * h, S0 * h + S0)], name="cvt")
+            [("OTv", 0, 20)], [("LST0", S0 * h, S0 * h + S0)])
     vcopy(("ER", 0, S0), ("EI", 0, S0))
     src = ("LST0", 0, 660)
-    send([(src, ("LST1", 0, 660), 1, "lst1")], 3.0)
-    send([(src, ("LST%d" % t, 0, 660), t, "lst%d" % t) for t in (2, 3)], 2.0)
+    send([(src, ("LST1", 0, 660), 1, "lst1")])
+    send([(src, ("LST%d" % t, 0, 660), t, "lst%d" % t) for t in (2, 3)])
 
     XA = ("X", 0, XW)
     dcount, ncount = [0], [0]
@@ -284,14 +269,14 @@ def build(case):
         L, XL = "LST%d" % t, "XL%d" % t
         act((XL, 0, S0), XA, AF.Copy, off=(L, 640, 660))
         for j in range(1, RV):
-            dma("Y", lambda g, T, cx, j=j: [g.sync.dma_start(T[XL][:, S0 * j:S0 * j + S0], T[XL][:, 0:S0])],
-                [(XL, 0, S0)], [(XL, S0 * j, S0 * j + S0)], "rep%d" % t, 2.2)
+            add("Y", lambda g, T, cx, j=j: [g.sync.dma_start(T[XL][:, S0 * j:S0 * j + S0], T[XL][:, 0:S0])],
+                [(XL, 0, S0)], [(XL, S0 * j, S0 * j + S0)], "rep%d" % t)
         count_row("CM", 0, ("CMP", 0, S0), "M" + str(t))
         rows(t, 1, 16, ALU.is_equal, LONE if t == 0 else 0)
         ow = ("RW0", 0, S0) if t == 0 else ("OUT%d" % t, 0, S0)
         act(ow, ("CM", 0, S0), AF.Relu, bias=BIG * TB[t], scale=-BIG)
         if t:
-            send([(ow, ("RW%d" % t, 0, S0), -t, "rw%d" % t)], 0.3)
+            send([(ow, ("RW%d" % t, 0, S0), -t, "rw%d" % t)])
 
     def bulk_e(t):
         L, XL, F = "LST%d" % t, "XL%d" % t, FS[t]
@@ -315,7 +300,7 @@ def build(case):
         od = ("RD0", 0, S0) if t == 0 else ("OUT%d" % t, NS, NS + S0)
         act(od, ("CE", 0, S0), AF.Relu, bias=col(16 + t), scale=col(scol[F] + 1))
         if t:
-            send([(od, ("RD%d" % t, 0, S0), -t, "rd%d" % t)], 0.3)
+            send([(od, ("RD%d" % t, 0, S0), -t, "rd%d" % t)])
 
     def fresh(k, t, h):
         NL, x, c = "NL%d" % t, 768 * PAIRS.index((k, t)), 768 * (ncount[0] % 3)
@@ -328,7 +313,7 @@ def build(case):
             if h == 0:
                 act(("NX", x + 16 * lo, x + 16 * hi), XA, AF.Copy, off=(NL, b + C + lo, b + C + hi))
             gtt(("NC", c + 16 * lo, c + 16 * hi), XA, (NL, off + lo, off + hi), ("NX", x + 16 * lo, x + 16 * hi), op)
-        mm([(("NB", 0, C), ("SEL", 15 - i, 143 - i), ("NC", c + i, c + 768), 16, i == 0, i == 15) for i in range(16)])
+        pick(("NB", 0, C), "SEL", "NC", c, c + 768)
         o = ("OUT%d" % t, NS * h + n, NS * h + n + C)
         act(o, ("NB", 0, C), AF.Relu, bias=BIG * th, scale=-BIG)
         send([(o, (R + str(t), n, n + C), -t, "%s%d%d" % (sm, k, t))])
@@ -351,28 +336,31 @@ def build(case):
             tt(("WB", lo, hi), ("MP", lo, hi), ("RW%d" % t, lo, hi), ALU.min)
         mm([(("LB", lo, hi), ("ONEB", 0, 128), ("WB", lo, hi), 1, True, True)])
         act(("HAS", lo, hi), ("LB", lo, hi), AF.Sign)
-        scan(("PP", lo, end), ("HAS", lo, end), ("HAS", lo, end), ALU.add, ALU.max, True, ("PP", lo - 1, lo) if lo else 0.0)
+        scan(("PP", lo, end), ("HAS", lo, end), ("HAS", lo, end), ALU.add, ALU.max, ("PP", lo - 1, lo) if lo else 0.0)
         for a in range(3):
             act(("JK", NS * a + lo, NS * a + end), ("PP", lo, end), AF.Sign, bias=col(4 + a), scale=-1.0,
                 acc=("ACC", j + a, j + a + 1))
 
     def logic_a(t):
         n = S0 + C * t
-        places(t, 0, n - C if t else n, n - C if t else n + C, 12 * t)
+        if t == 0 or SPLIT[t - 1]:
+            places(t, 0, n - C if t else n, n - C if t else n + C, 12 * t)
 
     def logic_m(t):
         n = S0 + C * t
         ids, new, j = ("IDS", 4 * t, 4 * t + 3), (n, n + C), 12 * t
-        if t:
+        if t and not SPLIT[t - 1]:
+            places(t, 0, n, n + C, j)
+        elif t:
             places(t, n - C, n, n + C, j + 4)
             tt(("ACC", j + 8, j + 11), ("ACC", j, j + 3), ("ACC", j + 4, j + 7), ALU.add)
             j += 8
         ts(ids, ("ACC", j, j + 3), 0.5, (n + C) / 2.0, ALU.mult, ALU.add)
         vgather(w(t, 0), ("MP", 0, NS), ids)
         gtt(w(t, 1), ("RW%d" % t, 0, n + C), ids, w(t, 0), ALU.min)
-        mm([(("LB", 0, C), ("TRI", 0, 128), w(t, 1), 1, True, True)], True)
+        mm([(("LB", 0, C), ("TRI", 0, 128), w(t, 1), 1, True, True)])
         act(w(t, 2), ("LB", 0, C), AF.Relu)
-        mm([(("LB", 0, C), ("ONEF", 0, 128), w(t, 2), 1, True, True)], True)
+        mm([(("LB", 0, C), ("ONEF", 0, 128), w(t, 2), 1, True, True)])
         act(w(t, 3), ("LP", 0, NS), AF.Copy, off=ids)
         gtt(w(t, 4), ("LP", 0, NS), ids, ("DIAG", 0, C), ALU.mult)
         act(("LP",) + new, ("LB", 0, C), AF.Copy)
@@ -392,8 +380,12 @@ def build(case):
         vscatter(("F", 0, FW), ols, w(t, 3), ("LP", S0 + C * t, S0 + C * t + C))
         vgather(("ELS", 0, C), ("ER", 0, NS), ids)
         act(w(t, 8), ("ER", 0, NS), AF.Copy, off=ids)
-        act(("FX", 0, 768), ("F", 0, FW), AF.Copy, off=("ELS", 0, C))
-        mm([(("LB", 0, C), ("SELF", 15 - i, 143 - i), ("FX", i, 768), 16, i == 0, i == 15) for i in range(16)], True)
+        if t == NT - 1 and LAST:
+            act(("FX", 0, 384), ("F", 0, FW), AF.Copy, off=("ELS", 0, C // 2))
+            vgather(("FX", 384, 768), ("F", 0, FW), ("ELS", C // 2, C))
+        else:
+            act(("FX", 0, 768), ("F", 0, FW), AF.Copy, off=("ELS", 0, C))
+        pick(("LB", 0, C), "SELF", "FX", 0, 768)
         tt(w(t, 8), ("LB", 0, C), w(t, 8), ALU.add)
         if t < NT - 1:
             vscatter(("F", 0, FW), ols, ("ZER", 0, C))
@@ -411,31 +403,28 @@ def build(case):
             share(t, 2 * C, 3 * C, "ne")
         else:
             tt(("YI", n, NS), w(t, 8), w(t, 9), ALU.min)
-            dma("Y", lambda g, T, cx: [g.sync.dma_start(T.yi[:, n:NS], T.YI[:, n:NS])], [("YI", n, NS)], [], "stored", 2.2)
+            add("Y", lambda g, T, cx: [g.sync.dma_start(T.yi[:, n:NS], T.YI[:, n:NS])], [("YI", n, NS)], [], "stored")
 
     def out_m():
         act(("YM", 0, NS), ("MP", 0, NS), AF.Identity, bias=float(NV), scale=-1.0)
-        dma("Y", lambda g, T, cx: [g.sync.dma_start(T.ym[:], T.YM[:])], [("YM", 0, NS)], [], "stored", 2.6)
+        add("Y", lambda g, T, cx: [g.sync.dma_start(T.ym[:], T.YM[:])], [("YM", 0, NS)], [], "stored")
 
     def out_e():
         n = NS - C
-        mm([(("CM", 0, n), ("IDF", 0, 128), ("ER", 0, n), 1, True, False)], True)
+        mm([(("CM", 0, n), ("IDF", 0, 128), ("ER", 0, n), 1, True, False)])
         for j in range(NT):
             mm([(("CM", 0, n), ("IDB", 0, 128), ("RD%d" % j, 0, n), 1, False, j == NT - 1)])
         ts(("YI", 0, n), ("CM", 0, n), float(NV), None, ALU.min)
-        dma("Y", lambda g, T, cx: [g.sync.dma_start(T.yi[:, 0:n], T.YI[:, 0:n])], [("YI", 0, n)], [], "stored", 2.6)
+        add("Y", lambda g, T, cx: [g.sync.dma_start(T.yi[:, 0:n], T.YI[:, 0:n])], [("YI", 0, n)], [], "stored")
 
     for b in BLOCKS.split():
-        block[0] = b
         {"bm": bulk_m, "be": bulk_e, "fm": lambda k, t: fresh(k, t, 0), "fe": lambda k, t: fresh(k, t, 1), "la": logic_a,
          "lm": logic_m, "lf": logic_f, "le": logic_e, "om": out_m, "oe": out_e}[b[:2]](*[int(x) for x in b[2:]])
     return ops
 
 
-def schedule(sets):
-    ops = sets[0]
-    n = len(ops)
-    by_sem = {}
+def plan():
+    ops, by_sem = build(), {}
     for i, o in enumerate(ops):
         if o["sem"]:
             by_sem.setdefault(o["sem"], []).append(i)
@@ -443,56 +432,13 @@ def schedule(sets):
         for d in list(o["deps"]):
             if ops[d]["sem"]:
                 o["deps"].update(by_sem[ops[d]["sem"]])
-    eng = [o["eng"] for o in ops]
-    succ = [[] for _ in range(n)]
-    for i in range(n):
-        for d in sorted(ops[i]["deps"]):
-            succ[d].append(i)
-
-    def lat(d, i, c):
-        if eng[d] == "P" and eng[i] == "P":
-            return 0.0
-        return CASES[c][6] * (0.6 if eng[d] == eng[i] else 1.0)
-
-    pr = [0.0] * n
-    for i in range(n - 1, -1, -1):
-        pr[i] = ops[i]["done"] + max([pr[s] + lat(i, s, 0) for s in succ[i]] + [-DUE.get(ops[i]["block"], 99.0)])
-    left, ready = [len(o["deps"]) for o in ops], [0.0] * n
-    cand = {e: [i for i in range(n) if eng[i] == e and not left[i]] for e in "VSPGY"}
-    free, order = {e: 0.0 for e in cand}, []
-    while len(order) < n:
-        t0, e = min((max(free[e], min(ready[i] for i in c)), e) for e, c in cand.items() if c)
-        now = max((i for i in cand[e] if ready[i] <= t0), key=lambda i: (pr[i], -i))
-        look = LOOK if ops[now]["busy"] > 0.2 else 0.0
-        i = max((i for i in cand[e] if ready[i] <= t0 + look), key=lambda i: (pr[i], -i))
-        cand[e].remove(i)
-        t0 = max(t0, ready[i])
-        free[e] = t0 + ops[i]["busy"]
-        order.append(i)
-        for s in succ[i]:
-            ready[s] = max(ready[s], t0 + ops[i]["done"] + lat(i, s, 0))
-            left[s] -= 1
-            if not left[s]:
-                cand[eng[s]].append(s)
-
-    def replay(c):
-        free, start = {e: 0.0 for e in "VSPGY"}, [0.0] * n
-        for i in order:
-            start[i] = max([free[eng[i]]] + [start[d] + sets[c][d]["done"] + lat(d, i, c) for d in ops[i]["deps"]])
-            free[eng[i]] = start[i] + sets[c][i]["busy"]
-        return max(start[i] + sets[c][i]["done"] for i in range(n)), start
-    return order, replay(0)[1], by_sem, [replay(c)[0] for c in range(len(sets))]
-
-
-_PLAN = {}
-
-
-def plan():
-    if not _PLAN:
-        sets = [build(c) for c in CASES]
-        _PLAN["ops"] = sets[0]
-        _PLAN["order"], _PLAN["start"], _PLAN["by_sem"], _PLAN["ends"] = schedule(sets)
-    return _PLAN
+    order = [int(ORDER[j:j + 2], 32) for j in range(0, len(ORDER), 2)]
+    assert sorted(order) == list(range(len(ops)))
+    seen = set()
+    for i in order:
+        assert ops[i]["deps"] <= seen
+        seen.add(i)
+    return ops, order, by_sem
 
 
 def engine_sets(topo, cores, r, tr):
@@ -511,8 +457,8 @@ def rank_program(g, core, T, topo):
     r = T.rank_of(core)
     if r is None:
         return
-    P = plan()
-    ops, cores = P["ops"], list(T.cores)
+    ops, order, by_sem = plan()
+    cores = list(T.cores)
     N = len(cores)
     queue = {"V": g.vector, "S": g.scalar, "P": g.tensor, "G": g, "Y": g.sync}
     count = {e: 0 for e in "VSPG"}
@@ -526,7 +472,7 @@ def rank_program(g, core, T, topo):
     def meets(x, y):
         return x[0] == y[0] and x[1] < y[2] and y[1] < x[2]
 
-    for i in P["order"]:
+    for i in order:
         o, need = ops[i], {}
         e = o["eng"]
         for d in o["deps"]:
@@ -536,7 +482,7 @@ def rank_program(g, core, T, topo):
                     if any(meets(x[1], y) for y in o["rd"] + o["wr"]):
                         need[x[3]] = len(engine_sets(topo, cores, (r - x[2]) % N, p["sends"])[j])
             elif p["sem"]:
-                need[p["sem"]] = 16 * len(P["by_sem"][p["sem"]])
+                need[p["sem"]] = 16 * len(by_sem[p["sem"]])
             elif not (e == "P" and p["eng"] == "P"):
                 s = "e" + p["eng"]
                 need[s] = max(need.get(s, 0), mark[d])
@@ -567,4 +513,4 @@ def rank_program(g, core, T, topo):
     for e in "VSPG":
         wait("G", "e" + e, count[e])
     wait("G", "sent", sent)
-    wait("G", "stored", 16 * len(P["by_sem"]["stored"]))
+    wait("G", "stored", 16 * len(by_sem["stored"]))

@@ -4,72 +4,76 @@ from concourse.mybir import AluOpType as ALU, ActivationFunctionType as AF
 NV, S0, C, NT, NS = 4096, 320, 48, 4, 512
 TA, TB = (14, 12, 13, 12), (8, 11, 10, 9)
 BIG = 8192.0
-FS = (12, 12, 10, 12)
-RV, RS, LONE, HALF = 2, 2, 4, 2
-LAST, SPLIT = 1, (0, 1, 1)
-BLOCKS = ("bm0 la0 lm0 lf0 fm01 fm02 bm1 bm2 la1 lm1 fm12 fm03 be0 be1 le0 lf1 fe01 fe02 fm13 le1 fe12 la2 lm2 fm23 "
-          "fe03 fe13 be2 lf2 le2 fe23 bm3 la3 lm3 lf3 om be3 oe le3")
-ORDER = (
-    "0k0h00060e010l03050i0u070v090c080b0204100d0f0g18110a0j1g0m0o1k1b1213141o1c1q1d1i151h191a1j261l1r3a1n0n1s271e171m1f2d2e1u0p"
-    "16282i2f0q292h2l2m2k2j2r2g2n2q312p2t32302s2o2v2u34332c388g2a8h353936378l8q0s0r8i0t3b423h3d3f3s3p3c438m8n8v3m3v3j3i3g8r3t3q"
-    "3r3e8p8j903u403o413l3k3n8s942b5j991t1p44205k1v9e6b6f954521468k478t8o916g6c22245l8u9f48239a9h25499692939g97989i9j4b4a4c5m77"
-    "624d5s5n5o4e5t4k4f4g649v9l9m9b4j4h9c4i9q4l9r9na49d63685p4m4n6i4q654u5v4v4r50516u5u5q4t9s9ka9525r696a4oa0606167669o9t595a57"
-    "6d4p9pa55853a14s6h6k5b745475716o6q725c6e6r556laa6t6v5d8ba65eaeabfcfd6s7b7c6n7673787d6j6p6m707eaf9ua279a3a77aar5f7fas8c5g7h"
-    "7i7gat567jaua8acadfeagaidj7k7qb5b2av7laj807mah7n7p5hb67o7rdtb0b1b37s7tb4amfofibbflb7aldkak7u7v5ianaob8dldoap8684e2bjdudp87"
-    "85aq888981bab9dnc4ffc5bfdq8a82838dfj8e8fdmbcc6e7bdc7dvhgbkfhe3fqbgc8cce1cdfrbececac9cfbobhchcicgcbfubpbicjbqckbrclbscmg1bt"
-    "crdsfpfkfgftfmfne8e4hle0g0blcncoercqbme5fvdre6cpg2fsg3cse9g4enbug5hhhmebcteocueqepg6escvbnbvg7hvhqd0efecc0eid4d6eaegetc1eh"
-    "eeekedejc2hic3elhneud5d3d7d8f0g8dbd1f1g9emd9i9i4dahkhrdcgahji0gbddhsd2dedfhpdgf2gcf3evf4f5ggf6i5ghiegegdgii1f7gjihglgkgmgf"
-    "gngoi6h8gpgvgqimhoifi3iaijighti7i2grhuibdhdigsi8idgticiiinh9guh0h5h1h6h4ikf8f9h7hbh2ilhafahcioipfbhditiuh3hehfiviqj0irj1j2"
-    "j3isj4")
-XW, FW = 4112, 4160
 PAIRS = [(0, 1), (0, 2), (1, 2), (0, 3), (1, 3), (2, 3)]
+TUNE = dict(
+    FS=(12, 14, 12, 8),
+    FB="VSSSVV",
+    RV=2, LONE=2,
+    PAD=0.15,
+    R0=6, R1=10, R2=4, SHAKE=2, PIECE=512, FP=(3,), LD=1.3, LR=1.2, WAKE=0.22, GA=1.3e-3, PE=0.42e-3, GI=0.3, VA=0.03, VG=0.05, SA=0.045,
+    FPE=(16, 16, 16, 16), RA=4, RG=2, GD=1.0, LA=(0,), OE=True, GS=1, SEED=7,
+    STEPS=45000, SLACK=0.07,
+    CASES=[dict(FIRST=2.5), dict(GA=0.95e-3, WAKE=0.27, FIRST=4.0, LD=1.6), dict(GA=1.55e-3, WAKE=0.17, LD=1.0, LR=1.0, FIRST=2.5),
+           dict(GA=1.1e-3, WAKE=0.15, LD=1.5, LR=2.0, GI=0.5, FIRST=5.5)],
+    SD=(3,), MG=0, FIRST=7.0, I3=1, MS=(0, 0, 0, 0),
+    BLOCKS="bm0 la0 lm0 lf0 bm1 sw1 be0 fm01 fm02 fm03 la1 lm1 le0 lf1 bm2 sw2 be1 sd1 fe01 fe02 fe03 fm12 fm13 le1 la2 lm2 lf2 "
+           "bm3 sw3 be2 sd2 fe12 fe13 fm23 le2 be3 sd3 fe23 la3 lm3 lf3 om oe le3")
+XW, FW = 4112, 4160
+POOL = {"D": ["D0", "D1"], "L": ["L0", "NB"], "H": ["L1"], "M": ["CM"], "E": ["CE"], "N": ["L0", "NB"], "T": ["TP"]}
 
-f32, bf, i32, u16 = "float32", "bfloat16", "int32", "uint16"
+f32, bf, f16, i32, u16 = "float32", "bfloat16", "float16", "int32", "uint16"
 SCRATCH = {
-    "Y0": ("sbuf", [128, 40, 16], i32), "Yf": ("sbuf", [128, 20, 32], f32), "OTf": ("sbuf", [128, 640], f32),
+    "OTf": ("sbuf", [128, 640], f32), "MH": ("sbuf", [128, S0], f16), "EH": ("sbuf", [128, S0], f16), "FH": ("sbuf", [128, S0], f16),
+    "QH": ("sbuf", [128, 288], f16), "SELH": ("sbuf", [128, 144], f16), "AB": ("sbuf", [128, 3 * C], bf),
+    "L1": ("psum", [128, 16, 32], f32),
     "MI": ("sbuf", [128, S0], i32), "EI": ("sbuf", [128, S0], i32), "X": ("sbuf", [128, XW], bf),
-    "CMP": ("sbuf", [128, 32 * S0], bf), "XE": ("sbuf", [128, 16 * S0], bf),
-    "NX": ("sbuf", [128, 6 * 768], bf), "NC": ("sbuf", [128, 3 * 768], bf),
-    "F": ("sbuf", [128, FW], f32), "FX": ("sbuf", [128, 768], f32),
+    "NC": ("sbuf", [128, 12 * 768], bf), "XF": ("sbuf", [128, 6 * 192], bf),
+    "F": ("sbuf", [128, FW], f32), "FX": ("sbuf", [128, 768], f32), "OT": ("sbuf", [128, 20 * 128], f32),
     "MP": ("sbuf", [128, NS], f32), "ER": ("sbuf", [128, NS], f32), "LP": ("sbuf", [128, NS], f32),
     "FM": ("sbuf", [128, S0], f32),
-    "WB": ("sbuf", [128, NS], bf), "HAS": ("sbuf", [128, NS], bf), "PP": ("sbuf", [128, NS], bf),
-    "JK": ("sbuf", [128, 3 * NS], bf), "ACC": ("sbuf", [128, 48], f32),
-    "IDS": ("sbuf", [128, 16], u16), "OLS": ("sbuf", [128, 16], u16), "ELS": ("sbuf", [128, C], u16),
+    "WB": ("sbuf", [128, NS], bf), "HAS": ("sbuf", [128, NS], bf), "PP": ("sbuf", [128, 368], bf),
+    "HW": ("sbuf", [128, 32], bf), "RR": ("sbuf", [128, 32], bf), "PW": ("sbuf", [128, 4 * C], bf), "Z": ("sbuf", [128, C], bf),
+    "JK": ("sbuf", [128, 6 * 416], bf), "ACC": ("sbuf", [128, 48], f32),
+    "IDS": ("sbuf", [128, 32], u16),
     "YM": ("sbuf", [128, NS], f32), "YI": ("sbuf", [128, NS], f32),
-    "PI": ("sbuf", [128, 8], i32), "COL": ("sbuf", [128, 24], f32),
-    "IA": ("sbuf", [128, 128], f32), "ID": ("sbuf", [128, 128], f32), "IX": ("sbuf", [128, 144], f32),
-    "IC": ("sbuf", [128, C], f32), "DIAG": ("sbuf", [128, C], f32), "RST": ("sbuf", [128, C], f32),
+    "PI": ("sbuf", [128, 8], i32), "COL": ("sbuf", [128, 32], f32),
+    "IA": ("sbuf", [128, 128], f32), "ID": ("sbuf", [128, 128], f32), "IX": ("sbuf", [128, 288], f32),
+    "IK": ("sbuf", [128, C], f32), "U": ("sbuf", [128, 1040], f32), "PO": ("sbuf", [128, 416], bf),
+    "CJ": ("sbuf", [128, 96], f32), "CI": ("sbuf", [128, 64], i32), "CL": ("sbuf", [128, 8], u16), "CG": ("sbuf", [128, 48], u16), "ZER": ("sbuf", [128, C], f32),
     "ONEF": ("sbuf", [128, 128], f32), "ONEB": ("sbuf", [128, 128], bf), "TRI": ("sbuf", [128, 128], f32),
     "IDF": ("sbuf", [128, 128], f32), "IDB": ("sbuf", [128, 128], bf), "NEG": ("sbuf", [128, 128], bf),
-    "SEL": ("sbuf", [128, 144], bf), "SELF": ("sbuf", [128, 144], f32), "ZER": ("sbuf", [128, C], f32),
-    "D0": ("psum", [128, 1024], f32), "D1": ("psum", [128, 1024], f32),
-    "CM": ("psum", [128, 512], f32), "CE": ("psum", [128, 512], f32),
-    "LB": ("psum", [128, 512], f32), "NB": ("psum", [128, 512], f32),
+    "I8": ("sbuf", [128, 128], f32), "IH": ("sbuf", [128, 128], f32), "TL": ("sbuf", [128, 128], bf), "TU": ("sbuf", [128, 128], bf),
+    "SEL": ("sbuf", [128, 144], bf), "SELF": ("sbuf", [128, 144], f32),
+    "TP": ("psum", [128, 16, 32], f32),
 }
+for _b in ("D0", "D1", "L0", "CM", "CE", "NB"):
+    SCRATCH[_b] = ("psum", [128, 512], f32)
 for _t in range(NT):
-    SCRATCH["LST%d" % _t] = ("sbuf", [128, 664], u16)
-    SCRATCH["XL%d" % _t] = ("sbuf", [128, RV * S0], bf)
+    SCRATCH["LST%d" % _t] = ("sbuf", [128, 656], u16)
+    SCRATCH["XL%d" % _t] = ("sbuf", [128, 4 * S0], bf)
+    SCRATCH["CMP%d" % _t] = ("sbuf", [128, 32 * S0], bf)
     SCRATCH["RW%d" % _t] = ("sbuf", [128, NS], bf)
     SCRATCH["RD%d" % _t] = ("sbuf", [128, NS], bf)
-    SCRATCH["W%d" % _t] = ("sbuf", [128, 10 * C], f32)
+    SCRATCH["W%d" % _t] = ("sbuf", [128, 11 * C], f32)
+    SCRATCH["SN%d" % _t] = ("sbuf", [128, 224], u16)
     if _t:
         SCRATCH["OUT%d" % _t] = ("sbuf", [128, 2 * NS], bf)
-        SCRATCH["NL%d" % _t] = ("sbuf", [128, 3 * C * _t], u16)
-    if _t < NT - 1:
-        SCRATCH["SN%d" % _t] = ("sbuf", [128, 3 * C], u16)
+        SCRATCH["NL%d" % _t] = ("sbuf", [128, 160 * _t], u16)
 
-SEMAPHORES = (["eV", "eS", "eP", "eG", "sent", "ldY", "ldM", "ldE", "ldX", "stored"]
-              + ["rep%d" % t for t in range(NT)]
+SEMAPHORES = (["eV", "eS", "eP", "eG", "sent", "lst0", "ldM", "ldE", "ldX", "stored"]
+              + [n + str(t) for n in ("rep", "fd") for t in range(NT)]
               + [n + str(t) for n in ("lst", "rw", "rd") for t in (1, 2, 3)]
+              + ["adde%d_%d" % (t, i) for t in range(NT) for i in range(TUNE["FPE"][t], TUNE["FS"][t], TUNE["RA"])]
+              + ["addm%d_%d" % (t, i) for t in range(NT) for i in range(16 - TUNE["MS"][t], 16, TUNE["RA"])]
               + ["%s%d%d" % (n, k, t) for n in ("nm", "ne", "nw", "nd") for k, t in PAIRS])
-BANK = ("D0", "D1", "CM", "CE", "LB", "NB")
+CY, PE, GA, SC, WAKE = 0.83e-3, 0.42e-3, 1.3e-3, 3.2e-3, 0.06
 
 
-def build():
-    ops, last = [], {}
+def build(P):
+    ops, last, tail, bank, nbank = [], {}, {}, {}, [0]
+    FS, RV, GA, PE, VA, VG, SA = P["FS"], P["RV"], P["GA"], P["PE"], P["VA"], P["VG"], P["SA"]
 
-    def add(eng, fn, rd, wr, sem=None, sends=None):
+    def add(eng, fn, rd, wr, dur, lat=0.0, sem=None, sends=None, chain=None):
         me, deps = len(ops), set()
         for (b, lo, hi) in rd:
             deps.update(o for (l2, h2, o, w) in last.get(b, []) if w and l2 < hi and lo < h2)
@@ -79,17 +83,25 @@ def build():
             last[b] = [e for e in last.get(b, []) if not (lo <= e[0] and e[1] <= hi)] + [(lo, hi, me, True)]
         for (b, lo, hi) in rd:
             last.setdefault(b, []).append((lo, hi, me, False))
-        ops.append(dict(eng=eng, fn=fn, deps=deps, sem=sem, sends=sends, rd=rd, wr=wr))
+        ops.append(dict(eng=eng, fn=fn, deps=deps, sem=sem, sends=sends, rd=rd, wr=wr, dur=dur, lat=lat,
+                        after=tail.get(chain), banks={r[0] for r in rd + wr if "#" in r[0]}))
+        if chain:
+            tail[chain] = me
 
-    def ap(T, r):
-        return T[r[0]][:, r[1]:r[2]]
+    def psum(pool):
+        nbank[0] += 1
+        return "%s#%d" % (pool, nbank[0])
+
+    def ap(T, r, step=1):
+        if r[0][:2] == "H#":
+            return T.L1[:, 0, r[1]:r[2]]
+        return T[bank.get(r[0], r[0])][:, r[1]:r[2]:step] if step > 1 else T[bank.get(r[0], r[0])][:, r[1]:r[2]]
 
     def ind(T, w, o):
         return ap(T, w).indirect(ap(T, o))
 
     def rw(rd, wr):
-        return ([r for r in rd if r[0] not in BANK],
-                [r for r in wr if r[0] not in BANK] + [(r[0], 0, 1024) for r in rd + wr if r[0] in BANK])
+        return [[(r[0], 0, 512) if "#" in r[0] else r for r in x] for x in (rd, wr)]
 
     def col(j):
         return ("COL", j, j + 1)
@@ -97,42 +109,46 @@ def build():
     def sv(T, s):
         return ap(T, s) if isinstance(s, tuple) else s
 
-    def ts(out, in0, s1, s2, op0, op1=None, step=1):
-        def fn(g, T, cx):
-            a = T[in0[0]][:, in0[1] + step - 1:in0[2]:step] if step > 1 else ap(T, in0)
-            if op1 is None:
-                return [g.vector.tensor_scalar(ap(T, out), a, sv(T, s1), None, op0)]
-            return [g.vector.tensor_scalar(ap(T, out), a, sv(T, s1), sv(T, s2), op0, op1)]
-        add("V", fn, *rw([in0] + [s for s in (s1, s2) if isinstance(s, tuple)], [out]))
+    def wid(r):
+        return r[2] - r[1]
 
-    def flip(out, in0, step=1, k=1.0):
-        ts(out, in0, -k, float(NV), ALU.mult, ALU.add, step)
+    def ts(out, in0, s1, s2, op0, op1=None):
+        def fn(g, T, cx):
+            if op1 is None:
+                return [g.vector.tensor_scalar(ap(T, out), ap(T, in0), sv(T, s1), None, op0)]
+            return [g.vector.tensor_scalar(ap(T, out), ap(T, in0), sv(T, s1), sv(T, s2), op0, op1)]
+        add("V", fn, *rw([in0] + [s for s in (s1, s2) if isinstance(s, tuple)], [out]), VA + wid(out) * CY)
+
+    def flip(out, in0, k=1.0):
+        ts(out, in0, -k, float(NV), ALU.mult, ALU.add)
 
     def tt(out, in0, in1, op):
-        add("V", lambda g, T, cx: [g.vector.tensor_tensor(ap(T, out), ap(T, in0), ap(T, in1), op)], *rw([in0, in1], [out]))
+        add("V", lambda g, T, cx: [g.vector.tensor_tensor(ap(T, out), ap(T, in0), ap(T, in1), op)], *rw([in0, in1], [out]),
+            VA + wid(out) * (1 if "#" in in0[0] + in1[0] else 2) * CY)
 
-    def gtt(out, win, off, in1, op):
+    def gtt(out, win, off, in1, op, chain=None):
         add("V", lambda g, T, cx: [g.vector.tensor_tensor(ap(T, out), ind(T, win, off), ap(T, in1), op)],
-            [win, off, in1], [out])
+            [win, off, in1], [out], VG + wid(out) * GA, chain=chain)
 
-    def vcopy(out, in0):
-        add("V", lambda g, T, cx: [g.vector.tensor_copy(ap(T, out), ap(T, in0))], [in0], [out])
+    def vcopy(out, in0, k=1.0):
+        add("V", lambda g, T, cx: [g.vector.tensor_copy(ap(T, out), ap(T, in0))], [in0], [out], VA + wid(out) * k * CY)
 
-    def vgather(out, win, off):
-        add("V", lambda g, T, cx: [g.vector.tensor_copy(ap(T, out), ind(T, win, off))], [win, off], [out])
+    def regather(out, win, off, k0, k1):
+        add("V", lambda g, T, cx: [g.vector.tensor_scalar(ap(T, out), ind(T, win, off), k0, k1, ALU.mult, ALU.add)],
+            [win, off], [out], VG + wid(out) * GA)
 
     def vscatter(win, off, in0, in1=None):
         def fn(g, T, cx):
             if in1 is None:
                 return [g.vector.tensor_copy(ind(T, win, off), ap(T, in0))]
             return [g.vector.tensor_tensor(ind(T, win, off), ap(T, in0), ap(T, in1), ALU.subtract)]
-        add("V", fn, [off, in0] + ([in1] if in1 else []), [win])
+        add("V", fn, [off, in0] + ([in1] if in1 else []), [win], VG + wid(in0) * SC)
 
-    def scan(out, d0, d1, op0, op1, init=0.0):
-        add("V", lambda g, T, cx: [g.vector.tensor_tensor_scan(ap(T, out), ap(T, d0), ap(T, d1), sv(T, init), op0, op1)],
-            [d0, d1] + ([init] if init else []), [out])
+    def scan(out, d0, init=0.0):
+        add("V", lambda g, T, cx: [g.vector.tensor_tensor_scan(ap(T, out), ap(T, d0), ap(T, d0), sv(T, init), ALU.add, ALU.max)],
+            [d0] + ([init] if init else []), [out], VA + wid(out) / 2 * CY)
 
-    def act(out, in0, func, bias=None, scale=None, acc=None, off=None):
+    def act(out, in0, func, bias=None, scale=None, acc=None, off=None, chain=None):
         def fn(g, T, cx):
             kw = {}
             if bias is not None:
@@ -142,88 +158,127 @@ def build():
             if acc is not None:
                 kw["accum_out"] = ap(T, acc)
             return [g.scalar.activation(ap(T, out), ap(T, in0) if off is None else ind(T, in0, off), func, **kw)]
-        add("S", fn, *rw([in0] + [s for s in (bias, scale, off) if isinstance(s, tuple)], [out] if acc is None else [out, acc]))
+        add("S", fn, *rw([in0] + [s for s in (bias, scale, off) if isinstance(s, tuple)], [out] if acc is None else [out, acc]),
+            SA + wid(out) * (GA if off else CY), chain=chain)
 
     def mm(items):
         def fn(g, T, cx):
-            return [g.tensor.matmul(ap(T, o), ap(T, l), T[x[0]][:, x[1]:x[2]:st] if st > 1 else ap(T, x), a, z)
+            return [g.tensor.matmul(T.TP[:, 0:3, o[1]:o[2]] if o[0][0] == "T" else ap(T, o), ap(T, l), ap(T, x, st), a, z)
                     for (o, l, x, st, a, z) in items]
-        add("P", fn, *rw([i[1] for i in items] + [i[2] for i in items], [i[0] for i in items]))
+        add("P", fn, *rw([i[1] for i in items] + [i[2] for i in items], [i[0] for i in items]),
+            sum(max(64, wid(i[2]) // i[3]) * PE * (4 if SCRATCH[i[1][0]][2] == f32 else 1) for i in items))
 
-    def pick(out, sel, buf, lo, hi):
-        mm([(out, (sel, 15 - i, 143 - i), (buf, lo + i, hi), 16, i == 0, i == 15) for i in range(16)])
+    def pick(out, sel, buf, lo, hi, stop=True):
+        mm([(out, (sel, 16 - i, 144 - i), (buf, lo + i, hi), 16, i == 0, stop and i == 15) for i in range(16)])
 
-    def count_row(bank, i, rhs, key):
+    def count_row(b, i, rhs, after=()):
         def fn(g, T, cx):
-            k = cx.get(key, 0)
-            cx[key] = k + 1
-            return [g.tensor.matmul(T[bank][:, 0:S0], T.SEL[:, 15 - i:143 - i], ap(T, rhs), k == 0, k == 15)]
-        add("P", fn, [rhs, ("SEL", 0, 144)], [(bank, i, i + 1)])
+            k = cx.get(b, 0)
+            cx[b] = k + 1
+            return [g.tensor.matmul(ap(T, (b, 0, wid(rhs))), T.SEL[:, 16 - i:144 - i], ap(T, rhs), k == 0, k == (14 if b[0] == "M" else 15))]
+        add("P", fn, [rhs, ("SEL", 0, 144), *after], [(b, i, i + 1)], max(64, wid(rhs)) * PE)
 
     def iota(out, pat, base, cm, flt=True):
         def fn(g, T, cx):
             if flt:
                 return [g.iota(ap(T, out), pat, base, cm, allow_small_or_imprecise_dtypes=True)]
             return [g.iota(ap(T, out), pat, base, cm)]
-        add("G", fn, [], [out])
+        add("G", fn, [], [out], 0.13 + 2 * wid(out) * CY)
 
     def fill(out, v):
-        iota(out, [[0, out[2] - out[1]]], v, 0)
+        iota(out, [[0, wid(out)]], v, 0)
 
-    def send(tr):
-        add("G", None, [x[0] for x in tr], [x[1] for x in tr], sends=tr)
+    def dma(q, fn, rd, wr, sem, kb):
+        add(q, lambda g, T, cx: [(g.sync if q == "Y" else g.scalar).dma_start(*fn(T))], rd, wr, 0.25, P["LD"] + kb / 300.0, sem)
 
-    add("Y", lambda g, T, cx: [g.sync.dma_start(T.MI[:], T.mem0[:])], [], [("MI", 0, S0)], "ldM")
-    k = 0
-    for G in range(4):
-        for kind in range(2):
-            for g0 in range(2):
-                def fn(g, T, cx, G=G, kind=kind, g0=g0, q=k % 2):
-                    src = (T.mem0, T.inv0)[kind][32 * G + 16 * g0:32 * G + 16 * g0 + 16, :]
-                    dst = T.Y0[32 * G + 16 * kind:32 * G + 16 * kind + 16, 20 * g0:20 * g0 + 20, :]
-                    return [(g.scalar, g.sync)[q].dma_start(dst, src)]
-                add("SY"[k % 2], fn, [], [("Y0", k, k + 1)], "ldY")
-                k += 1
-    add("S", lambda g, T, cx: [g.scalar.dma_start(T.X[:, 0:2048], T.xs[:, 0:2048])], [], [("X", 0, 2048)], "ldX")
-    add("Y", lambda g, T, cx: [g.sync.dma_start(T.X[:, 2048:NV], T.xs[:, 2048:NV])], [], [("X", 2048, NV)], "ldX")
-    add("Y", lambda g, T, cx: [g.sync.dma_start(T.EI[:], T.inv0[:])], [], [("EI", 0, S0)], "ldE")
+    def send(tr, first=0.0):
+        add("G", None, [x[0] for x in tr], [x[1] for x in tr], P["GI"] + first, P["LR"] + wid(tr[0][0]) * len(tr) / 500.0, sends=tr)
+
+    dma("Y", lambda T: (T.MI[0:64, :], T.mem0[0:64, :]), [], [("MI", 0, 1)], "ldM", 160)
+    dma("S", lambda T: (T.MI[64:128, :], T.mem0[64:128, :]), [], [("MI", 1, S0)], "ldM", 160)
+    dma("S", lambda T: (T.EI[:], T.inv0[:]), [], [("EI", 0, S0)], "ldE", 320)
+    dma("Y", lambda T: (T.X[:, 0:2048], T.xs[:, 0:2048]), [], [("X", 0, 2048)], "ldX", 1100)
+    dma("S", lambda T: (T.X[:, 2048:NV], T.xs[:, 2048:NV]), [], [("X", 2048, NV)], "ldX", 1100)
+    nload = len(ops)
 
     iota(("PI", 0, 1), [[0, 1]], 0, 1, flt=False)
     iota(("IA", 0, 128), [[1, 8], [0, 16]], 0, 0)
     iota(("ID", 0, 128), [[1, 128]], 0, -1)
-    iota(("IC", 0, C), [[0, 3], [1, 16]], 0, 0)
-    iota(("IX", 0, 144), [[1, 144]], -15, 0)
-    iota(("LP", S0, NS), [[0, 4], [-1, C]], -1, 0)
-    for j in range(4):
-        fill(("F", j * FW // 4, (j + 1) * FW // 4), 0)
+    iota(("IK", 0, C), [[1, C]], 0, 0)
+    iota(("IX", 0, 144), [[1, 144]], -16, 0)
+    iota(("IX", 144, 288), [[1, 144]], 128, 0)
+    iota(("LP", S0, NS), [[0, 4], [1, C]], NV + 1, 0)
+    fill(("ACC", 44, 47), 0)
+    fill(("ACC", 47, 48), 1)
+    for j in range(13):
+        fill(("F", j * FW // 13, (j + 1) * FW // 13), 0)
     ts(("PI", 2, 3), ("PI", 0, 1), 4, None, ALU.arith_shift_right)
     ts(("PI", 3, 4), ("PI", 0, 1), 15, None, ALU.bitwise_and)
-    vcopy(("COL", 0, 2), ("PI", 2, 4))
+    ts(("PI", 4, 5), ("PI", 0, 1), 4, 1, ALU.arith_shift_right, ALU.bitwise_and)
+    vcopy(("COL", 0, 3), ("PI", 2, 5))
     ts(("ONEF", 0, 128), ("IA", 0, 128), col(0), None, ALU.is_equal)
     ts(("TRI", 0, 128), ("ID", 0, 128), 0.0, -BIG, ALU.is_gt, ALU.mult)
     tt(("TRI", 0, 128), ("TRI", 0, 128), ("ONEF", 0, 128), ALU.mult)
     ts(("IDF", 0, 128), ("ID", 0, 128), 0.0, None, ALU.is_equal)
     tt(("TRI", 0, 128), ("TRI", 0, 128), ("IDF", 0, 128), ALU.add)
-    ts(("DIAG", 0, C), ("IC", 0, C), col(1), None, ALU.is_equal)
-    ts(("RST", 0, C), ("IC", 0, C), 0.0, None, ALU.is_gt)
-    ts(col(2), col(0), 16.0, None, ALU.mult)
-    ts(("SEL", 0, 144), ("IX", 0, 144), col(2), None, ALU.is_equal)
-    act(("SELF", 0, 144), ("SEL", 0, 144), AF.Copy, scale=1.0 / 16)
+    ts(col(3), col(0), 16.0, None, ALU.mult)
+    ts(("SEL", 0, 144), ("IX", 0, 144), col(3), None, ALU.is_equal)
+    ts(col(7), col(2), 128.0, col(3), ALU.mult, ALU.add)
+    ts(("SELH", 0, 144), ("IX", 0, 144), col(3), None, ALU.is_equal)
+    ts(("QH", 0, 288), ("IX", 0, 288), col(7), col(1), ALU.subtract, ALU.is_equal)
+    ts(col(21), col(1), 0.0, -1.0, ALU.is_equal, ALU.mult)
+    act(col(20), col(21), AF.Copy, scale=-float(NV))
+    ts(col(22), col(1), 1.0, BIG, ALU.is_ge, ALU.mult)
+    ts(col(23), col(1), 2.0, BIG, ALU.is_ge, ALU.mult)
+    for t in range(NT):
+        act(col(24 + t), col(22), AF.Copy, scale=float(TB[t]))
+        if t:
+            act(col(27 + t), col(23), AF.Copy, scale=float(TB[t]))
+    act(("CJ", 0, 40), ("IK", 0, 40), AF.Identity, bias=col(1), scale=16.0)
+    act(("CJ", 40, 80), ("CJ", 0, 40), AF.Identity, bias=10.5 / 20, scale=1.0 / 20)
+    vcopy(("CI", 0, 40), ("CJ", 40, 80))
+    ts(("CJ", 40, 80), ("CI", 0, 40), -639.0 / 32, 20.0, ALU.mult, ALU.add)
+    tt(("CJ", 40, 80), ("CJ", 40, 80), ("CJ", 0, 40), ALU.add)
+    ts(("CG", 0, 20), ("CJ", 40, 60), 32.0, None, ALU.mult)
+    ts(("CG", 20, 40), ("CJ", 59, 79), 32.0, None, ALU.mult)
+    act(("CJ", 80, 84), ("CJ", 0, 4), AF.Identity, bias=-1.0 / 3, scale=1.0 / 3)
+    vcopy(("CI", 40, 44), ("CJ", 80, 84))
+    ts(("CJ", 84, 88), ("CI", 40, 44), -3.0, col(2), ALU.mult, ALU.add)
+    tt(("CJ", 84, 88), ("CJ", 84, 88), ("CJ", 0, 4), ALU.add)
+    tt(("CI", 44, 48), ("CJ", 84, 88), ("ACC", 44, 48), ALU.add)
+    ts(("CI", 48, 52), ("CI", 44, 48), 1, None, ALU.bitwise_and)
+    ts(("CJ", 88, 92), ("CI", 48, 52), 7.0, None, ALU.mult)
+    tt(("CJ", 88, 92), ("CJ", 88, 92), ("CJ", 0, 4), ALU.add)
+    ts(("CJ", 92, 96), ("CI", 40, 44), -47.0 / 16, None, ALU.mult)
+    tt(("CJ", 88, 92), ("CJ", 88, 92), ("CJ", 92, 96), ALU.add)
+    ts(("CL", 0, 3), ("CJ", 88, 91), 16.0, None, ALU.mult)
+    ts(("CL", 3, 4), ("CJ", 91, 92), 16.0, 32.0, ALU.mult, ALU.add)
+    act(("SELF", 0, 144), ("SEL", 0, 144), AF.Copy)
     act(("ONEB", 0, 128), ("ONEF", 0, 128), AF.Copy)
     act(("IDB", 0, 128), ("IDF", 0, 128), AF.Copy)
     act(("NEG", 0, 128), ("IDF", 0, 128), AF.Copy, scale=-1.0)
-    ts(("COL", 4, 7), ("IC", 0, 3), 16.0, 0.5, ALU.mult, ALU.add)
+    if len(P["LA"]) < NT:
+        act(("I8", 0, 128), ("IDF", 0, 128), AF.Copy, scale=8.0)
+        act(("IH", 0, 128), ("IDF", 0, 128), AF.Copy, scale=0.5)
+        act(("TU", 0, 128), ("TRI", 0, 128), AF.Abs)
+        act(("TL", 0, 128), ("TU", 0, 128), AF.Sign)
+        tt(("TU", 0, 128), ("ONEB", 0, 128), ("TL", 0, 128), ALU.subtract)
+    ts(("COL", 4, 7), ("IK", 0, 3), 16.0, 0.5, ALU.mult, ALU.add)
     ts(("COL", 4, 7), ("COL", 4, 7), col(1), None, ALU.add)
     scol = {}
     for t in range(NT):
-        if FS[t] not in scol:
-            j = scol[FS[t]] = 8 + 2 * len(scol)
-            ts(col(j), col(1), float(FS[t]), None, ALU.is_lt)
-            ts(col(j + 1), col(j), BIG / 2, -BIG, ALU.mult, ALU.add)
-        ts(col(16 + t), col(scol[FS[t]]), -8 * BIG, BIG * TA[t], ALU.mult, ALU.add)
+        fp = min(FS[t], P["FPE"][t])
+        if fp not in scol:
+            j = scol[fp] = 8 + 2 * len(scol)
+            ts(col(j), col(1), float(fp), None, ALU.is_lt)
+            act(col(j + 1), col(j), AF.Identity, bias=-BIG, scale=BIG / 2)
+        act(col(16 + t), col(scol[fp]), AF.Identity, bias=BIG * TA[t], scale=-8 * BIG)
     fill(("X", NV, XW), 0)
     fill(("ZER", 0, C), 0)
-    fill(("CMP", 0, S0), 1)
+    for j in range(2 * NT + 1):
+        fill(("U", 112 * j, 112 * j + 16), 0)
+    fill(("RR", 0, 1), 0)
+    fill(("PW", 0, 4 * C), 256)
     fill(("HAS", S0, NS), 1)
     fill(("MP", S0, NS), 0)
     fill(("ER", S0, NS), NV)
@@ -233,218 +288,476 @@ def build():
         fill(("RD%d" % t, n, NS), 0)
 
     flip(("MP", 0, S0), ("MI", 0, S0))
-    mm([(("LB", 0, S0), ("TRI", 0, 128), ("MP", 0, S0), 1, True, True)])
-    act(("FM", 0, S0), ("LB", 0, S0), AF.Relu)
-    pick(("NB", 0, 20), "SELF", "FM", 0, S0)
-    mm([(("LB", 0, S0), ("ONEF", 0, 128), ("FM", 0, S0), 1, True, True)])
-    act(("LP", 0, S0), ("LB", 0, S0), AF.Copy)
-    flip(("LST0", 640, 660), ("NB", 0, 20), k=16.0)
-    for g0 in range(2):
-        add("V", lambda g, T, cx, g0=g0: [g.vector.tensor_copy(T.Yf[:, :, 16 * g0:16 * g0 + 16], T.Y0[:, 20 * g0:20 * g0 + 20, :])],
-            [("Y0", 0, 16)], [("Yf", g0, g0 + 1)])
-    for a in range(20):
-        add("V", lambda g, T, cx, a=a: [g.vector.transpose(T.OTf[:, a:640:20], T.Yf[:, a, :])], [("Yf", 0, 2)], [("OTv", a, a + 1)])
-    for h in (1, 0):
-        add("V", lambda g, T, cx, h=h: [g.vector.tensor_copy(T.LST0[:, S0 * h:S0 * h + S0], T.OTf[:, S0 * h:S0 * h + S0])],
-            [("OTv", 0, 20)], [("LST0", S0 * h, S0 * h + S0)])
+    b = psum("L")
+    mm([((b, 0, S0), ("TRI", 0, 128), ("MP", 0, S0), 1, True, True)])
+    ts(("FH", 0, S0), (b, 0, S0), 0.0, -2048.0, ALU.max, ALU.add)
+    add("S", lambda g, T, cx, b=b: [g.scalar.activation(T.FM[:], ap(T, (b, 0, S0)), AF.Relu)], [], [(b, 0, 512), ("FM", 0, S0)], SA + S0 * CY)
+    b = psum("N")
+    pick((b, 0, 20), "SELH", "FH", 0, S0)
+    ts(("LST0", 0, 20), (b, 0, 20), -1.0, NV - 16 * 2048.0, ALU.mult, ALU.add)
+    b = psum("L")
+    mm([((b, 0, S0), ("ONEF", 0, 128), ("FM", 0, S0), 1, True, True)])
+    act(("LP", 0, S0), (b, 0, S0), AF.Identity, bias=float(NV), scale=-1.0)
+    ts(("MH", 0, S0), ("MI", 0, S0), -1.0, 2048.0, ALU.mult, ALU.add)
+    ts(("EH", 0, S0), ("EI", 0, S0), -1.0, 2048.0, ALU.mult, ALU.add)
+    for b, a0, a1 in ((psum("T"), 0, 16), (psum("H"), 16, 20)):
+        for g0 in range(2):
+            def fn(g, T, cx, b=b, a0=a0, a1=a1, g0=g0):
+                parts = (("QH", 16 + 144 * g0, "MH"), ("QH", 144 * g0, "EH"))
+                return [g.tensor.matmul(T[bank[b]][:, 0:a1 - a0, 16 * g0:16 * g0 + 16], T[m][:, lo:lo + 128], T[x][:, 16 * a0:16 * a1],
+                                        j == 0, j == 1) for j, (m, lo, x) in enumerate(parts)]
+            add("P", fn, [("QH", 0, 288), ("MH", 0, S0), ("EH", 0, S0)], [(b, 0, 512)], 32 * (a1 - a0) * PE)
+        add("V", lambda g, T, cx, b=b, a0=a0, a1=a1: [g.vector.transpose(T.OTf[:, 32 * a0:32 * a1], T[bank[b]][:, 0:a1 - a0, :])],
+            [(b, 0, 512)], [("OTf", 32 * a0, 32 * a1)], VA + 32 * (a1 - a0) * CY)
+    for lo, hi, j in ((20, 324, 0), (324, 644, 20)):
+        regather(("LST0", lo, hi), ("OTf", 0, 640), ("CG", j, j + (hi - lo) // 16), -1.0, 2048.0)
     vcopy(("ER", 0, S0), ("EI", 0, S0))
-    src = ("LST0", 0, 660)
-    send([(src, ("LST1", 0, 660), 1, "lst1")])
-    send([(src, ("LST%d" % t, 0, 660), t, "lst%d" % t) for t in (2, 3)])
+    send([(("LST0", 0, S0), ("LST1", 0, S0), 1, "lst0")], P["FIRST"])
+    send([(("LST0", S0, 640), ("LST1", S0, 640), 1, "lst1")])
+    send([(("LST0", 0, 640), ("LST%d" % t, 0, 640), t, "lst%d" % t) for t in (2, 3)])
 
     XA = ("X", 0, XW)
-    dcount, ncount = [0], [0]
 
-    def rows(t, i0, i1, op, single):
-        L, XL = "LST%d" % t, "XL%d" % t
-        i = i0
+    def by_vector(b, n, per, i0, i1, lst, cmp_, lead, op, single=0, chain=None):
+        i, k = i0, n // 16
         while i < i1:
-            m = 1 if i - i0 < single else min(RV, i1 - i)
-            gtt(("CMP", S0 * i, S0 * (i + m)), XA, (L, 20 * i, 20 * (i + m)), (XL, 0, S0 * m), op)
-            for j in range(i, i + m):
-                count_row("CM" if j < 16 else "CE", j % 16, ("CMP", S0 * j, S0 * j + S0), "ME"[j // 16] + str(t))
+            m = 1 if i - i0 < single else min(per, i1 - i)
+            gtt((cmp_[0], cmp_[1] + n * i, cmp_[1] + n * (i + m)), XA, (lst[0], lst[1] + k * i, lst[1] + k * (i + m)),
+                (lead[0], lead[1], lead[1] + n * m), op, chain)
+            for j in range(i, i + m if b else i):
+                count_row(b, j, (cmp_[0], cmp_[1] + n * j, cmp_[1] + n * j + n))
             i += m
 
-    def bulk_m(t):
+    def by_scalar(b, n, rows, piece, lst, cmp_, lead, nl, chain=None):
+        done = 0
+        for lo in range(0, n * rows, piece):
+            hi, D = min(lo + piece, n * rows), psum("D")
+            x = (cmp_[0], cmp_[1] + lo, cmp_[1] + hi)
+            if lo // piece % P["GS"] == 0:
+                h2 = min(lo + piece * P["GS"], n * rows)
+                act((x[0], x[1], cmp_[1] + h2), XA, AF.Copy, off=(lst[0], lst[1] + lo // 16, lst[1] + h2 // 16), chain=chain)
+            cuts = [lo] + [c for c in range(0, n * rows, nl) if lo < c < hi] + [hi]
+            mm([((D, 0, hi - lo), ("IDB", 0, 128), x, 1, True, False)]
+               + [((D, u - lo, v - lo), ("NEG", 0, 128), (lead[0], lead[1] + u % nl, lead[1] + u % nl + v - u), 1, False, v == hi)
+                  for u, v in zip(cuts, cuts[1:])])
+            act((cmp_[0], cmp_[1] + lo, cmp_[1] + hi), (D, 0, hi - lo), AF.Sign, bias=2.0 ** -110, chain=chain)
+            while b and (done + 1) * n <= hi:
+                count_row(b, done, (cmp_[0], cmp_[1] + n * done, cmp_[1] + n * done + n))
+                done += 1
+
+    def by_adding(b, t, i0, i1, lst, cmp_, op, kind):
         L, XL = "LST%d" % t, "XL%d" % t
-        act((XL, 0, S0), XA, AF.Copy, off=(L, 640, 660))
-        for j in range(1, RV):
-            add("Y", lambda g, T, cx, j=j: [g.sync.dma_start(T[XL][:, S0 * j:S0 * j + S0], T[XL][:, 0:S0])],
-                [(XL, 0, S0)], [(XL, S0 * j, S0 * j + S0)], "rep%d" % t)
-        count_row("CM", 0, ("CMP", 0, S0), "M" + str(t))
-        rows(t, 1, 16, ALU.is_equal, LONE if t == 0 else 0)
+        for i in range(i0, i1, P["RA"]):
+            m = min(P["RA"], i1 - i)
+            x = (cmp_[0], cmp_[1] + S0 * i, cmp_[1] + S0 * (i + m))
+            for j in range(0, m, P["RG"]):
+                u = min(P["RG"], m - j)
+                act((x[0], x[1] + S0 * j, x[1] + S0 * (j + u)), XA, AF.Copy, scale=-1.0,
+                    off=(L, lst + 20 * (i + j), lst + 20 * (i + j + u)), chain="S%s%d" % (kind, t))
+            add("G", lambda g, T, cx, x=x, m=m: [g.dma_start(ap(T, x), T[XL][:, 0:S0 * m], accum_op=ALU.add)],
+                [(XL, 0, S0 * m), x], [x], P["GD"], P["LD"] + 160 * m / 300.0, "add%s%d_%d" % (kind, t, i))
+            add("V", lambda g, T, cx, x=x: [g.vector.tensor_scalar(ap(T, x), ap(T, x), 0.0, None, op)], [x], [x], VA + wid(x) * CY / 2)
+            for q in range(i, i + m):
+                count_row(b, q, (cmp_[0], cmp_[1] + S0 * q, cmp_[1] + S0 * q + S0))
+
+    def bulk_m(t):
+        L, XL, b = "LST%d" % t, "XL%d" % t, psum("M")
+        act((XL, 0, S0), XA, AF.Copy, off=(L, 0, 20))
+        for j in range(1, max(RV, P["RA"] if FS[t] > P["FPE"][t] or P["MS"][t] else 1)):
+            if t == 0 and P["LONE"] < 4:
+                act((XL, S0 * j, S0 * j + S0), (XL, 0, S0), AF.Copy)
+                continue
+            dma("Y", lambda T, j=j: (T[XL][:, S0 * j:S0 * j + S0], T[XL][:, 0:S0]), [(XL, 0, S0)], [(XL, S0 * j, S0 * j + S0)], "rep%d" % t, 80)
+        by_vector(b, S0, RV, 1, 16, (L, 0), ("CMP%d" % t, 0), (XL, 0), ALU.is_equal, P["LONE"] if t == 0 else 0, "Vm%d" % t)
         ow = ("RW0", 0, S0) if t == 0 else ("OUT%d" % t, 0, S0)
-        act(ow, ("CM", 0, S0), AF.Relu, bias=BIG * TB[t], scale=-BIG)
-        if t:
-            send([(ow, ("RW%d" % t, 0, S0), -t, "rw%d" % t)])
+        act(ow, (b, 0, S0), AF.Relu, bias=col(24 + t), scale=-BIG)
+
 
     def bulk_e(t):
-        L, XL, F = "LST%d" % t, "XL%d" % t, FS[t]
-        for p in range(F // 2):
-            D = "D%d" % (dcount[0] % 2)
-            dcount[0] += 1
-            if 2 * p % RS == 0:
-                m = min(RS, F - 2 * p)
-                act(("XE", 640 * p, 640 * p + S0 * m), XA, AF.Copy, off=(L, S0 + 40 * p, S0 + 40 * p + 20 * m))
-            it = []
-            for j in range(2):
-                o = (D, 192 + S0 * j, 512 + S0 * j)
-                it.append((o, ("NEG", 0, 128), (XL, 0, S0), 1, True, False))
-                it.append((o, ("IDB", 0, 128), ("XE", 640 * p + S0 * j, 640 * p + S0 * j + S0), 1, False, True))
-            mm(it)
-            c0 = S0 * (16 + 2 * p)
-            act(("CMP", c0, c0 + 640), (D, 192, 832), AF.Sign, bias=2.0 ** -110)
-            for j in range(2):
-                count_row("CE", 2 * p + j, ("CMP", c0 + S0 * j, c0 + S0 * j + S0), "E" + str(t))
-        rows(t, 16 + F, 32, ALU.is_ge, 0)
+        L, XL, b, cmp_ = "LST%d" % t, "XL%d" % t, psum("E"), ("CMP%d" % t, 16 * S0)
+        fp = min(FS[t], P["FPE"][t])
+        by_scalar(b, S0, fp, P["PIECE"], (L, S0), cmp_, (XL, 0), S0, "S%d" % t)
+        by_vector(b, S0, RV, FS[t], 16, (L, S0), cmp_, (XL, 0), ALU.is_ge, 0, "Ve%d" % t)
         od = ("RD0", 0, S0) if t == 0 else ("OUT%d" % t, NS, NS + S0)
-        act(od, ("CE", 0, S0), AF.Relu, bias=col(16 + t), scale=col(scol[F] + 1))
-        if t:
-            send([(od, ("RD%d" % t, 0, S0), -t, "rd%d" % t)])
+        act(od, (b, 0, S0), AF.Relu, bias=col(16 + t), scale=col(scol[fp] + 1))
 
-    def fresh(k, t, h):
-        NL, x, c = "NL%d" % t, 768 * PAIRS.index((k, t)), 768 * (ncount[0] % 3)
-        ncount[0] += 1
-        b, n = 3 * C * k, S0 + C * k
-        off, op, th, R, sm = ((b, ALU.is_equal, TB[t], "RW", "nw"), (b + 2 * C, ALU.is_ge, TA[t], "RD", "nd"))[h]
-        m = HALF if (h == 0 and t == k + 1) else 1
-        for j in range(m):
-            lo, hi = C * j // m, C * (j + 1) // m
-            if h == 0:
-                act(("NX", x + 16 * lo, x + 16 * hi), XA, AF.Copy, off=(NL, b + C + lo, b + C + hi))
-            gtt(("NC", c + 16 * lo, c + 16 * hi), XA, (NL, off + lo, off + hi), ("NX", x + 16 * lo, x + 16 * hi), op)
-        pick(("NB", 0, C), "SEL", "NC", c, c + 768)
-        o = ("OUT%d" % t, NS * h + n, NS * h + n + C)
-        act(o, ("NB", 0, C), AF.Relu, bias=BIG * th, scale=-BIG)
-        send([(o, (R + str(t), n, n + C), -t, "%s%d%d" % (sm, k, t))])
+    def back_m(t):
+        n = S0 + C * (t - 1) * P["MG"]
+        send([(("OUT%d" % t, 0, n), ("RW%d" % t, 0, n), -t, "rw%d" % t)])
 
-    def share(k, lo, hi, sm):
-        s = ("SN%d" % k, lo, hi)
-        tr = [(s, ("NL%d" % t, 3 * C * k + lo, 3 * C * k + hi), t, "%s%d%d" % (sm, k, t)) for t in range(k + 1, NT)]
+    def back_e(t):
+        n = S0 + C * (t - 1 if t in P["SD"] else t) * P["MG"]
+        send([(("OUT%d" % t, NS, NS + n), ("RD%d" % t, 0, n), -t, "rd%d" % t)])
+
+    def count_all(b, c, i0, i1, first=True, stop=True):
+        mm([((b, 0, C), ("SEL", 16 - i, 144 - i), ("NC", c + C * i, c + C * i + C), 1, first and i == i0, stop and i == i1 - 1)
+            for i in range(i0, i1)])
+
+    def fresh_m(k, t):
+        NL, p, b, n = "NL%d" % t, PAIRS.index((k, t)), psum("N"), S0 + C * k
+        x, c = 192 * p, 1536 * p
+        act(("XF", x, x + 4 * C), XA, AF.Copy, off=(NL, 160 * k + C, 160 * k + C + 12))
+        by_vector(None, C, 4, 2, 16, (NL, 160 * k), ("NC", c), ("XF", x), ALU.is_equal)
+        if t == k + 1:
+            count_all(b, c, 2, 10, stop=False)
+            count_all(b, c, 10, 14, False, False)
+            count_all(b, c, 14, 16, False)
+        else:
+            count_all(b, c, 2, 16)
+        o = ("OUT%d" % t, n, n + C)
+        act(o, (b, 0, C), AF.Relu, bias=col(27 + t), scale=-BIG)
+        if t == k + 1 or not P["MG"]:
+            send([(o, ("RW%d" % t, n, n + C), -t, "nw%d%d" % (k, t))])
+
+    def fresh_e(k, t):
+        NL, p, b, n = "NL%d" % t, PAIRS.index((k, t)), psum("N"), S0 + C * k
+        o, lst, cmp_, lead = ("OUT%d" % t, NS + n, NS + n + C), (NL, 160 * k + 64), ("NC", 1536 * p + 768), ("XF", 192 * p)
+        if P["FB"][p] == "S":
+            by_scalar(None, C, 16, 384, lst, cmp_, lead, 192)
+        else:
+            by_vector(None, C, 4, 0, 16, lst, cmp_, lead, ALU.is_ge)
+        if t == k + 1:
+            count_all(b, cmp_[1], 0, 12, stop=False)
+            count_all(b, cmp_[1], 12, 16, False)
+        else:
+            count_all(b, cmp_[1], 0, 16)
+        if P["FB"][p] == "S":
+            act(o, (b, 0, C), AF.Relu, bias=BIG * (TA[t] - 8), scale=-BIG / 2)
+        else:
+            act(o, (b, 0, C), AF.Relu, bias=BIG * TA[t], scale=-BIG)
+        if t == k + 1 and t in P["SD"] or not P["MG"]:
+            send([(o, ("RD%d" % t, n, n + C), -t, "nd%d%d" % (k, t))])
+
+    def share(k, lo, hi, hi2, sm):
+        tr = [(("SN%d" % k, lo, hi2 if t > k + 1 else hi), ("NL%d" % t, 160 * k + lo, 160 * k + (hi2 if t > k + 1 else hi)), t,
+               "%s%d%d" % (sm, k, t)) for t in range(k + 1, NT)]
         send(tr[:1])
         if tr[1:]:
             send(tr[1:])
 
     def w(t, j):
+        if j in (1, 2, 8, 3):
+            lo = 16 + 224 * t + (0, C, 112, 112 + C)[(1, 2, 8, 3).index(j)]
+            return ("U", lo, lo + C)
         return ("W%d" % t, C * j, C * j + C)
 
-    def places(t, lo, hi, end, j):
-        if hi - lo > 2 * C:
-            mm([(("LB", lo, hi), ("IDB", 0, 128), ("RW%d" % t, lo, hi), 1, True, True)])
-            tt(("WB", lo, hi), ("MP", lo, hi), ("LB", lo, hi), ALU.min)
-        else:
-            tt(("WB", lo, hi), ("MP", lo, hi), ("RW%d" % t, lo, hi), ALU.min)
-        mm([(("LB", lo, hi), ("ONEB", 0, 128), ("WB", lo, hi), 1, True, True)])
-        act(("HAS", lo, hi), ("LB", lo, hi), AF.Sign)
-        scan(("PP", lo, end), ("HAS", lo, end), ("HAS", lo, end), ALU.add, ALU.max, ("PP", lo - 1, lo) if lo else 0.0)
+    def turn(out, j, x, two, k0, k1):
+        for h in range(2):
+            m = 64 + 32 * two * (1 + h)
+            a, o = (x[0], x[1] - 16 * h, x[1] - 16 * h + m), ("OT", 224 * j + 96 * h, 224 * j + 96 * h + m)
+            add("V", lambda g, T, cx, a=a, o=o: [g.vector.transpose(ap(T, o), ap(T, a))], *rw([a], [o]), VA + m * CY)
+        regather(out, ("OT", 224 * j, 224 * j + 224), ("CL", 0, 3 + two), k0, k1)
+
+    held = {}
+
+    def sums(src, lo, hi, j, jk):
         for a in range(3):
-            act(("JK", NS * a + lo, NS * a + end), ("PP", lo, end), AF.Sign, bias=col(4 + a), scale=-1.0,
+            act(("JK", 416 * (jk + a), 416 * (jk + a) + hi - lo), (src, lo, hi), AF.Sign, bias=col(4 + a), scale=-1.0,
                 acc=("ACC", j + a, j + a + 1))
 
     def logic_a(t):
-        n = S0 + C * t
-        if t == 0 or SPLIT[t - 1]:
-            places(t, 0, n - C if t else n, n - C if t else n + C, 12 * t)
+        n = S0 + C * max(t - 1, 0)
+        L, pw, cs = n // 16, C * t + 16, ("IDS", 8 * t + 4, 8 * t + 7)
+        b = psum("L")
+        mm([((b, 0, n), ("IDB", 0, 128), ("RW%d" % t, 0, n), 1, True, True)])
+        tt(("WB", 0, n), ("MP", 0, n), (b, 0, n), ALU.min)
+        b = psum("L")
+        if t in P["LA"]:
+            mm([((b, 0, n), ("ONEB", 0, 128), ("WB", 0, n), 1, True, True)])
+            act(("HAS", 0, n), (b, 0, n), AF.Sign)
+            m = n if t else n + C
+            scan(("PO", 0, m), ("HAS", 0, m))
+            sums("PO", 0, m, 8 * t, 0)
+            held["n", t] = ("PO", n - 1, n)
+            if t and P["I3"]:
+                act(("ACC", 32, 35), ("ACC", 8 * t, 8 * t + 3), AF.Identity, bias=n / 2.0 + C, scale=0.5)
+            return
+        pick((b, 0, L), "SEL", "WB", 0, 16 * L)
+        act(("HW", 0, L), (b, 0, L), AF.Sign)
+        scan(("RR", 1, L + 1), ("HW", 0, L))
+        b = psum("L")
+        mm([((b, 32 - L, 32), ("ONEB", 0, 128), ("RR", 1, L + 1), 1, True, True),
+            ((b, 32, 32 + L), ("TL", 0, 128), ("RR", 1, L + 1), 1, True, False),
+            ((b, 32, 32 + L), ("TU", 0, 128), ("RR", 0, L), 1, False, True)])
+        sums(b, 32 - L, 32, 8 * t, 0)
+        act(("PW", pw - 1, pw + L), (b, 31, 32 + L), AF.Copy)
+        ts(cs, ("ACC", 8 * t, 8 * t + 3), 0.5, L / 2.0, ALU.mult, ALU.add)
+        gtt(("Z", 0, C), ("PW", pw, pw + 32), cs, ("IK", 0, C), ALU.is_le)
+        b = psum("H")
+        held[t], held["n", t] = b, ("PW", pw - 1, pw)
+        pick((b, 0, 3), "SEL", "Z", 0, C, stop=False)
+        mm([((b, 0, 3), ("I8", 0, 128), ("ACC", 8 * t, 8 * t + 3), 1, False, bool(P["I3"]))])
+        if P["I3"]:
+            act(("ACC", 32, 35), (b, 0, 3), AF.Identity, bias=n / 2.0 + C)
 
     def logic_m(t):
         n = S0 + C * t
-        ids, new, j = ("IDS", 4 * t, 4 * t + 3), (n, n + C), 12 * t
-        if t and not SPLIT[t - 1]:
-            places(t, 0, n, n + C, j)
-        elif t:
-            places(t, n - C, n, n + C, j + 4)
-            tt(("ACC", j + 8, j + 11), ("ACC", j, j + 3), ("ACC", j + 4, j + 7), ALU.add)
-            j += 8
-        ts(ids, ("ACC", j, j + 3), 0.5, (n + C) / 2.0, ALU.mult, ALU.add)
-        vgather(w(t, 0), ("MP", 0, NS), ids)
+        ids, new = ("IDS", 8 * t, 8 * t + 3), (n, n + C)
+        if t:
+            b = psum("L")
+            tt(("WB", n - C, n), ("MP", n - C, n), ("RW%d" % t, n - C, n), ALU.min)
+            mm([((b, 0, C), ("ONEB", 0, 128), ("WB", n - C, n), 1, True, True)])
+            act(("HAS", n - C, n), (b, 0, C), AF.Sign)
+            scan(("PP", 0, 96), ("HAS", n - C, n + C), held["n", t])
+            sums("PP", 0, 96, 8 * t + 4, 3)
+            if P["I3"]:
+                for a in range(3):
+                    ts(("IDS", 8 * t + a, 8 * t + a + 1), ("ACC", 8 * t + 4 + a, 8 * t + 5 + a), 0.5,
+                       ("ACC", 32 + a, 33 + a), ALU.mult, ALU.add)
+            elif t in P["LA"]:
+                tt(("ACC", 8 * t, 8 * t + 3), ("ACC", 8 * t, 8 * t + 3), ("ACC", 8 * t + 4, 8 * t + 7), ALU.add)
+                ts(ids, ("ACC", 8 * t, 8 * t + 3), 0.5, (n + C) / 2.0, ALU.mult, ALU.add)
+            else:
+                mm([((held[t], 0, 3), ("IH", 0, 128), ("ACC", 8 * t + 4, 8 * t + 7), 1, False, True)])
+                ts(ids, (held[t], 0, 3), (n + C) / 2.0, None, ALU.add)
+        else:
+            ts(ids, ("ACC", 0, 3), 0.5, (n + C) / 2.0, ALU.mult, ALU.add)
+        act(w(t, 0), ("MP", 0, NS), AF.Copy, off=ids)
         gtt(w(t, 1), ("RW%d" % t, 0, n + C), ids, w(t, 0), ALU.min)
-        mm([(("LB", 0, C), ("TRI", 0, 128), w(t, 1), 1, True, True)])
-        act(w(t, 2), ("LB", 0, C), AF.Relu)
-        mm([(("LB", 0, C), ("ONEF", 0, 128), w(t, 2), 1, True, True)])
+        b = psum("L")
+        mm([((b, 0, C), ("TRI", 0, 128), w(t, 1), 1, True, True)])
+        act(w(t, 2), (b, 0, C), AF.Relu)
         act(w(t, 3), ("LP", 0, NS), AF.Copy, off=ids)
-        gtt(w(t, 4), ("LP", 0, NS), ids, ("DIAG", 0, C), ALU.mult)
-        act(("LP",) + new, ("LB", 0, C), AF.Copy)
+        b, x, y = psum("L"), w(t, 1), w(t, 2)
         if t < NT - 1:
-            flip(("SN%d" % t, 0, C), w(t, 1))
-            flip(("SN%d" % t, C, 2 * C), ("LP",) + new)
-            share(t, 0, 2 * C, "nm")
-        tt(w(t, 6), w(t, 0), w(t, 1), ALU.subtract)
-        vscatter(("MP", 0, NS), ids, w(t, 6))
+            mm([((b, 0, 64), ("IDF", 0, 128), (x[0], x[1] - 16, x[2]), 1, True, True)])
+        if t < NT - 1 or t not in P["FP"]:
+            mm([((b, 64, 128), ("ONEF", 0, 128), (y[0], y[1], y[2] + 16), 1, True, True)])
+        if t < NT - 1:
+            turn(("SN%d" % t, 0, 64), 2 * t, (b, 16, 112), 1, -1.0, float(NV))
+            send([(("SN%d" % t, 0, 64), ("NL%d" % (t + 1), 160 * t, 160 * t + 64), t + 1, "nm%d%d" % (t, t + 1))])
+            if t + 2 < NT and not P["MG"]:
+                send([(("SN%d" % t, 0, 64), ("NL%d" % u, 160 * t, 160 * t + 64), u, "nm%d%d" % (t, u)) for u in range(t + 2, NT)])
+        if t in P["FP"]:
+            act(w(t, 6), ("LP", 0, NS), AF.Identity, bias=col(20), scale=col(21), off=ids)
+        if t < NT - 1 or t not in P["FP"]:
+            add("S", lambda g, T, cx: [g.scalar.activation(T.LP[:, n:n + C], ap(T, (b, 64, 112)), AF.Identity, bias=float(NV), scale=-1.0)],
+                [], [(b, 0, 512), ("LP",) + new], SA + C * CY)
+        vscatter(("MP", 0, NS), ids, w(t, 0), w(t, 1))
+        act(w(t, 7), ("MP", 0, NS), AF.Identity, bias=float(NV), scale=-1.0, off=ids)
         act(("MP",) + new, w(t, 1), AF.Copy)
-        act(w(t, 7), w(t, 6), AF.Identity, bias=float(NV), scale=-1.0)
 
     def logic_f(t):
-        ids, ols = ("IDS", 4 * t, 4 * t + 3), ("OLS", 4 * t, 4 * t + 3)
-        scan(w(t, 5), ("RST", 0, C), w(t, 4), ALU.mult, ALU.add)
-        flip(ols, w(t, 5), 16)
-        vscatter(("F", 0, FW), ols, w(t, 3), ("LP", S0 + C * t, S0 + C * t + C))
-        vgather(("ELS", 0, C), ("ER", 0, NS), ids)
-        act(w(t, 8), ("ER", 0, NS), AF.Copy, off=ids)
-        if t == NT - 1 and LAST:
-            act(("FX", 0, 384), ("F", 0, FW), AF.Copy, off=("ELS", 0, C // 2))
-            vgather(("FX", 384, 768), ("F", 0, FW), ("ELS", C // 2, C))
+        els, ols = ("SN%d" % t, 160, 208), ("SN%d" % t, 208, 211)
+        act(w(t, 8), ("ER", 0, NS), AF.Copy, off=("IDS", 8 * t, 8 * t + 3))
+        turn((els[0], 160, 224), 2 * t + 1, w(t, 8), 1, 1.0, 0.0)
+        if t not in P["FP"]:
+            vscatter(("F", 0, FW), ols, ("LP", S0 + C * t, S0 + C * t + C), w(t, 3))
+        if t in P["FP"]:
+            vscatter(("F", 0, FW), ols, w(t, 6), w(t, 2))
+            b = psum("L")
+            held["f", t] = (b, 0, C)
+            mm([((b, 0, C), ("IDF", 0, 128), w(t, 8), 1, True, False)])
+            for j, q in enumerate((0, 2, 1, 3)):
+                x, o = ("FX", 192 * q, 192 * q + 192), (els[0], els[1] + 12 * q, els[1] + 12 * q + 12)
+                if q < 2:
+                    act(x, ("F", 0, FW), AF.Copy, off=o)
+                else:
+                    add("V", lambda g, T, cx, x=x, o=o: [g.vector.tensor_copy(ap(T, x), ind(T, ("F", 0, FW), o))],
+                        [("F", 0, FW), o], [x], VG + 192 * GA)
+                mm([((b, 0, C), ("SELF", 16 - i, 144 - i), ("FX", C * i, C * i + C), 1, False, False) for i in range(4 * q, 4 * q + 4)])
         else:
-            act(("FX", 0, 768), ("F", 0, FW), AF.Copy, off=("ELS", 0, C))
-        pick(("LB", 0, C), "SELF", "FX", 0, 768)
-        tt(w(t, 8), ("LB", 0, C), w(t, 8), ALU.add)
+            act(("FX", 0, 768), ("F", 0, FW), AF.Copy, off=els)
+            dma("Y", lambda T: (ap(T, w(t, 10)), T.FX[0:128:16, :]), [("FX", 0, 768)], [w(t, 10)], "fd%d" % t, 60)
+            tt(w(t, 5), w(t, 10), w(t, 8), ALU.add)
+            held["f", t] = w(t, 5)
         if t < NT - 1:
             vscatter(("F", 0, FW), ols, ("ZER", 0, C))
 
     def logic_e(t):
         n = S0 + C * t
-        ids = ("IDS", 4 * t, 4 * t + 3)
+        ids = ("IDS", 8 * t, 8 * t + 3)
+        act(w(t, 4), w(t, 8), AF.Relu, bias=-BIG * (NV - 1), scale=BIG)
         for j in range(t + 1):
-            gtt(w(t, 8), ("RD%d" % j, 0, NS), ids, w(t, 8), ALU.max)
-        ts(w(t, 9), w(t, 8), float(NV), BIG, ALU.is_lt, ALU.mult)
+            gtt(w(t, 4), ("RD%d" % j, 0, NS), ids, w(t, 4), ALU.max)
+        if t in P["FP"]:
+            mm([(held["f", t], ("IDF", 0, 128), w(t, 4), 1, False, True)])
+        else:
+            tt(w(t, 5), w(t, 5), w(t, 4), ALU.max)
+        ts(w(t, 9), w(t, 4), 0.0, BIG, ALU.is_le, ALU.mult)
         tt(w(t, 9), w(t, 9), w(t, 7), ALU.add)
         if t < NT - 1:
-            tt(("ER", n, n + C), w(t, 8), w(t, 9), ALU.min)
-            vcopy(("SN%d" % t, 2 * C, 3 * C), ("ER", n, n + C))
-            share(t, 2 * C, 3 * C, "ne")
+            tt(("ER", n, n + C), held["f", t], w(t, 9), ALU.min)
+            turn(("SN%d" % t, 64, 112), 2 * t, ("ER", n, n + C), 0, 1.0, 0.0)
+            send([(("SN%d" % t, 64, 112), ("NL%d" % (t + 1), 160 * t + 64, 160 * t + 112), t + 1, "ne%d%d" % (t, t + 1))])
+            if t + 2 < NT:
+                lo = 0 if P["MG"] else 64
+                send([(("SN%d" % t, lo, 112), ("NL%d" % u, 160 * t + lo, 160 * t + 112), u, "ne%d%d" % (t, u)) for u in range(t + 2, NT)])
         else:
-            tt(("YI", n, NS), w(t, 8), w(t, 9), ALU.min)
-            add("Y", lambda g, T, cx: [g.sync.dma_start(T.yi[:, n:NS], T.YI[:, n:NS])], [("YI", n, NS)], [], "stored")
+            tt(("YI", n, NS), held["f", t], w(t, 9), ALU.min)
+            dma("Y", lambda T: (T.yi[:, n:NS], T.YI[:, n:NS]), [("YI", n, NS)], [], "stored", 30)
 
     def out_m():
         act(("YM", 0, NS), ("MP", 0, NS), AF.Identity, bias=float(NV), scale=-1.0)
-        add("Y", lambda g, T, cx: [g.sync.dma_start(T.ym[:], T.YM[:])], [("YM", 0, NS)], [], "stored")
+        dma("Y", lambda T: (T.ym[:], T.YM[:]), [("YM", 0, NS)], [], "stored", 260)
 
     def out_e():
-        n = NS - C
-        mm([(("CM", 0, n), ("IDF", 0, 128), ("ER", 0, n), 1, True, False)])
+        n, b = NS - C, psum("M")
+        last[b] = [e for e in last["OUT3"] if e[1] <= S0]
+        if P["OE"]:
+            mm([((b, 0, n), ("IDF", 0, 128), ("ER", 0, n), 1, True, False)])
         for j in range(NT):
-            mm([(("CM", 0, n), ("IDB", 0, 128), ("RD%d" % j, 0, n), 1, False, j == NT - 1)])
-        ts(("YI", 0, n), ("CM", 0, n), float(NV), None, ALU.min)
-        add("Y", lambda g, T, cx: [g.sync.dma_start(T.yi[:, 0:n], T.YI[:, 0:n])], [("YI", 0, n)], [], "stored")
+            mm([((b, 0, n), ("IDB", 0, 128), ("RD%d" % j, 0, n), 1, j == 0 and not P["OE"], j == NT - 1)])
+        if P["OE"]:
+            ts(("YI", 0, n), (b, 0, n), float(NV), None, ALU.min)
+        else:
+            tt(("YI", 0, n), (b, 0, n), ("ER", 0, n), ALU.max)
+            ts(("YI", 0, n), ("YI", 0, n), float(NV), None, ALU.min)
+        dma("Y", lambda T: (T.yi[:, 0:n], T.YI[:, 0:n]), [("YI", 0, n)], [], "stored", 240)
 
-    for b in BLOCKS.split():
-        {"bm": bulk_m, "be": bulk_e, "fm": lambda k, t: fresh(k, t, 0), "fe": lambda k, t: fresh(k, t, 1), "la": logic_a,
-         "lm": logic_m, "lf": logic_f, "le": logic_e, "om": out_m, "oe": out_e}[b[:2]](*[int(x) for x in b[2:]])
-    return ops
+    for b in P["BLOCKS"].split():
+        {"bm": bulk_m, "be": bulk_e, "fm": fresh_m, "fe": fresh_e, "la": logic_a, "lm": logic_m, "lf": logic_f,
+         "le": logic_e, "om": out_m, "oe": out_e, "sw": back_m, "sd": back_e}[b[:2]](*[int(x) for x in b[2:]])
+    return ops, bank, nload
 
 
-def plan():
-    ops, by_sem = build(), {}
+def plan(P=TUNE):
+    ops, bank, nload = build(P)
+    n, by_sem, users, WAKE = len(ops), {}, {}, P["WAKE"]
     for i, o in enumerate(ops):
         if o["sem"]:
             by_sem.setdefault(o["sem"], []).append(i)
+        for b in o["banks"]:
+            users.setdefault(b, []).append(i)
     for o in ops:
         for d in list(o["deps"]):
             if ops[d]["sem"]:
                 o["deps"].update(by_sem[ops[d]["sem"]])
-    order = [int(ORDER[j:j + 2], 32) for j in range(0, len(ORDER), 2)]
-    assert sorted(order) == list(range(len(ops)))
-    seen = set()
-    for i in order:
-        assert ops[i]["deps"] <= seen
-        seen.add(i)
-    return ops, order, by_sem
+    way = [0.0] * n
+    for i in range(n - 1, -1, -1):
+        o = ops[i]
+        way[i] += o["dur"] + o["lat"] + WAKE + (1e3 - i if i < nload else 0) + (0 if o["after"] else P["PAD"])
+        for d in o["deps"]:
+            way[d] = max(way[d], way[i])
+        if o["after"] is not None:
+            way[o["after"]] = max(way[o["after"]], way[i] - WAKE)
+
+
+    def place(seq, before, back):
+        busy, start, end = {e: [] for e in "VSPGY"}, {}, {}
+        for i in seq:
+            o = ops[i]
+            t = max([0.0] + [end[d] for d in before[i]]) + (o["lat"] + WAKE if back else 0.0)
+            q, k = busy[o["eng"]], 0
+            while k < len(q) and q[k][0] < t + o["dur"]:
+                t = max(t, q[k][1])
+                k += 1
+            q.insert(k, (t, t + o["dur"]))
+            start[i], end[i] = t, t + o["dur"] + (0.0 if back else o["lat"] + WAKE)
+        return start, end
+
+    def passes(deps, key, rounds):
+        succ, best = [set() for o in ops], None
+        for i in range(n):
+            for d in deps[i]:
+                succ[d].add(i)
+        for r in range(rounds):
+            seq, left, heap = [], [len(d) for d in deps], sorted((key[i], i) for i in range(n) if not deps[i])
+            while heap:
+                i = heap.pop(0)[1]
+                seq.append(i)
+                for x in succ[i]:
+                    left[x] -= 1
+                    if not left[x]:
+                        heap.append((key[x], x))
+                heap.sort()
+            start, end = place(seq, deps, False)
+            if best is None or max(end.values()) < best[0]:
+                best = (max(end.values()), start, end)
+            back = place(sorted(range(n), key=lambda i: (-end[i], -start[i])), succ, True)[1]
+            key = [-1e3 + i if i < nload else -back[i] for i in range(n)]
+        return best + (key,)
+
+    span, start, end, key = passes([o["deps"] for o in ops], [-x for x in way], P["R0"])
+    best = None
+    for r in range(P["R1"]):
+        deps, holder, got = [set(o["deps"]) for o in ops], {}, {}
+        for b in sorted(users, key=lambda b: max(start[u] for u in users[b] if ops[u]["eng"] == "P")):
+            x = got[b] = min(POOL[b[0]], key=lambda x: max([0.0] + [end[u] for u in users.get(holder.get(x), [])]))
+            for u in users[b]:
+                deps[u].update(users.get(holder.get(x), []))
+            holder[x] = b
+        shake = [((i + 1) * (r + P["SEED"]) * 7919 % 1009) / 1009.0 * P["SHAKE"] * (r % 3) for i in range(n)]
+        span, start, end, key = passes(deps, [start[i] + shake[i] for i in range(n)], P["R2"])
+        if best is None or span < best[0]:
+            best = (span, start, deps, got, end)
+        start, end = best[1], best[4]
+    bank.update(best[3])
+    for o, d in zip(ops, best[2]):
+        o["deps"] = d
+    order = sorted(range(n), key=lambda i: (i >= nload, best[1][i] if i >= nload else i))
+    return ops, tighten(P, ops, order, nload), by_sem
+
+
+def tighten(P, ops, order, nload):
+    n, deps, eng = len(ops), [sorted(o["deps"]) for o in ops], ["VSPGY".index(o["eng"]) for o in ops]
+    cases = []
+    for c in P["CASES"]:
+        other = build(dict(P, **c))[0]
+        cases.append(([o["dur"] for o in other], [o["lat"] + c.get("WAKE", P["WAKE"]) for o in other]))
+
+    def run(seq, p0=0, old=None):
+        total, pairs, out, head = 0.0, [], [], [-1] * 5
+        for i in seq[:p0]:
+            head[eng[i]] = i
+        for c, (dur, lat) in enumerate(cases):
+            end, why = (old[c][0][:], old[c][1][:]) if old else ([0.0] * n, [-1] * n)
+            free, prev = [end[i] - lat[i] if i >= 0 else 0.0 for i in head], head[:]
+            out.append((end, why))
+            for i in seq[p0:]:
+                e = eng[i]
+                t, y = free[e], prev[e]
+                for d in deps[i]:
+                    if end[d] > t:
+                        t, y = end[d], d
+                why[i], prev[e] = y, i
+                free[e] = t = t + dur[i]
+                end[i] = t + lat[i]
+            i = end.index(max(end))
+            total += end[i]
+            while why[i] >= 0:
+                if eng[why[i]] == eng[i] and why[i] not in ops[i]["deps"]:
+                    pairs.append((why[i], i))
+                i = why[i]
+        return total / len(cases), pairs, out
+
+    seed, (now, pairs, times) = 12345, run(order)
+    best = (now, order)
+    for step in range(P["STEPS"]):
+        seed = (seed * 1103515245 + 12345) % 2147483648
+        a, b = pairs[(seed >> 8) % len(pairs)]
+        pa, pb = order.index(a), order.index(b)
+        if pa < nload:
+            continue
+        if seed >> 7 & 1:
+            pa = max(nload, pa - (seed >> 20) % 3 * ((seed >> 24) % 12))
+            part, move = order[pa:pb + 1], {b}
+            for x in reversed(part):
+                if x in move:
+                    move.update(deps[x])
+            new = [x for x in part if x in move] + [x for x in part if x not in move]
+        else:
+            pb = min(n - 1, pb + (seed >> 20) % 3 * ((seed >> 24) % 12))
+            part, move = order[pa:pb + 1], {a}
+            for x in part:
+                if not move.isdisjoint(deps[x]):
+                    move.add(x)
+            new = [x for x in part if x not in move] + [x for x in part if x in move]
+        cand = order[:pa] + new + order[pb + 1:]
+        t, pr, tm = run(cand, pa, times)
+        if t <= now + P["SLACK"] * (1.0 - step / P["STEPS"]) * ((seed >> 12) % 16) / 16.0:
+            now, pairs, order, times = t, pr, cand, tm
+            if t < best[0]:
+                best = (t, cand)
+    ops[0]["span"] = best[0]
+    return best[1]
 
 
 def engine_sets(topo, cores, r, tr):
     can = [topo.engines(cores[r], cores[(r + x[2]) % len(cores)]) for x in tr]
     if len(tr) == 1:
-        return can
+        few = min(len(topo.engines(cores[r], c)) for c in cores if c != cores[r])
+        return [can[0][:few]] if tr[0][3] == "lst0" else can
     a, b = can
     if len(a) > len(b):
         return [[e for e in a if e not in b][:len(b)], b]
@@ -453,16 +766,21 @@ def engine_sets(topo, cores, r, tr):
     return [a[:len(a) // 2], b[len(b) // 2:]]
 
 
+PLAN = []
+
+
 def rank_program(g, core, T, topo):
     r = T.rank_of(core)
     if r is None:
         return
-    ops, order, by_sem = plan()
+    if not PLAN:
+        PLAN.append(plan())
+    ops, order, by_sem = PLAN[0]
     cores = list(T.cores)
     N = len(cores)
     queue = {"V": g.vector, "S": g.scalar, "P": g.tensor, "G": g, "Y": g.sync}
     count = {e: 0 for e in "VSPG"}
-    mark, waited, cx, sent = {}, {}, {}, 0
+    mark, waited, knew, cx, sent = {}, {}, {}, {}, 0
 
     def wait(e, sem, val):
         if waited.get((e, sem), 0) < val:
@@ -486,8 +804,15 @@ def rank_program(g, core, T, topo):
             elif not (e == "P" and p["eng"] == "P"):
                 s = "e" + p["eng"]
                 need[s] = max(need.get(s, 0), mark[d])
+        for s in need:
+            for s2 in need:
+                if s != s2 and need[s2] <= knew.get((s, need[s]), {}).get(s2, 0):
+                    need[s2] = 0
         for s in sorted(need):
             wait(e, s, need[s])
+            for s2, v in knew.get((s, need[s]), {}).items():
+                waited[(e, s2)] = max(waited.get((e, s2), 0), v)
+        seen = {s: v for (q, s), v in waited.items() if q == e}
         if o["sends"]:
             trs = []
             for x, en in zip(o["sends"], engine_sets(topo, cores, r, o["sends"])):
@@ -510,6 +835,7 @@ def rank_program(g, core, T, topo):
                 ins.then_inc(T.sem["e" + e], 1)
                 count[e] += 1
             mark[i] = count[e]
+            knew[("e" + e, count[e])] = seen
     for e in "VSPG":
         wait("G", "e" + e, count[e])
     wait("G", "sent", sent)

from concourse.bass import DstId, RemoteDMATransfer
from concourse.mybir import AluOpType as ALU, ActivationFunctionType as AF

NV, S0, C, NT, NS = 4096, 320, 48, 4, 512
TA, TB = (14, 12, 13, 12), (8, 11, 10, 9)
BIG = 8192.0
PAIRS = [(0, 1), (0, 2), (1, 2), (0, 3), (1, 3), (2, 3)]
TUNE = dict(
    FS=(12, 14, 12, 8),
    FB="VSSSVV",
    RV=2, LONE=2,
    PAD=0.15,
    R0=6, R1=10, R2=4, SHAKE=2, PIECE=512, FP=(3,), LD=1.3, LR=1.2, WAKE=0.22, GA=1.3e-3, PE=0.42e-3, GI=0.3, VA=0.03, VG=0.05, SA=0.045,
    FPE=(16, 16, 16, 16), RA=4, RG=2, GD=1.0, LA=(0,), OE=True, GS=1, SEED=7,
    STEPS=45000, SLACK=0.07,
    CASES=[dict(FIRST=2.5), dict(GA=0.95e-3, WAKE=0.27, FIRST=4.0, LD=1.6), dict(GA=1.55e-3, WAKE=0.17, LD=1.0, LR=1.0, FIRST=2.5),
           dict(GA=1.1e-3, WAKE=0.15, LD=1.5, LR=2.0, GI=0.5, FIRST=5.5)],
    SD=(3,), MG=0, FIRST=7.0, I3=1, MS=(0, 0, 0, 0),
    BLOCKS="bm0 la0 lm0 lf0 bm1 sw1 be0 fm01 fm02 fm03 la1 lm1 le0 lf1 bm2 sw2 be1 sd1 fe01 fe02 fe03 fm12 fm13 le1 la2 lm2 lf2 "
           "bm3 sw3 be2 sd2 fe12 fe13 fm23 le2 be3 sd3 fe23 la3 lm3 lf3 om oe le3")
XW, FW = 4112, 4160
POOL = {"D": ["D0", "D1"], "L": ["L0", "NB"], "H": ["L1"], "M": ["CM"], "E": ["CE"], "N": ["L0", "NB"], "T": ["TP"]}

f32, bf, f16, i32, u16 = "float32", "bfloat16", "float16", "int32", "uint16"
SCRATCH = {
    "OTf": ("sbuf", [128, 640], f32), "MH": ("sbuf", [128, S0], f16), "EH": ("sbuf", [128, S0], f16), "FH": ("sbuf", [128, S0], f16),
    "QH": ("sbuf", [128, 288], f16), "SELH": ("sbuf", [128, 144], f16), "AB": ("sbuf", [128, 3 * C], bf),
    "L1": ("psum", [128, 16, 32], f32),
    "MI": ("sbuf", [128, S0], i32), "EI": ("sbuf", [128, S0], i32), "X": ("sbuf", [128, XW], bf),
    "NC": ("sbuf", [128, 12 * 768], bf), "XF": ("sbuf", [128, 6 * 192], bf),
    "F": ("sbuf", [128, FW], f32), "FX": ("sbuf", [128, 768], f32), "OT": ("sbuf", [128, 20 * 128], f32),
    "MP": ("sbuf", [128, NS], f32), "ER": ("sbuf", [128, NS], f32), "LP": ("sbuf", [128, NS], f32),
    "FM": ("sbuf", [128, S0], f32),
    "WB": ("sbuf", [128, NS], bf), "HAS": ("sbuf", [128, NS], bf), "PP": ("sbuf", [128, 368], bf),
    "HW": ("sbuf", [128, 32], bf), "RR": ("sbuf", [128, 32], bf), "PW": ("sbuf", [128, 4 * C], bf), "Z": ("sbuf", [128, C], bf),
    "JK": ("sbuf", [128, 6 * 416], bf), "ACC": ("sbuf", [128, 48], f32),
    "IDS": ("sbuf", [128, 32], u16),
    "YM": ("sbuf", [128, NS], f32), "YI": ("sbuf", [128, NS], f32),
    "PI": ("sbuf", [128, 8], i32), "COL": ("sbuf", [128, 32], f32),
    "IA": ("sbuf", [128, 128], f32), "ID": ("sbuf", [128, 128], f32), "IX": ("sbuf", [128, 288], f32),
    "IK": ("sbuf", [128, C], f32), "U": ("sbuf", [128, 1040], f32), "PO": ("sbuf", [128, 416], bf),
    "CJ": ("sbuf", [128, 96], f32), "CI": ("sbuf", [128, 64], i32), "CL": ("sbuf", [128, 8], u16), "CG": ("sbuf", [128, 48], u16), "ZER": ("sbuf", [128, C], f32),
    "ONEF": ("sbuf", [128, 128], f32), "ONEB": ("sbuf", [128, 128], bf), "TRI": ("sbuf", [128, 128], f32),
    "IDF": ("sbuf", [128, 128], f32), "IDB": ("sbuf", [128, 128], bf), "NEG": ("sbuf", [128, 128], bf),
    "I8": ("sbuf", [128, 128], f32), "IH": ("sbuf", [128, 128], f32), "TL": ("sbuf", [128, 128], bf), "TU": ("sbuf", [128, 128], bf),
    "SEL": ("sbuf", [128, 144], bf), "SELF": ("sbuf", [128, 144], f32),
    "TP": ("psum", [128, 16, 32], f32),
}
for _b in ("D0", "D1", "L0", "CM", "CE", "NB"):
    SCRATCH[_b] = ("psum", [128, 512], f32)
for _t in range(NT):
    SCRATCH["LST%d" % _t] = ("sbuf", [128, 656], u16)
    SCRATCH["XL%d" % _t] = ("sbuf", [128, 4 * S0], bf)
    SCRATCH["CMP%d" % _t] = ("sbuf", [128, 32 * S0], bf)
    SCRATCH["RW%d" % _t] = ("sbuf", [128, NS], bf)
    SCRATCH["RD%d" % _t] = ("sbuf", [128, NS], bf)
    SCRATCH["W%d" % _t] = ("sbuf", [128, 11 * C], f32)
    SCRATCH["SN%d" % _t] = ("sbuf", [128, 224], u16)
    if _t:
        SCRATCH["OUT%d" % _t] = ("sbuf", [128, 2 * NS], bf)
        SCRATCH["NL%d" % _t] = ("sbuf", [128, 160 * _t], u16)

SEMAPHORES = (["eV", "eS", "eP", "eG", "sent", "lst0", "ldM", "ldE", "ldX", "stored"]
              + [n + str(t) for n in ("rep", "fd") for t in range(NT)]
              + [n + str(t) for n in ("lst", "rw", "rd") for t in (1, 2, 3)]
              + ["adde%d_%d" % (t, i) for t in range(NT) for i in range(TUNE["FPE"][t], TUNE["FS"][t], TUNE["RA"])]
              + ["addm%d_%d" % (t, i) for t in range(NT) for i in range(16 - TUNE["MS"][t], 16, TUNE["RA"])]
              + ["%s%d%d" % (n, k, t) for n in ("nm", "ne", "nw", "nd") for k, t in PAIRS])
CY, PE, GA, SC, WAKE = 0.83e-3, 0.42e-3, 1.3e-3, 3.2e-3, 0.06


def build(P):
    ops, last, tail, bank, nbank = [], {}, {}, {}, [0]
    FS, RV, GA, PE, VA, VG, SA = P["FS"], P["RV"], P["GA"], P["PE"], P["VA"], P["VG"], P["SA"]

    def add(eng, fn, rd, wr, dur, lat=0.0, sem=None, sends=None, chain=None):
        me, deps = len(ops), set()
        for (b, lo, hi) in rd:
            deps.update(o for (l2, h2, o, w) in last.get(b, []) if w and l2 < hi and lo < h2)
        for (b, lo, hi) in wr:
            deps.update(o for (l2, h2, o, w) in last.get(b, []) if l2 < hi and lo < h2)
        for (b, lo, hi) in wr:
            last[b] = [e for e in last.get(b, []) if not (lo <= e[0] and e[1] <= hi)] + [(lo, hi, me, True)]
        for (b, lo, hi) in rd:
            last.setdefault(b, []).append((lo, hi, me, False))
        ops.append(dict(eng=eng, fn=fn, deps=deps, sem=sem, sends=sends, rd=rd, wr=wr, dur=dur, lat=lat,
                        after=tail.get(chain), banks={r[0] for r in rd + wr if "#" in r[0]}))
        if chain:
            tail[chain] = me

    def psum(pool):
        nbank[0] += 1
        return "%s#%d" % (pool, nbank[0])

    def ap(T, r, step=1):
        if r[0][:2] == "H#":
            return T.L1[:, 0, r[1]:r[2]]
        return T[bank.get(r[0], r[0])][:, r[1]:r[2]:step] if step > 1 else T[bank.get(r[0], r[0])][:, r[1]:r[2]]

    def ind(T, w, o):
        return ap(T, w).indirect(ap(T, o))

    def rw(rd, wr):
        return [[(r[0], 0, 512) if "#" in r[0] else r for r in x] for x in (rd, wr)]

    def col(j):
        return ("COL", j, j + 1)

    def sv(T, s):
        return ap(T, s) if isinstance(s, tuple) else s

    def wid(r):
        return r[2] - r[1]

    def ts(out, in0, s1, s2, op0, op1=None):
        def fn(g, T, cx):
            if op1 is None:
                return [g.vector.tensor_scalar(ap(T, out), ap(T, in0), sv(T, s1), None, op0)]
            return [g.vector.tensor_scalar(ap(T, out), ap(T, in0), sv(T, s1), sv(T, s2), op0, op1)]
        add("V", fn, *rw([in0] + [s for s in (s1, s2) if isinstance(s, tuple)], [out]), VA + wid(out) * CY)

    def flip(out, in0, k=1.0):
        ts(out, in0, -k, float(NV), ALU.mult, ALU.add)

    def tt(out, in0, in1, op):
        add("V", lambda g, T, cx: [g.vector.tensor_tensor(ap(T, out), ap(T, in0), ap(T, in1), op)], *rw([in0, in1], [out]),
            VA + wid(out) * (1 if "#" in in0[0] + in1[0] else 2) * CY)

    def gtt(out, win, off, in1, op, chain=None):
        add("V", lambda g, T, cx: [g.vector.tensor_tensor(ap(T, out), ind(T, win, off), ap(T, in1), op)],
            [win, off, in1], [out], VG + wid(out) * GA, chain=chain)

    def vcopy(out, in0, k=1.0):
        add("V", lambda g, T, cx: [g.vector.tensor_copy(ap(T, out), ap(T, in0))], [in0], [out], VA + wid(out) * k * CY)

    def regather(out, win, off, k0, k1):
        add("V", lambda g, T, cx: [g.vector.tensor_scalar(ap(T, out), ind(T, win, off), k0, k1, ALU.mult, ALU.add)],
            [win, off], [out], VG + wid(out) * GA)

    def vscatter(win, off, in0, in1=None):
        def fn(g, T, cx):
            if in1 is None:
                return [g.vector.tensor_copy(ind(T, win, off), ap(T, in0))]
            return [g.vector.tensor_tensor(ind(T, win, off), ap(T, in0), ap(T, in1), ALU.subtract)]
        add("V", fn, [off, in0] + ([in1] if in1 else []), [win], VG + wid(in0) * SC)

    def scan(out, d0, init=0.0):
        add("V", lambda g, T, cx: [g.vector.tensor_tensor_scan(ap(T, out), ap(T, d0), ap(T, d0), sv(T, init), ALU.add, ALU.max)],
            [d0] + ([init] if init else []), [out], VA + wid(out) / 2 * CY)

    def act(out, in0, func, bias=None, scale=None, acc=None, off=None, chain=None):
        def fn(g, T, cx):
            kw = {}
            if bias is not None:
                kw["bias"] = sv(T, bias)
            if scale is not None:
                kw["scale"] = sv(T, scale)
            if acc is not None:
                kw["accum_out"] = ap(T, acc)
            return [g.scalar.activation(ap(T, out), ap(T, in0) if off is None else ind(T, in0, off), func, **kw)]
        add("S", fn, *rw([in0] + [s for s in (bias, scale, off) if isinstance(s, tuple)], [out] if acc is None else [out, acc]),
            SA + wid(out) * (GA if off else CY), chain=chain)

    def mm(items):
        def fn(g, T, cx):
            return [g.tensor.matmul(T.TP[:, 0:3, o[1]:o[2]] if o[0][0] == "T" else ap(T, o), ap(T, l), ap(T, x, st), a, z)
                    for (o, l, x, st, a, z) in items]
        add("P", fn, *rw([i[1] for i in items] + [i[2] for i in items], [i[0] for i in items]),
            sum(max(64, wid(i[2]) // i[3]) * PE * (4 if SCRATCH[i[1][0]][2] == f32 else 1) for i in items))

    def pick(out, sel, buf, lo, hi, stop=True):
        mm([(out, (sel, 16 - i, 144 - i), (buf, lo + i, hi), 16, i == 0, stop and i == 15) for i in range(16)])

    def count_row(b, i, rhs, after=()):
        def fn(g, T, cx):
            k = cx.get(b, 0)
            cx[b] = k + 1
            return [g.tensor.matmul(ap(T, (b, 0, wid(rhs))), T.SEL[:, 16 - i:144 - i], ap(T, rhs), k == 0, k == (14 if b[0] == "M" else 15))]
        add("P", fn, [rhs, ("SEL", 0, 144), *after], [(b, i, i + 1)], max(64, wid(rhs)) * PE)

    def iota(out, pat, base, cm, flt=True):
        def fn(g, T, cx):
            if flt:
                return [g.iota(ap(T, out), pat, base, cm, allow_small_or_imprecise_dtypes=True)]
            return [g.iota(ap(T, out), pat, base, cm)]
        add("G", fn, [], [out], 0.13 + 2 * wid(out) * CY)

    def fill(out, v):
        iota(out, [[0, wid(out)]], v, 0)

    def dma(q, fn, rd, wr, sem, kb):
        add(q, lambda g, T, cx: [(g.sync if q == "Y" else g.scalar).dma_start(*fn(T))], rd, wr, 0.25, P["LD"] + kb / 300.0, sem)

    def send(tr, first=0.0):
        add("G", None, [x[0] for x in tr], [x[1] for x in tr], P["GI"] + first, P["LR"] + wid(tr[0][0]) * len(tr) / 500.0, sends=tr)

    dma("Y", lambda T: (T.MI[0:64, :], T.mem0[0:64, :]), [], [("MI", 0, 1)], "ldM", 160)
    dma("S", lambda T: (T.MI[64:128, :], T.mem0[64:128, :]), [], [("MI", 1, S0)], "ldM", 160)
    dma("S", lambda T: (T.EI[:], T.inv0[:]), [], [("EI", 0, S0)], "ldE", 320)
    dma("Y", lambda T: (T.X[:, 0:2048], T.xs[:, 0:2048]), [], [("X", 0, 2048)], "ldX", 1100)
    dma("S", lambda T: (T.X[:, 2048:NV], T.xs[:, 2048:NV]), [], [("X", 2048, NV)], "ldX", 1100)
    nload = len(ops)

    iota(("PI", 0, 1), [[0, 1]], 0, 1, flt=False)
    iota(("IA", 0, 128), [[1, 8], [0, 16]], 0, 0)
    iota(("ID", 0, 128), [[1, 128]], 0, -1)
    iota(("IK", 0, C), [[1, C]], 0, 0)
    iota(("IX", 0, 144), [[1, 144]], -16, 0)
    iota(("IX", 144, 288), [[1, 144]], 128, 0)
    iota(("LP", S0, NS), [[0, 4], [1, C]], NV + 1, 0)
    fill(("ACC", 44, 47), 0)
    fill(("ACC", 47, 48), 1)
    for j in range(13):
        fill(("F", j * FW // 13, (j + 1) * FW // 13), 0)
    ts(("PI", 2, 3), ("PI", 0, 1), 4, None, ALU.arith_shift_right)
    ts(("PI", 3, 4), ("PI", 0, 1), 15, None, ALU.bitwise_and)
    ts(("PI", 4, 5), ("PI", 0, 1), 4, 1, ALU.arith_shift_right, ALU.bitwise_and)
    vcopy(("COL", 0, 3), ("PI", 2, 5))
    ts(("ONEF", 0, 128), ("IA", 0, 128), col(0), None, ALU.is_equal)
    ts(("TRI", 0, 128), ("ID", 0, 128), 0.0, -BIG, ALU.is_gt, ALU.mult)
    tt(("TRI", 0, 128), ("TRI", 0, 128), ("ONEF", 0, 128), ALU.mult)
    ts(("IDF", 0, 128), ("ID", 0, 128), 0.0, None, ALU.is_equal)
    tt(("TRI", 0, 128), ("TRI", 0, 128), ("IDF", 0, 128), ALU.add)
    ts(col(3), col(0), 16.0, None, ALU.mult)
    ts(("SEL", 0, 144), ("IX", 0, 144), col(3), None, ALU.is_equal)
    ts(col(7), col(2), 128.0, col(3), ALU.mult, ALU.add)
    ts(("SELH", 0, 144), ("IX", 0, 144), col(3), None, ALU.is_equal)
    ts(("QH", 0, 288), ("IX", 0, 288), col(7), col(1), ALU.subtract, ALU.is_equal)
    ts(col(21), col(1), 0.0, -1.0, ALU.is_equal, ALU.mult)
    act(col(20), col(21), AF.Copy, scale=-float(NV))
    ts(col(22), col(1), 1.0, BIG, ALU.is_ge, ALU.mult)
    ts(col(23), col(1), 2.0, BIG, ALU.is_ge, ALU.mult)
    for t in range(NT):
        act(col(24 + t), col(22), AF.Copy, scale=float(TB[t]))
        if t:
            act(col(27 + t), col(23), AF.Copy, scale=float(TB[t]))
    act(("CJ", 0, 40), ("IK", 0, 40), AF.Identity, bias=col(1), scale=16.0)
    act(("CJ", 40, 80), ("CJ", 0, 40), AF.Identity, bias=10.5 / 20, scale=1.0 / 20)
    vcopy(("CI", 0, 40), ("CJ", 40, 80))
    ts(("CJ", 40, 80), ("CI", 0, 40), -639.0 / 32, 20.0, ALU.mult, ALU.add)
    tt(("CJ", 40, 80), ("CJ", 40, 80), ("CJ", 0, 40), ALU.add)
    ts(("CG", 0, 20), ("CJ", 40, 60), 32.0, None, ALU.mult)
    ts(("CG", 20, 40), ("CJ", 59, 79), 32.0, None, ALU.mult)
    act(("CJ", 80, 84), ("CJ", 0, 4), AF.Identity, bias=-1.0 / 3, scale=1.0 / 3)
    vcopy(("CI", 40, 44), ("CJ", 80, 84))
    ts(("CJ", 84, 88), ("CI", 40, 44), -3.0, col(2), ALU.mult, ALU.add)
    tt(("CJ", 84, 88), ("CJ", 84, 88), ("CJ", 0, 4), ALU.add)
    tt(("CI", 44, 48), ("CJ", 84, 88), ("ACC", 44, 48), ALU.add)
    ts(("CI", 48, 52), ("CI", 44, 48), 1, None, ALU.bitwise_and)
    ts(("CJ", 88, 92), ("CI", 48, 52), 7.0, None, ALU.mult)
    tt(("CJ", 88, 92), ("CJ", 88, 92), ("CJ", 0, 4), ALU.add)
    ts(("CJ", 92, 96), ("CI", 40, 44), -47.0 / 16, None, ALU.mult)
    tt(("CJ", 88, 92), ("CJ", 88, 92), ("CJ", 92, 96), ALU.add)
    ts(("CL", 0, 3), ("CJ", 88, 91), 16.0, None, ALU.mult)
    ts(("CL", 3, 4), ("CJ", 91, 92), 16.0, 32.0, ALU.mult, ALU.add)
    act(("SELF", 0, 144), ("SEL", 0, 144), AF.Copy)
    act(("ONEB", 0, 128), ("ONEF", 0, 128), AF.Copy)
    act(("IDB", 0, 128), ("IDF", 0, 128), AF.Copy)
    act(("NEG", 0, 128), ("IDF", 0, 128), AF.Copy, scale=-1.0)
    if len(P["LA"]) < NT:
        act(("I8", 0, 128), ("IDF", 0, 128), AF.Copy, scale=8.0)
        act(("IH", 0, 128), ("IDF", 0, 128), AF.Copy, scale=0.5)
        act(("TU", 0, 128), ("TRI", 0, 128), AF.Abs)
        act(("TL", 0, 128), ("TU", 0, 128), AF.Sign)
        tt(("TU", 0, 128), ("ONEB", 0, 128), ("TL", 0, 128), ALU.subtract)
    ts(("COL", 4, 7), ("IK", 0, 3), 16.0, 0.5, ALU.mult, ALU.add)
    ts(("COL", 4, 7), ("COL", 4, 7), col(1), None, ALU.add)
    scol = {}
    for t in range(NT):
        fp = min(FS[t], P["FPE"][t])
        if fp not in scol:
            j = scol[fp] = 8 + 2 * len(scol)
            ts(col(j), col(1), float(fp), None, ALU.is_lt)
            act(col(j + 1), col(j), AF.Identity, bias=-BIG, scale=BIG / 2)
        act(col(16 + t), col(scol[fp]), AF.Identity, bias=BIG * TA[t], scale=-8 * BIG)
    fill(("X", NV, XW), 0)
    fill(("ZER", 0, C), 0)
    for j in range(2 * NT + 1):
        fill(("U", 112 * j, 112 * j + 16), 0)
    fill(("RR", 0, 1), 0)
    fill(("PW", 0, 4 * C), 256)
    fill(("HAS", S0, NS), 1)
    fill(("MP", S0, NS), 0)
    fill(("ER", S0, NS), NV)
    for t in range(NT):
        n = S0 + C * t
        fill(("RW%d" % t, n, n + C), 0)
        fill(("RD%d" % t, n, NS), 0)

    flip(("MP", 0, S0), ("MI", 0, S0))
    b = psum("L")
    mm([((b, 0, S0), ("TRI", 0, 128), ("MP", 0, S0), 1, True, True)])
    ts(("FH", 0, S0), (b, 0, S0), 0.0, -2048.0, ALU.max, ALU.add)
    add("S", lambda g, T, cx, b=b: [g.scalar.activation(T.FM[:], ap(T, (b, 0, S0)), AF.Relu)], [], [(b, 0, 512), ("FM", 0, S0)], SA + S0 * CY)
    b = psum("N")
    pick((b, 0, 20), "SELH", "FH", 0, S0)
    ts(("LST0", 0, 20), (b, 0, 20), -1.0, NV - 16 * 2048.0, ALU.mult, ALU.add)
    b = psum("L")
    mm([((b, 0, S0), ("ONEF", 0, 128), ("FM", 0, S0), 1, True, True)])
    act(("LP", 0, S0), (b, 0, S0), AF.Identity, bias=float(NV), scale=-1.0)
    ts(("MH", 0, S0), ("MI", 0, S0), -1.0, 2048.0, ALU.mult, ALU.add)
    ts(("EH", 0, S0), ("EI", 0, S0), -1.0, 2048.0, ALU.mult, ALU.add)
    for b, a0, a1 in ((psum("T"), 0, 16), (psum("H"), 16, 20)):
        for g0 in range(2):
            def fn(g, T, cx, b=b, a0=a0, a1=a1, g0=g0):
                parts = (("QH", 16 + 144 * g0, "MH"), ("QH", 144 * g0, "EH"))
                return [g.tensor.matmul(T[bank[b]][:, 0:a1 - a0, 16 * g0:16 * g0 + 16], T[m][:, lo:lo + 128], T[x][:, 16 * a0:16 * a1],
                                        j == 0, j == 1) for j, (m, lo, x) in enumerate(parts)]
            add("P", fn, [("QH", 0, 288), ("MH", 0, S0), ("EH", 0, S0)], [(b, 0, 512)], 32 * (a1 - a0) * PE)
        add("V", lambda g, T, cx, b=b, a0=a0, a1=a1: [g.vector.transpose(T.OTf[:, 32 * a0:32 * a1], T[bank[b]][:, 0:a1 - a0, :])],
            [(b, 0, 512)], [("OTf", 32 * a0, 32 * a1)], VA + 32 * (a1 - a0) * CY)
    for lo, hi, j in ((20, 324, 0), (324, 644, 20)):
        regather(("LST0", lo, hi), ("OTf", 0, 640), ("CG", j, j + (hi - lo) // 16), -1.0, 2048.0)
    vcopy(("ER", 0, S0), ("EI", 0, S0))
    send([(("LST0", 0, S0), ("LST1", 0, S0), 1, "lst0")], P["FIRST"])
    send([(("LST0", S0, 640), ("LST1", S0, 640), 1, "lst1")])
    send([(("LST0", 0, 640), ("LST%d" % t, 0, 640), t, "lst%d" % t) for t in (2, 3)])

    XA = ("X", 0, XW)

    def by_vector(b, n, per, i0, i1, lst, cmp_, lead, op, single=0, chain=None):
        i, k = i0, n // 16
        while i < i1:
            m = 1 if i - i0 < single else min(per, i1 - i)
            gtt((cmp_[0], cmp_[1] + n * i, cmp_[1] + n * (i + m)), XA, (lst[0], lst[1] + k * i, lst[1] + k * (i + m)),
                (lead[0], lead[1], lead[1] + n * m), op, chain)
            for j in range(i, i + m if b else i):
                count_row(b, j, (cmp_[0], cmp_[1] + n * j, cmp_[1] + n * j + n))
            i += m

    def by_scalar(b, n, rows, piece, lst, cmp_, lead, nl, chain=None):
        done = 0
        for lo in range(0, n * rows, piece):
            hi, D = min(lo + piece, n * rows), psum("D")
            x = (cmp_[0], cmp_[1] + lo, cmp_[1] + hi)
            if lo // piece % P["GS"] == 0:
                h2 = min(lo + piece * P["GS"], n * rows)
                act((x[0], x[1], cmp_[1] + h2), XA, AF.Copy, off=(lst[0], lst[1] + lo // 16, lst[1] + h2 // 16), chain=chain)
            cuts = [lo] + [c for c in range(0, n * rows, nl) if lo < c < hi] + [hi]
            mm([((D, 0, hi - lo), ("IDB", 0, 128), x, 1, True, False)]
               + [((D, u - lo, v - lo), ("NEG", 0, 128), (lead[0], lead[1] + u % nl, lead[1] + u % nl + v - u), 1, False, v == hi)
                  for u, v in zip(cuts, cuts[1:])])
            act((cmp_[0], cmp_[1] + lo, cmp_[1] + hi), (D, 0, hi - lo), AF.Sign, bias=2.0 ** -110, chain=chain)
            while b and (done + 1) * n <= hi:
                count_row(b, done, (cmp_[0], cmp_[1] + n * done, cmp_[1] + n * done + n))
                done += 1

    def by_adding(b, t, i0, i1, lst, cmp_, op, kind):
        L, XL = "LST%d" % t, "XL%d" % t
        for i in range(i0, i1, P["RA"]):
            m = min(P["RA"], i1 - i)
            x = (cmp_[0], cmp_[1] + S0 * i, cmp_[1] + S0 * (i + m))
            for j in range(0, m, P["RG"]):
                u = min(P["RG"], m - j)
                act((x[0], x[1] + S0 * j, x[1] + S0 * (j + u)), XA, AF.Copy, scale=-1.0,
                    off=(L, lst + 20 * (i + j), lst + 20 * (i + j + u)), chain="S%s%d" % (kind, t))
            add("G", lambda g, T, cx, x=x, m=m: [g.dma_start(ap(T, x), T[XL][:, 0:S0 * m], accum_op=ALU.add)],
                [(XL, 0, S0 * m), x], [x], P["GD"], P["LD"] + 160 * m / 300.0, "add%s%d_%d" % (kind, t, i))
            add("V", lambda g, T, cx, x=x: [g.vector.tensor_scalar(ap(T, x), ap(T, x), 0.0, None, op)], [x], [x], VA + wid(x) * CY / 2)
            for q in range(i, i + m):
                count_row(b, q, (cmp_[0], cmp_[1] + S0 * q, cmp_[1] + S0 * q + S0))

    def bulk_m(t):
        L, XL, b = "LST%d" % t, "XL%d" % t, psum("M")
        act((XL, 0, S0), XA, AF.Copy, off=(L, 0, 20))
        for j in range(1, max(RV, P["RA"] if FS[t] > P["FPE"][t] or P["MS"][t] else 1)):
            if t == 0 and P["LONE"] < 4:
                act((XL, S0 * j, S0 * j + S0), (XL, 0, S0), AF.Copy)
                continue
            dma("Y", lambda T, j=j: (T[XL][:, S0 * j:S0 * j + S0], T[XL][:, 0:S0]), [(XL, 0, S0)], [(XL, S0 * j, S0 * j + S0)], "rep%d" % t, 80)
        by_vector(b, S0, RV, 1, 16, (L, 0), ("CMP%d" % t, 0), (XL, 0), ALU.is_equal, P["LONE"] if t == 0 else 0, "Vm%d" % t)
        ow = ("RW0", 0, S0) if t == 0 else ("OUT%d" % t, 0, S0)
        act(ow, (b, 0, S0), AF.Relu, bias=col(24 + t), scale=-BIG)


    def bulk_e(t):
        L, XL, b, cmp_ = "LST%d" % t, "XL%d" % t, psum("E"), ("CMP%d" % t, 16 * S0)
        fp = min(FS[t], P["FPE"][t])
        by_scalar(b, S0, fp, P["PIECE"], (L, S0), cmp_, (XL, 0), S0, "S%d" % t)
        by_vector(b, S0, RV, FS[t], 16, (L, S0), cmp_, (XL, 0), ALU.is_ge, 0, "Ve%d" % t)
        od = ("RD0", 0, S0) if t == 0 else ("OUT%d" % t, NS, NS + S0)
        act(od, (b, 0, S0), AF.Relu, bias=col(16 + t), scale=col(scol[fp] + 1))

    def back_m(t):
        n = S0 + C * (t - 1) * P["MG"]
        send([(("OUT%d" % t, 0, n), ("RW%d" % t, 0, n), -t, "rw%d" % t)])

    def back_e(t):
        n = S0 + C * (t - 1 if t in P["SD"] else t) * P["MG"]
        send([(("OUT%d" % t, NS, NS + n), ("RD%d" % t, 0, n), -t, "rd%d" % t)])

    def count_all(b, c, i0, i1, first=True, stop=True):
        mm([((b, 0, C), ("SEL", 16 - i, 144 - i), ("NC", c + C * i, c + C * i + C), 1, first and i == i0, stop and i == i1 - 1)
            for i in range(i0, i1)])

    def fresh_m(k, t):
        NL, p, b, n = "NL%d" % t, PAIRS.index((k, t)), psum("N"), S0 + C * k
        x, c = 192 * p, 1536 * p
        act(("XF", x, x + 4 * C), XA, AF.Copy, off=(NL, 160 * k + C, 160 * k + C + 12))
        by_vector(None, C, 4, 2, 16, (NL, 160 * k), ("NC", c), ("XF", x), ALU.is_equal)
        if t == k + 1:
            count_all(b, c, 2, 10, stop=False)
            count_all(b, c, 10, 14, False, False)
            count_all(b, c, 14, 16, False)
        else:
            count_all(b, c, 2, 16)
        o = ("OUT%d" % t, n, n + C)
        act(o, (b, 0, C), AF.Relu, bias=col(27 + t), scale=-BIG)
        if t == k + 1 or not P["MG"]:
            send([(o, ("RW%d" % t, n, n + C), -t, "nw%d%d" % (k, t))])

    def fresh_e(k, t):
        NL, p, b, n = "NL%d" % t, PAIRS.index((k, t)), psum("N"), S0 + C * k
        o, lst, cmp_, lead = ("OUT%d" % t, NS + n, NS + n + C), (NL, 160 * k + 64), ("NC", 1536 * p + 768), ("XF", 192 * p)
        if P["FB"][p] == "S":
            by_scalar(None, C, 16, 384, lst, cmp_, lead, 192)
        else:
            by_vector(None, C, 4, 0, 16, lst, cmp_, lead, ALU.is_ge)
        if t == k + 1:
            count_all(b, cmp_[1], 0, 12, stop=False)
            count_all(b, cmp_[1], 12, 16, False)
        else:
            count_all(b, cmp_[1], 0, 16)
        if P["FB"][p] == "S":
            act(o, (b, 0, C), AF.Relu, bias=BIG * (TA[t] - 8), scale=-BIG / 2)
        else:
            act(o, (b, 0, C), AF.Relu, bias=BIG * TA[t], scale=-BIG)
        if t == k + 1 and t in P["SD"] or not P["MG"]:
            send([(o, ("RD%d" % t, n, n + C), -t, "nd%d%d" % (k, t))])

    def share(k, lo, hi, hi2, sm):
        tr = [(("SN%d" % k, lo, hi2 if t > k + 1 else hi), ("NL%d" % t, 160 * k + lo, 160 * k + (hi2 if t > k + 1 else hi)), t,
               "%s%d%d" % (sm, k, t)) for t in range(k + 1, NT)]
        send(tr[:1])
        if tr[1:]:
            send(tr[1:])

    def w(t, j):
        if j in (1, 2, 8, 3):
            lo = 16 + 224 * t + (0, C, 112, 112 + C)[(1, 2, 8, 3).index(j)]
            return ("U", lo, lo + C)
        return ("W%d" % t, C * j, C * j + C)

    def turn(out, j, x, two, k0, k1):
        for h in range(2):
            m = 64 + 32 * two * (1 + h)
            a, o = (x[0], x[1] - 16 * h, x[1] - 16 * h + m), ("OT", 224 * j + 96 * h, 224 * j + 96 * h + m)
            add("V", lambda g, T, cx, a=a, o=o: [g.vector.transpose(ap(T, o), ap(T, a))], *rw([a], [o]), VA + m * CY)
        regather(out, ("OT", 224 * j, 224 * j + 224), ("CL", 0, 3 + two), k0, k1)

    held = {}

    def sums(src, lo, hi, j, jk):
        for a in range(3):
            act(("JK", 416 * (jk + a), 416 * (jk + a) + hi - lo), (src, lo, hi), AF.Sign, bias=col(4 + a), scale=-1.0,
                acc=("ACC", j + a, j + a + 1))

    def logic_a(t):
        n = S0 + C * max(t - 1, 0)
        L, pw, cs = n // 16, C * t + 16, ("IDS", 8 * t + 4, 8 * t + 7)
        b = psum("L")
        mm([((b, 0, n), ("IDB", 0, 128), ("RW%d" % t, 0, n), 1, True, True)])
        tt(("WB", 0, n), ("MP", 0, n), (b, 0, n), ALU.min)
        b = psum("L")
        if t in P["LA"]:
            mm([((b, 0, n), ("ONEB", 0, 128), ("WB", 0, n), 1, True, True)])
            act(("HAS", 0, n), (b, 0, n), AF.Sign)
            m = n if t else n + C
            scan(("PO", 0, m), ("HAS", 0, m))
            sums("PO", 0, m, 8 * t, 0)
            held["n", t] = ("PO", n - 1, n)
            if t and P["I3"]:
                act(("ACC", 32, 35), ("ACC", 8 * t, 8 * t + 3), AF.Identity, bias=n / 2.0 + C, scale=0.5)
            return
        pick((b, 0, L), "SEL", "WB", 0, 16 * L)
        act(("HW", 0, L), (b, 0, L), AF.Sign)
        scan(("RR", 1, L + 1), ("HW", 0, L))
        b = psum("L")
        mm([((b, 32 - L, 32), ("ONEB", 0, 128), ("RR", 1, L + 1), 1, True, True),
            ((b, 32, 32 + L), ("TL", 0, 128), ("RR", 1, L + 1), 1, True, False),
            ((b, 32, 32 + L), ("TU", 0, 128), ("RR", 0, L), 1, False, True)])
        sums(b, 32 - L, 32, 8 * t, 0)
        act(("PW", pw - 1, pw + L), (b, 31, 32 + L), AF.Copy)
        ts(cs, ("ACC", 8 * t, 8 * t + 3), 0.5, L / 2.0, ALU.mult, ALU.add)
        gtt(("Z", 0, C), ("PW", pw, pw + 32), cs, ("IK", 0, C), ALU.is_le)
        b = psum("H")
        held[t], held["n", t] = b, ("PW", pw - 1, pw)
        pick((b, 0, 3), "SEL", "Z", 0, C, stop=False)
        mm([((b, 0, 3), ("I8", 0, 128), ("ACC", 8 * t, 8 * t + 3), 1, False, bool(P["I3"]))])
        if P["I3"]:
            act(("ACC", 32, 35), (b, 0, 3), AF.Identity, bias=n / 2.0 + C)

    def logic_m(t):
        n = S0 + C * t
        ids, new = ("IDS", 8 * t, 8 * t + 3), (n, n + C)
        if t:
            b = psum("L")
            tt(("WB", n - C, n), ("MP", n - C, n), ("RW%d" % t, n - C, n), ALU.min)
            mm([((b, 0, C), ("ONEB", 0, 128), ("WB", n - C, n), 1, True, True)])
            act(("HAS", n - C, n), (b, 0, C), AF.Sign)
            scan(("PP", 0, 96), ("HAS", n - C, n + C), held["n", t])
            sums("PP", 0, 96, 8 * t + 4, 3)
            if P["I3"]:
                for a in range(3):
                    ts(("IDS", 8 * t + a, 8 * t + a + 1), ("ACC", 8 * t + 4 + a, 8 * t + 5 + a), 0.5,
                       ("ACC", 32 + a, 33 + a), ALU.mult, ALU.add)
            elif t in P["LA"]:
                tt(("ACC", 8 * t, 8 * t + 3), ("ACC", 8 * t, 8 * t + 3), ("ACC", 8 * t + 4, 8 * t + 7), ALU.add)
                ts(ids, ("ACC", 8 * t, 8 * t + 3), 0.5, (n + C) / 2.0, ALU.mult, ALU.add)
            else:
                mm([((held[t], 0, 3), ("IH", 0, 128), ("ACC", 8 * t + 4, 8 * t + 7), 1, False, True)])
                ts(ids, (held[t], 0, 3), (n + C) / 2.0, None, ALU.add)
        else:
            ts(ids, ("ACC", 0, 3), 0.5, (n + C) / 2.0, ALU.mult, ALU.add)
        act(w(t, 0), ("MP", 0, NS), AF.Copy, off=ids)
        gtt(w(t, 1), ("RW%d" % t, 0, n + C), ids, w(t, 0), ALU.min)
        b = psum("L")
        mm([((b, 0, C), ("TRI", 0, 128), w(t, 1), 1, True, True)])
        act(w(t, 2), (b, 0, C), AF.Relu)
        act(w(t, 3), ("LP", 0, NS), AF.Copy, off=ids)
        b, x, y = psum("L"), w(t, 1), w(t, 2)
        if t < NT - 1:
            mm([((b, 0, 64), ("IDF", 0, 128), (x[0], x[1] - 16, x[2]), 1, True, True)])
        if t < NT - 1 or t not in P["FP"]:
            mm([((b, 64, 128), ("ONEF", 0, 128), (y[0], y[1], y[2] + 16), 1, True, True)])
        if t < NT - 1:
            turn(("SN%d" % t, 0, 64), 2 * t, (b, 16, 112), 1, -1.0, float(NV))
            send([(("SN%d" % t, 0, 64), ("NL%d" % (t + 1), 160 * t, 160 * t + 64), t + 1, "nm%d%d" % (t, t + 1))])
            if t + 2 < NT and not P["MG"]:
                send([(("SN%d" % t, 0, 64), ("NL%d" % u, 160 * t, 160 * t + 64), u, "nm%d%d" % (t, u)) for u in range(t + 2, NT)])
        if t in P["FP"]:
            act(w(t, 6), ("LP", 0, NS), AF.Identity, bias=col(20), scale=col(21), off=ids)
        if t < NT - 1 or t not in P["FP"]:
            add("S", lambda g, T, cx: [g.scalar.activation(T.LP[:, n:n + C], ap(T, (b, 64, 112)), AF.Identity, bias=float(NV), scale=-1.0)],
                [], [(b, 0, 512), ("LP",) + new], SA + C * CY)
        vscatter(("MP", 0, NS), ids, w(t, 0), w(t, 1))
        act(w(t, 7), ("MP", 0, NS), AF.Identity, bias=float(NV), scale=-1.0, off=ids)
        act(("MP",) + new, w(t, 1), AF.Copy)

    def logic_f(t):
        els, ols = ("SN%d" % t, 160, 208), ("SN%d" % t, 208, 211)
        act(w(t, 8), ("ER", 0, NS), AF.Copy, off=("IDS", 8 * t, 8 * t + 3))
        turn((els[0], 160, 224), 2 * t + 1, w(t, 8), 1, 1.0, 0.0)
        if t not in P["FP"]:
            vscatter(("F", 0, FW), ols, ("LP", S0 + C * t, S0 + C * t + C), w(t, 3))
        if t in P["FP"]:
            vscatter(("F", 0, FW), ols, w(t, 6), w(t, 2))
            b = psum("L")
            held["f", t] = (b, 0, C)
            mm([((b, 0, C), ("IDF", 0, 128), w(t, 8), 1, True, False)])
            for j, q in enumerate((0, 2, 1, 3)):
                x, o = ("FX", 192 * q, 192 * q + 192), (els[0], els[1] + 12 * q, els[1] + 12 * q + 12)
                if q < 2:
                    act(x, ("F", 0, FW), AF.Copy, off=o)
                else:
                    add("V", lambda g, T, cx, x=x, o=o: [g.vector.tensor_copy(ap(T, x), ind(T, ("F", 0, FW), o))],
                        [("F", 0, FW), o], [x], VG + 192 * GA)
                mm([((b, 0, C), ("SELF", 16 - i, 144 - i), ("FX", C * i, C * i + C), 1, False, False) for i in range(4 * q, 4 * q + 4)])
        else:
            act(("FX", 0, 768), ("F", 0, FW), AF.Copy, off=els)
            dma("Y", lambda T: (ap(T, w(t, 10)), T.FX[0:128:16, :]), [("FX", 0, 768)], [w(t, 10)], "fd%d" % t, 60)
            tt(w(t, 5), w(t, 10), w(t, 8), ALU.add)
            held["f", t] = w(t, 5)
        if t < NT - 1:
            vscatter(("F", 0, FW), ols, ("ZER", 0, C))

    def logic_e(t):
        n = S0 + C * t
        ids = ("IDS", 8 * t, 8 * t + 3)
        act(w(t, 4), w(t, 8), AF.Relu, bias=-BIG * (NV - 1), scale=BIG)
        for j in range(t + 1):
            gtt(w(t, 4), ("RD%d" % j, 0, NS), ids, w(t, 4), ALU.max)
        if t in P["FP"]:
            mm([(held["f", t], ("IDF", 0, 128), w(t, 4), 1, False, True)])
        else:
            tt(w(t, 5), w(t, 5), w(t, 4), ALU.max)
        ts(w(t, 9), w(t, 4), 0.0, BIG, ALU.is_le, ALU.mult)
        tt(w(t, 9), w(t, 9), w(t, 7), ALU.add)
        if t < NT - 1:
            tt(("ER", n, n + C), held["f", t], w(t, 9), ALU.min)
            turn(("SN%d" % t, 64, 112), 2 * t, ("ER", n, n + C), 0, 1.0, 0.0)
            send([(("SN%d" % t, 64, 112), ("NL%d" % (t + 1), 160 * t + 64, 160 * t + 112), t + 1, "ne%d%d" % (t, t + 1))])
            if t + 2 < NT:
                lo = 0 if P["MG"] else 64
                send([(("SN%d" % t, lo, 112), ("NL%d" % u, 160 * t + lo, 160 * t + 112), u, "ne%d%d" % (t, u)) for u in range(t + 2, NT)])
        else:
            tt(("YI", n, NS), held["f", t], w(t, 9), ALU.min)
            dma("Y", lambda T: (T.yi[:, n:NS], T.YI[:, n:NS]), [("YI", n, NS)], [], "stored", 30)

    def out_m():
        act(("YM", 0, NS), ("MP", 0, NS), AF.Identity, bias=float(NV), scale=-1.0)
        dma("Y", lambda T: (T.ym[:], T.YM[:]), [("YM", 0, NS)], [], "stored", 260)

    def out_e():
        n, b = NS - C, psum("M")
        last[b] = [e for e in last["OUT3"] if e[1] <= S0]
        if P["OE"]:
            mm([((b, 0, n), ("IDF", 0, 128), ("ER", 0, n), 1, True, False)])
        for j in range(NT):
            mm([((b, 0, n), ("IDB", 0, 128), ("RD%d" % j, 0, n), 1, j == 0 and not P["OE"], j == NT - 1)])
        if P["OE"]:
            ts(("YI", 0, n), (b, 0, n), float(NV), None, ALU.min)
        else:
            tt(("YI", 0, n), (b, 0, n), ("ER", 0, n), ALU.max)
            ts(("YI", 0, n), ("YI", 0, n), float(NV), None, ALU.min)
        dma("Y", lambda T: (T.yi[:, 0:n], T.YI[:, 0:n]), [("YI", 0, n)], [], "stored", 240)

    for b in P["BLOCKS"].split():
        {"bm": bulk_m, "be": bulk_e, "fm": fresh_m, "fe": fresh_e, "la": logic_a, "lm": logic_m, "lf": logic_f,
         "le": logic_e, "om": out_m, "oe": out_e, "sw": back_m, "sd": back_e}[b[:2]](*[int(x) for x in b[2:]])
    return ops, bank, nload


def plan(P=TUNE):
    ops, bank, nload = build(P)
    n, by_sem, users, WAKE = len(ops), {}, {}, P["WAKE"]
    for i, o in enumerate(ops):
        if o["sem"]:
            by_sem.setdefault(o["sem"], []).append(i)
        for b in o["banks"]:
            users.setdefault(b, []).append(i)
    for o in ops:
        for d in list(o["deps"]):
            if ops[d]["sem"]:
                o["deps"].update(by_sem[ops[d]["sem"]])
    way = [0.0] * n
    for i in range(n - 1, -1, -1):
        o = ops[i]
        way[i] += o["dur"] + o["lat"] + WAKE + (1e3 - i if i < nload else 0) + (0 if o["after"] else P["PAD"])
        for d in o["deps"]:
            way[d] = max(way[d], way[i])
        if o["after"] is not None:
            way[o["after"]] = max(way[o["after"]], way[i] - WAKE)


    def place(seq, before, back):
        busy, start, end = {e: [] for e in "VSPGY"}, {}, {}
        for i in seq:
            o = ops[i]
            t = max([0.0] + [end[d] for d in before[i]]) + (o["lat"] + WAKE if back else 0.0)
            q, k = busy[o["eng"]], 0
            while k < len(q) and q[k][0] < t + o["dur"]:
                t = max(t, q[k][1])
                k += 1
            q.insert(k, (t, t + o["dur"]))
            start[i], end[i] = t, t + o["dur"] + (0.0 if back else o["lat"] + WAKE)
        return start, end

    def passes(deps, key, rounds):
        succ, best = [set() for o in ops], None
        for i in range(n):
            for d in deps[i]:
                succ[d].add(i)
        for r in range(rounds):
            seq, left, heap = [], [len(d) for d in deps], sorted((key[i], i) for i in range(n) if not deps[i])
            while heap:
                i = heap.pop(0)[1]
                seq.append(i)
                for x in succ[i]:
                    left[x] -= 1
                    if not left[x]:
                        heap.append((key[x], x))
                heap.sort()
            start, end = place(seq, deps, False)
            if best is None or max(end.values()) < best[0]:
                best = (max(end.values()), start, end)
            back = place(sorted(range(n), key=lambda i: (-end[i], -start[i])), succ, True)[1]
            key = [-1e3 + i if i < nload else -back[i] for i in range(n)]
        return best + (key,)

    span, start, end, key = passes([o["deps"] for o in ops], [-x for x in way], P["R0"])
    best = None
    for r in range(P["R1"]):
        deps, holder, got = [set(o["deps"]) for o in ops], {}, {}
        for b in sorted(users, key=lambda b: max(start[u] for u in users[b] if ops[u]["eng"] == "P")):
            x = got[b] = min(POOL[b[0]], key=lambda x: max([0.0] + [end[u] for u in users.get(holder.get(x), [])]))
            for u in users[b]:
                deps[u].update(users.get(holder.get(x), []))
            holder[x] = b
        shake = [((i + 1) * (r + P["SEED"]) * 7919 % 1009) / 1009.0 * P["SHAKE"] * (r % 3) for i in range(n)]
        span, start, end, key = passes(deps, [start[i] + shake[i] for i in range(n)], P["R2"])
        if best is None or span < best[0]:
            best = (span, start, deps, got, end)
        start, end = best[1], best[4]
    bank.update(best[3])
    for o, d in zip(ops, best[2]):
        o["deps"] = d
    order = sorted(range(n), key=lambda i: (i >= nload, best[1][i] if i >= nload else i))
    return ops, tighten(P, ops, order, nload), by_sem


def tighten(P, ops, order, nload):
    n, deps, eng = len(ops), [sorted(o["deps"]) for o in ops], ["VSPGY".index(o["eng"]) for o in ops]
    cases = []
    for c in P["CASES"]:
        other = build(dict(P, **c))[0]
        cases.append(([o["dur"] for o in other], [o["lat"] + c.get("WAKE", P["WAKE"]) for o in other]))

    def run(seq, p0=0, old=None):
        total, pairs, out, head = 0.0, [], [], [-1] * 5
        for i in seq[:p0]:
            head[eng[i]] = i
        for c, (dur, lat) in enumerate(cases):
            end, why = (old[c][0][:], old[c][1][:]) if old else ([0.0] * n, [-1] * n)
            free, prev = [end[i] - lat[i] if i >= 0 else 0.0 for i in head], head[:]
            out.append((end, why))
            for i in seq[p0:]:
                e = eng[i]
                t, y = free[e], prev[e]
                for d in deps[i]:
                    if end[d] > t:
                        t, y = end[d], d
                why[i], prev[e] = y, i
                free[e] = t = t + dur[i]
                end[i] = t + lat[i]
            i = end.index(max(end))
            total += end[i]
            while why[i] >= 0:
                if eng[why[i]] == eng[i] and why[i] not in ops[i]["deps"]:
                    pairs.append((why[i], i))
                i = why[i]
        return total / len(cases), pairs, out

    seed, (now, pairs, times) = 12345, run(order)
    best = (now, order)
    for step in range(P["STEPS"]):
        seed = (seed * 1103515245 + 12345) % 2147483648
        a, b = pairs[(seed >> 8) % len(pairs)]
        pa, pb = order.index(a), order.index(b)
        if pa < nload:
            continue
        if seed >> 7 & 1:
            pa = max(nload, pa - (seed >> 20) % 3 * ((seed >> 24) % 12))
            part, move = order[pa:pb + 1], {b}
            for x in reversed(part):
                if x in move:
                    move.update(deps[x])
            new = [x for x in part if x in move] + [x for x in part if x not in move]
        else:
            pb = min(n - 1, pb + (seed >> 20) % 3 * ((seed >> 24) % 12))
            part, move = order[pa:pb + 1], {a}
            for x in part:
                if not move.isdisjoint(deps[x]):
                    move.add(x)
            new = [x for x in part if x not in move] + [x for x in part if x in move]
        cand = order[:pa] + new + order[pb + 1:]
        t, pr, tm = run(cand, pa, times)
        if t <= now + P["SLACK"] * (1.0 - step / P["STEPS"]) * ((seed >> 12) % 16) / 16.0:
            now, pairs, order, times = t, pr, cand, tm
            if t < best[0]:
                best = (t, cand)
    ops[0]["span"] = best[0]
    return best[1]


def engine_sets(topo, cores, r, tr):
    can = [topo.engines(cores[r], cores[(r + x[2]) % len(cores)]) for x in tr]
    if len(tr) == 1:
        few = min(len(topo.engines(cores[r], c)) for c in cores if c != cores[r])
        return [can[0][:few]] if tr[0][3] == "lst0" else can
    a, b = can
    if len(a) > len(b):
        return [[e for e in a if e not in b][:len(b)], b]
    if len(b) > len(a):
        return [a, [e for e in b if e not in a][:len(a)]]
    return [a[:len(a) // 2], b[len(b) // 2:]]


PLAN = []


def rank_program(g, core, T, topo):
    r = T.rank_of(core)
    if r is None:
        return
    if not PLAN:
        PLAN.append(plan())
    ops, order, by_sem = PLAN[0]
    cores = list(T.cores)
    N = len(cores)
    queue = {"V": g.vector, "S": g.scalar, "P": g.tensor, "G": g, "Y": g.sync}
    count = {e: 0 for e in "VSPG"}
    mark, waited, knew, cx, sent = {}, {}, {}, {}, 0

    def wait(e, sem, val):
        if waited.get((e, sem), 0) < val:
            waited[(e, sem)] = val
            queue[e].wait_ge(T.sem[sem], val)

    def meets(x, y):
        return x[0] == y[0] and x[1] < y[2] and y[1] < x[2]

    for i in order:
        o, need = ops[i], {}
        e = o["eng"]
        for d in o["deps"]:
            p = ops[d]
            if p["sends"]:
                for j, x in enumerate(p["sends"]):
                    if any(meets(x[1], y) for y in o["rd"] + o["wr"]):
                        need[x[3]] = len(engine_sets(topo, cores, (r - x[2]) % N, p["sends"])[j])
            elif p["sem"]:
                need[p["sem"]] = 16 * len(by_sem[p["sem"]])
            elif not (e == "P" and p["eng"] == "P"):
                s = "e" + p["eng"]
                need[s] = max(need.get(s, 0), mark[d])
        for s in need:
            for s2 in need:
                if s != s2 and need[s2] <= knew.get((s, need[s]), {}).get(s2, 0):
                    need[s2] = 0
        for s in sorted(need):
            wait(e, s, need[s])
            for s2, v in knew.get((s, need[s]), {}).items():
                waited[(e, s2)] = max(waited.get((e, s2), 0), v)
        seen = {s: v for (q, s), v in waited.items() if q == e}
        if o["sends"]:
            trs = []
            for x, en in zip(o["sends"], engine_sets(topo, cores, r, o["sends"])):
                rid, pid = topo.addr(cores[(r + x[2]) % N], core)
                trs.append((T[x[1][0]][:, x[1][1]:x[1][2]], T[x[0][0]][:, x[0][1]:x[0][2]], T.sem[x[3]], pid, rid,
                            sum(1 << k for k in en)))
                sent += len(en)
            if len(trs) == 1:
                x = trs[0]
                g.remote_dma(x[0], x[1], x[2], T.sem.sent, x[3], x[4], x[5])
            else:
                g.remote_dma_fused([RemoteDMATransfer(dst_ids=[DstId(rid=x[4], pnc=x[3])], dma_engine_mask=x[5],
                                                      remote_sem=x[2], src=x[1], dst=x[0]) for x in trs],
                                   local_sem=T.sem.sent)
        elif o["sem"]:
            for ins in o["fn"](g, T, cx):
                ins.then_inc(T.sem[o["sem"]], 16)
        else:
            for ins in o["fn"](g, T, cx):
                ins.then_inc(T.sem["e" + e], 1)
                count[e] += 1
            mark[i] = count[e]
            knew[("e" + e, count[e])] = seen
    for e in "VSPG":
        wait("G", "e" + e, count[e])
    wait("G", "sent", sent)
    wait("G", "stored", 16 * len(by_sem["stored"]))
